import numpy as np
import ml_dtypes


def mxq(x, axis, fmt="e4m3"):
    dtype, down = {"e4m3": (ml_dtypes.float8_e4m3fn, 7), "e5m2": (ml_dtypes.float8_e5m2, 14)}[fmt]
    v = np.moveaxis(np.asarray(x, np.float32).astype(ml_dtypes.bfloat16).astype(np.float64), axis, -1)
    blocks = v.reshape(v.shape[:-1] + (-1, 32))
    amax = np.abs(blocks).max(-1, keepdims=True)
    byte = np.maximum(np.where(amax > 0, np.frexp(amax)[1] - 1 + 127, 0) - down, 1)
    scale = np.exp2(byte - 127.0)
    codes = (blocks / scale).astype(np.float32).astype(dtype).astype(np.float64)
    return np.moveaxis((codes * scale).reshape(v.shape), -1, axis)


WIDE = False


def mx_kscale(k):
    if not WIDE:
        return np.ones(k)
    levels = np.array([10, -10, 5, -5, 0])
    if k % 512:
        return np.exp2(np.random.permutation(np.resize(levels, k // 32))).repeat(32)
    a = np.empty((k // 512, 16))
    for p in range(k // 512):
        a[p, :8] = np.random.permutation(np.resize(levels, 8))
        for g in range(8):
            far = levels[np.abs(levels - a[p, g]) >= 10]
            a[p, g + 8] = far[np.random.randint(len(far))]
    return np.exp2(a.ravel()).repeat(32)


BF16 = ml_dtypes.bfloat16


def bf(x):
    return np.asarray(x, np.float32).astype(BF16)


def f64(x):
    return np.asarray(x).astype(np.float64)


E2M1 = np.array([0.0, 0.5, 1.0, 1.5, 2.0, 3.0, 4.0, 6.0, -0.0, -0.5, -1.0, -1.5, -2.0, -3.0, -4.0, -6.0])


def pack_weight(w, fmt):
    k, n = w.shape
    w = f64(bf(w)).reshape(k // 32, 32, n)
    amax = np.abs(w).max(1)
    if fmt == "e4m3":
        byte = np.frexp(amax)[1] - 1 + 127 - 7
    else:
        mant, ex = np.frexp(amax / 6.0)
        byte = np.where(mant > 0.5, ex, ex - 1) + 127
    byte = np.clip(np.where(amax > 0, byte, 1), 1, 254)
    scaled = (w * np.exp2(127.0 - byte)[:, None, :]).reshape(k, n).astype(np.float32)
    by_word = np.ascontiguousarray(scaled.reshape(k // 512, 128, 4, n).transpose(0, 1, 3, 2))
    if fmt == "e4m3":
        words = by_word.astype(ml_dtypes.float8_e4m3fn).view(np.uint8)
    else:
        c = by_word.astype(ml_dtypes.float4_e2m1fn).view(np.uint8) & 0xF
        words = c[..., 0::2] | (c[..., 1::2] << 4)
    return np.ascontiguousarray(words), np.ascontiguousarray(byte.astype(np.uint8).reshape(k // 512, 16, n))


def unpack_weight(words, scales, fmt):
    g, p, n, _ = words.shape
    if fmt == "e4m3":
        vals = np.ascontiguousarray(words).view(ml_dtypes.float8_e4m3fn).astype(np.float64)
    else:
        nib = np.empty((g, p, n, 4), np.uint8)
        nib[..., 0::2] = words & 0xF
        nib[..., 1::2] = words >> 4
        vals = E2M1[nib]
    vals = vals * np.repeat(np.exp2(scales.astype(np.float64) - 127.0), 8, axis=1)[..., None]
    return vals.transpose(0, 1, 3, 2).reshape(g * 512, n)
def pack4(w):
    words, scales = pack_weight(w, "e2m1")
    return words.reshape(words.shape[0], 128, -1), scales


def unpack4(words, scales):
    return unpack_weight(words.reshape(words.shape[0], 128, -1, 2), scales, "e2m1")


def planes(Y):
    n, m = Y.shape
    b = f64(bf(Y)).reshape(n // 32, 32, m)
    amax = np.abs(b).max(1)
    byte = np.clip(np.where(amax > 0, np.frexp(amax)[1] - 1 + 127 - 7, 1), 1, 254)
    codes = (b * np.exp2(127.0 - byte)[:, None, :]).reshape(n, m).astype(np.float32).astype(ml_dtypes.float8_e4m3fn).view(np.uint8)
    words = codes.reshape(n // 512, 128, 4, m).transpose(0, 1, 3, 2)
    return np.ascontiguousarray(words), np.ascontiguousarray(byte.astype(np.uint8).reshape(n // 512, 16, m))


N, M, D, F = 1024, 1024, 512, 1024


def hidden_sensitivity(inp_q, w, b, v):
    t = np.tanh((inp_q @ w) + f64(b))
    return (1.0 - t * t) * f64(v)


def setup_inputs():
    s, u = mx_kscale(D), mx_kscale(F)
    x = bf(np.random.standard_normal((N, D)) * s)
    y = bf(np.random.standard_normal((M, D)) / s)
    wa_words, wa_scales = pack4(np.random.standard_normal((D, F)) / np.sqrt(D) / s[:, None])
    wb_words, wb_scales = pack4(np.random.standard_normal((D, F)) / np.sqrt(D) * s[:, None])
    return {
        "x": x,
        "y": y,
        "wa_words": wa_words,
        "wa_scales": wa_scales,
        "wb_words": wb_words,
        "wb_scales": wb_scales,
        "b": bf(0.5 * np.random.standard_normal(F)),
        "va": bf(np.random.standard_normal(F) * u),
        "vb": bf(np.random.standard_normal(F) / u),
    }


def core(x, y, wa_words, wa_scales, wb_words, wb_scales, b, va, vb):
    d = x.shape[1]
    f = wa_scales.shape[2]
    xq = mxq(f64(x), 1, "e4m3")
    yq = mxq(f64(y), 1, "e4m3")
    da = hidden_sensitivity(xq, unpack4(wa_words, wa_scales), b, va)
    db = hidden_sensitivity(yq, unpack4(wb_words, wb_scales), b, vb)
    gram = (mxq(da, 1, "e4m3") @ mxq(db, 1, "e4m3").T) / np.sqrt(f)
    base = (xq @ yq.T) / np.sqrt(d)
    return base * gram


def reference(x, y, wa_words, wa_scales, wb_words, wb_scales, b, va, vb):
    R_out = core(x, y, wa_words, wa_scales, wb_words, wb_scales, b, va, vb)
    words, scales = planes(R_out)
    return R_out, words, scales

@@ -1,0 +1,397 @@
+from contextlib import ExitStack
+
+import concourse.mybir as mybir
+from concourse.masks import make_identity
+
+F32 = mybir.dt.float32
+BF16 = mybir.dt.bfloat16
+I32 = mybir.dt.int32
+U32 = mybir.dt.uint32
+U8 = mybir.dt.uint8
+FP8X4 = mybir.dt.float8_e4m3fn_x4
+FP4X4 = mybir.dt.float4_e2m1fn_x4
+ACT = mybir.ActivationFunctionType
+ALU = mybir.AluOpType
+
+N, M, D, F = 1024, 1024, 512, 1024
+P = 128
+HALF = 512
+FLOPS = 2 * (N * D * F + M * D * F + N * D * M + N * F * M)
+SCALE = 1.0 / (32.0 * 512.0 ** 0.5)
+
+UNITS = [
+    (0, 0, 0, 0, 512), (0, 0, 1, 0, 512), (1, 0, 0, 0, 512), (1, 0, 1, 0, 512), (1, 1, 0, 0, 512), (1, 1, 1, 0, 512),
+    (0, 1, 0, 0, 256), (0, 1, 1, 0, 256), (0, 1, 0, 256, 512), (0, 1, 1, 256, 512),
+]
+QUADS = [(0, 0), (0, 1), (1, 0), (1, 1)]
+STEPS = [
+    (0, 0), (0, 1), (0, 2), (0, 3), (1, 0), (1, 1), (1, 2), (1, 3),
+    (2, 0), (2, 1), (3, 0), (3, 1), (2, 2), (2, 3), (3, 2), (3, 3),
+]
+SQUARE_ON_ACT = (4, 5, 6, 7, 8)
+BASE_AT = [5, 6, 7, 8, 9, 10, 11, 12, 13, 14, 15, 16, 17, 18, 19, 20]
+HAD_AT = [20, 21, 22, 23, 28, 29, 30, 31, 36, 37, 38, 39]
+
+
+def tile_twotimehiddentangentkernel_x2_kernel(
+    tc, x, y, wa_words, wa_scales, wb_words, wb_scales, b, va, vb, out_0, out_1, out_2
+):
+    nc = tc.nc
+    with ExitStack() as ctx:
+        keep = ctx.enter_context(tc.tile_pool(name="keep", bufs=1))
+        work = ctx.enter_context(tc.tile_pool(name="work", bufs=3))
+        psum = ctx.enter_context(tc.psum_pool(name="psum", bufs=1))
+        ctx.enter_context(tc.manual_schedule())
+
+        warm = keep.tile([P, 1], F32, name="warm")
+        nc.vector.memset(warm[:], 0.0)
+        nc.scalar.activation(out=warm[:], in_=warm[:], func=ACT.Tanh)
+
+        ident = keep.tile([P, P], F32, name="ident", align_bytes=64)
+        make_identity(nc, ident[:])
+
+        raw = {}
+        for s in (0, 1):
+            for h in (0, 1):
+                raw[s, h] = keep.tile([P, 4, D], BF16, name="raw_%d%d" % (s, h), align_bytes=64)
+
+        def load_rows(s, h, j0, j1):
+            src = (x, y)[s][HALF * h : HALF * (h + 1), :]
+            view = src.rearrange("(p t) k -> p t k", t=4) if s == 0 else src.rearrange("(t p) k -> p t k", t=4)
+            nc.sync.dma_start(out=raw[s, h][:, j0:j1, :], in_=view[:, j0:j1, :])
+
+        w_raw = [keep.tile([P, 2 * F], U8, name="w_raw%d" % s, align_bytes=64) for s in (0, 1)]
+        w_perm = [keep.tile([P, 2 * F], U8, name="w_perm%d" % s, align_bytes=64) for s in (0, 1)]
+        wp_raw = [keep.tile([P, F], U8, name="wp_raw%d" % s, align_bytes=64) for s in (0, 1)]
+        wp_perm = [keep.tile([P, F], U8, name="wp_perm%d" % s, align_bytes=64) for s in (0, 1)]
+        for s in (0, 1):
+            nc.vector.memset(wp_raw[s][:].bitcast(I32), 0)
+
+        def load_words(s):
+            nc.sync.dma_start(out=w_raw[s][:].bitcast(I32), in_=(wa_words, wb_words)[s][0].bitcast(I32))
+
+        def load_scales(s):
+            for q in range(4):
+                nc.scalar.dma_start(
+                    out=wp_raw[s][32 * q : 32 * q + 4, :].bitcast(I32),
+                    in_=(wa_scales, wb_scales)[s][0][4 * q : 4 * q + 4, :].bitcast(I32),
+                )
+
+        vec16 = keep.tile([24, P], BF16, name="vec16")
+        vec32 = keep.tile([P, P], F32, name="vec32", align_bytes=64)
+        nc.vector.memset(vec32[:], 0.0)
+
+        load_rows(0, 0, 0, 2)
+        load_scales(0)
+        load_words(0)
+        load_rows(0, 0, 2, 4)
+        for j, v in enumerate((b, va, vb)):
+            nc.gpsimd.dma_start(
+                out=vec16[8 * j : 8 * j + 8, :].rearrange("r (q i) -> r q i", i=8),
+                in_=v.rearrange("(q r i) -> r q i", r=8, i=8),
+            )
+        load_rows(1, 0, 0, 4)
+        load_words(1)
+        load_scales(1)
+        load_rows(1, 1, 0, 4)
+        load_rows(0, 1, 0, 4)
+
+        def permute(s):
+            nc.vector.tensor_copy(
+                out=w_perm[s][:].bitcast(I32).rearrange("p (r q i) -> p r q i", r=8, q=16),
+                in_=w_raw[s][:].bitcast(I32).rearrange("p (q r i) -> p r q i", r=8, q=16),
+            )
+            nc.vector.tensor_copy(
+                out=wp_perm[s][:].bitcast(I32).rearrange("p (r q i) -> p r q i", r=8, q=16),
+                in_=wp_raw[s][:].bitcast(I32).rearrange("p (q r i) -> p r q i", r=8, q=16),
+            )
+
+        grouped, codes, planes = {}, {}, {}
+
+        def turn(s, h, pair, on_act):
+            if (s, h) not in grouped:
+                grouped[s, h] = keep.tile([P, HALF, 4], BF16, name="grouped_%d%d" % (s, h), align_bytes=64)
+                codes[s, h] = keep.tile([P, HALF], U32, name="codes_%d%d" % (s, h), align_bytes=64)
+                planes[s, h] = keep.tile([P, HALF], U8, name="planes_%d%d" % (s, h), align_bytes=64)
+            xt = psum.tile([P, 2, 2, P], F32, name="xt", tag="z", bufs=4)
+            for j in (0, 1):
+                words = raw[s, h][:, 2 * pair + j, :].bitcast(F32)
+                for u in (0, 1):
+                    nc.tensor.transpose(xt[:, j, u, :], words[:, u : D // 2 : 2], ident[:])
+            flat = grouped[s, h][:].rearrange("p n t -> p (n t)")[:, 1024 * pair : 1024 * (pair + 1)]
+            dst = flat.bitcast(F32).rearrange("p (j r u) -> p j r u", j=2, u=2)
+            src = xt[:].rearrange("p j u r -> p j r u")
+            if on_act:
+                nc.scalar.copy(out=dst, in_=src)
+            else:
+                nc.vector.tensor_copy(out=dst, in_=src)
+
+        def quant_in(s, h, c0, c1):
+            nc.vector.quantize_mx(
+                out=codes[s, h][:, c0:c1].bitcast(FP8X4),
+                scales=planes[s, h][:, c0:c1],
+                in_=grouped[s, h][:, c0:c1, :].rearrange("p n t -> p (n t)"),
+            )
+
+        z_tiles, t_tiles, r_tiles, d16_tiles, dq, dpl = {}, {}, {}, {}, {}, {}
+        vcol = keep.tile([P, 24], F32, name="vcol")
+        nvcol = keep.tile([P, 24], F32, name="nvcol")
+
+        def z_mm(u, t):
+            s, h, g, c0, c1 = UNITS[u]
+            r = 4 * g + t
+            z = psum.tile([P, c1 - c0], F32, name="z", tag="z", bufs=4)
+            z_tiles[u, t] = z
+            nc.tensor.matmul_mx(
+                out=z[:],
+                lhsT=w_perm[s][:, 256 * r : 256 * (r + 1)].bitcast(FP4X4),
+                lhsT_scale=wp_perm[s][:, P * r : P * (r + 1)],
+                rhs=codes[s, h][:, c0:c1].bitcast(FP8X4),
+                rhs_scale=planes[s, h][:, c0:c1],
+                start=True,
+                stop=True,
+            )
+
+        def tanh(u, t):
+            s, h, g, c0, c1 = UNITS[u]
+            r = 4 * g + t
+            if t == 0:
+                t_tiles[u] = work.tile([P, 4, c1 - c0], F32, name="th", tag="th", bufs=3, align_bytes=64)
+                r_tiles[u] = work.tile([P, 4, c1 - c0], F32, name="rr", tag="rr", bufs=3, align_bytes=64)
+            nc.scalar.activation(
+                out=t_tiles[u][:, t, :], in_=z_tiles[u, t][:], func=ACT.Tanh, bias=vcol[:, r : r + 1]
+            )
+
+        def factor(u, t):
+            s, h, g = UNITS[u][:3]
+            if u in SQUARE_ON_ACT:
+                if t % 2 == 1:
+                    nc.scalar.activation(
+                        out=r_tiles[u][:, t - 1 : t + 1, :].rearrange("p t n -> p (t n)"),
+                        in_=t_tiles[u][:, t - 1 : t + 1, :].rearrange("p t n -> p (t n)"),
+                        func=ACT.Square,
+                    )
+            else:
+                c = 8 * (s + 1) + 4 * g + t
+                nc.vector.tensor_scalar(
+                    out=r_tiles[u][:, t, :],
+                    in0=t_tiles[u][:, t, :],
+                    scalar1=1.0,
+                    scalar2=nvcol[:, c : c + 1],
+                    op0=ALU.subtract,
+                    op1=ALU.mult,
+                )
+
+        def product(u, part):
+            s, h, g, c0, c1 = UNITS[u]
+            w = c1 - c0
+            if part == 0:
+                d16_tiles[u] = work.tile([P, w, 4], BF16, name="d16", tag="d16", bufs=2, align_bytes=64)
+            c = slice(w // 2 * part, w // 2 * (part + 1))
+            rr = r_tiles[u][:, :, c].rearrange("p t n -> p n t")
+            if u in SQUARE_ON_ACT:
+                col = 8 * (s + 1) + 4 * g
+                nc.vector.scalar_tensor_tensor(
+                    out=d16_tiles[u][:, c, :],
+                    in0=rr,
+                    scalar=1.0,
+                    in1=nvcol[:, col : col + 4].unsqueeze(1).to_broadcast([P, w // 2, 4]),
+                    op0=ALU.subtract,
+                    op1=ALU.mult,
+                )
+            else:
+                nc.vector.scalar_tensor_tensor(
+                    out=d16_tiles[u][:, c, :],
+                    in0=t_tiles[u][:, :, c].rearrange("p t n -> p n t"),
+                    scalar=1.0,
+                    in1=rr,
+                    op0=ALU.add,
+                    op1=ALU.mult,
+                )
+
+        def quant_d(u):
+            s, h, g, c0, c1 = UNITS[u]
+            if c0 == 0:
+                dq[s, h, g] = keep.tile([P, HALF], U32, name="dq_%d%d%d" % (s, h, g), align_bytes=64)
+                dpl[s, h, g] = keep.tile([P, HALF], U8, name="dpl_%d%d%d" % (s, h, g), align_bytes=64)
+            nc.vector.quantize_mx(
+                out=dq[s, h, g][:, c0:c1].bitcast(FP8X4),
+                scales=dpl[s, h, g][:, c0:c1],
+                in_=d16_tiles[u][:].rearrange("p n t -> p (n t)"),
+            )
+
+        gram_ps, base_sb, o_tiles, o16_tiles = {}, {}, {}, {}
+        oq, opl = {}, {}
+
+        def base(j):
+            q, t = STEPS[j]
+            ha, hb = QUADS[q]
+            bp = psum.tile([P, HALF], F32, name="bp", tag="bp", bufs=2)
+            nc.tensor.matmul_mx(
+                out=bp[:],
+                lhsT=codes[0, ha][:, P * t : P * (t + 1)].bitcast(FP8X4),
+                lhsT_scale=planes[0, ha][:, P * t : P * (t + 1)],
+                rhs=codes[1, hb][:].bitcast(FP8X4),
+                rhs_scale=planes[1, hb][:],
+                start=True,
+                stop=True,
+            )
+            bs = work.tile([P, HALF], F32, name="bs", tag="bs", bufs=16, align_bytes=64)
+            base_sb[j] = bs
+            nc.scalar.activation(out=bs[:], in_=bp[:], func=ACT.Copy, scale=SCALE)
+
+        def gram(j):
+            q, t = STEPS[j]
+            ha, hb = QUADS[q]
+            if j >= 12:
+                gp = psum.tile([P, HALF], F32, name="gz", tag="z", bufs=4)
+            else:
+                gp = psum.tile([P, HALF], F32, name="gp", tag="gp", bufs=2)
+            gram_ps[j] = gp
+            for g in (0, 1):
+                nc.tensor.matmul_mx(
+                    out=gp[:],
+                    lhsT=dq[0, ha, g][:, P * t : P * (t + 1)].bitcast(FP8X4),
+                    lhsT_scale=dpl[0, ha, g][:, P * t : P * (t + 1)],
+                    rhs=dq[1, hb, g][:].bitcast(FP8X4),
+                    rhs_scale=dpl[1, hb, g][:],
+                    start=(g == 0),
+                    stop=(g == 1),
+                )
+
+        def hadamard(j):
+            q, t = STEPS[j]
+            if t == 0:
+                o_tiles[q] = work.tile([P, 4, HALF], F32, name="o32", tag="o32", bufs=3, align_bytes=64)
+                o16_tiles[q] = work.tile([P, HALF, 4], BF16, name="o16", tag="o16", bufs=2, align_bytes=64)
+                oq[q] = keep.tile([P, HALF], U32, name="oq%d" % q, align_bytes=64)
+                opl[q] = keep.tile([P, HALF], U8, name="opl%d" % q, align_bytes=64)
+            nc.vector.tensor_tensor(out=o_tiles[q][:, t, :], in0=gram_ps[j][:], in1=base_sb[j][:], op=ALU.mult)
+
+        def store_out(q, t0, t1):
+            ha, hb = QUADS[q]
+            rows = out_0[HALF * ha : HALF * (ha + 1), HALF * hb : HALF * (hb + 1)]
+            nc.sync.dma_start(out=rows.rearrange("(p t) m -> p t m", t=4)[:, t0:t1, :], in_=o_tiles[q][:, t0:t1, :])
+
+        def cast(q, on_act, c0=0, c1=HALF):
+            dst = o16_tiles[q][:, c0:c1, :].rearrange("p (c i) t -> p c t i", i=4)
+            src = o_tiles[q][:, :, c0:c1].rearrange("p t (c i) -> p c t i", i=4)
+            if on_act:
+                nc.scalar.copy(out=dst, in_=src)
+            else:
+                nc.vector.tensor_copy(out=dst, in_=src)
+
+        def quant_o(q, c0=0, c1=HALF):
+            nc.vector.quantize_mx(
+                out=oq[q][:, c0:c1].bitcast(FP8X4),
+                scales=opl[q][:, c0:c1],
+                in_=o16_tiles[q][:, c0:c1, :].rearrange("p n t -> p (n t)"),
+            )
+
+        def store_planes(q, c0=0, c1=HALF):
+            ha, hb = QUADS[q]
+            cols = slice(HALF * hb + c0, HALF * hb + c1)
+            nc.sync.dma_start(
+                out=out_1[ha][:, cols, :].rearrange("p m t -> p (m t)").bitcast(I32),
+                in_=oq[q][:, c0:c1].bitcast(I32),
+            )
+            for k in range(4):
+                nc.sync.dma_start(
+                    out=out_2[ha][4 * k : 4 * k + 4, cols].bitcast(I32),
+                    in_=opl[q][32 * k : 32 * k + 4, c0:c1].bitcast(I32),
+                )
+
+        turn(0, 0, 0, True)
+        permute(0)
+        turn(0, 0, 1, False)
+        quant_in(0, 0, 0, 256)
+        quant_in(0, 0, 256, 512)
+        nc.vector.tensor_copy(out=vec32[0:24, :], in_=vec16[:])
+        vps = psum.tile([P, P], F32, name="vps", tag="bp", bufs=2)
+        nc.tensor.transpose(vps[:], vec32[:], ident[:])
+        nc.vector.tensor_copy(out=vcol[:], in_=vps[:, 0:24])
+        nc.vector.tensor_scalar(
+            out=nvcol[:, 8:24], in0=vcol[:, 8:24], scalar1=-1.0, scalar2=None, op0=ALU.mult
+        )
+
+        tiles = [(u, t) for u in range(len(UNITS)) for t in range(4)]
+        ahead = {"z": 0, "g": 0, "had": 0}
+
+        def z_ahead(k):
+            while ahead["z"] < min(k, len(tiles)):
+                z_mm(*tiles[ahead["z"]])
+                ahead["z"] += 1
+
+        def gram_ahead(j):
+            while ahead["g"] < min(j, 16):
+                gram(ahead["g"])
+                ahead["g"] += 1
+
+        def next_hadamard():
+            j = ahead["had"]
+            hadamard(j)
+            q, t = STEPS[j]
+            if t % 2 == 1:
+                store_out(q, t - 1, t + 1)
+            ahead["had"] += 1
+
+        for k, (u, t) in enumerate(tiles):
+            z_ahead(k + 3)
+            tanh(u, t)
+            if k == 0:
+                turn(1, 0, 0, False)
+                turn(1, 0, 1, False)
+                permute(1)
+            if k == 1:
+                quant_in(1, 0, 0, 512)
+                turn(1, 1, 0, False)
+            if k == 2:
+                turn(1, 1, 1, False)
+            if k == 3:
+                quant_in(1, 1, 0, 512)
+            if k == 5:
+                turn(0, 1, 0, False)
+            if k == 8:
+                turn(0, 1, 1, False)
+            if k == 10:
+                quant_in(0, 1, 0, 512)
+            if k > 0:
+                factor(*tiles[k - 1])
+            for j, at in enumerate(BASE_AT):
+                if at == k:
+                    base(j)
+            if u > 0 and t in (1, 2):
+                product(u - 1, t - 1)
+            if k in HAD_AT:
+                next_hadamard()
+            if u > 0 and t == 3:
+                quant_d(u - 1)
+            if k + 1 in HAD_AT:
+                gram_ahead(HAD_AT.index(k + 1) + 1)
+            if k == 26:
+                cast(0, True)
+            if k == 29:
+                quant_o(0)
+                store_planes(0)
+            if k == 35:
+                cast(1, True)
+            if k == 39:
+                quant_o(1)
+                store_planes(1)
+        factor(*tiles[39])
+        product(9, 0)
+        product(9, 1)
+        quant_d(9)
+        for j in range(12, 16):
+            gram_ahead(j + 3)
+            next_hadamard()
+            if j == 13:
+                cast(2, True)
+        quant_o(2)
+        store_planes(2)
+        cast(3, True, 0, 256)
+        cast(3, False, 256, 512)
+        quant_o(3, 256, 512)
+        store_planes(3, 256, 512)
+        quant_o(3, 0, 256)
+        store_planes(3, 0, 256)

@@ -15,22 +15,26 @@ ALU = mybir.AluOpType
 
 N, M, D, F = 1024, 1024, 512, 1024
 P = 128
-HALF = 512
+BANK = 512
+CHUNK = 256
+RUN = 4
 FLOPS = 2 * (N * D * F + M * D * F + N * D * M + N * F * M)
 SCALE = 1.0 / (32.0 * 512.0 ** 0.5)
+X, Y = 0, 1
 
-UNITS = [
-    (0, 0, 0, 0, 512), (0, 0, 1, 0, 512), (1, 0, 0, 0, 512), (1, 0, 1, 0, 512), (1, 1, 0, 0, 512), (1, 1, 1, 0, 512),
-    (0, 1, 0, 0, 256), (0, 1, 1, 0, 256), (0, 1, 0, 256, 512), (0, 1, 1, 256, 512),
-]
-QUADS = [(0, 0), (0, 1), (1, 0), (1, 1)]
-STEPS = [
-    (0, 0), (0, 1), (0, 2), (0, 3), (1, 0), (1, 1), (1, 2), (1, 3),
-    (2, 0), (2, 1), (3, 0), (3, 1), (2, 2), (2, 3), (3, 2), (3, 3),
-]
-SQUARE_ON_ACT = (4, 5, 6, 7, 8)
-BASE_AT = [5, 6, 7, 8, 9, 10, 11, 12, 13, 14, 15, 16, 17, 18, 19, 20]
-HAD_AT = [20, 21, 22, 23, 28, 29, 30, 31, 36, 37, 38, 39]
+
+def narrow(side, chunk):
+    return [(side, g, chunk, 1) for g in (0, 1)]
+
+
+def wide(side, chunk, g):
+    return [(side, g, chunk, 2)]
+
+
+UNITS = [narrow(X, 0), narrow(X, 1), wide(X, 2, 0), wide(X, 2, 1)] + [narrow(Y, j) for j in range(4)]
+X_UNITS = 4
+ACT_BANKS = (0, 2)
+SHARED = (1, 2, 3, 7)
 
 
 def tile_twotimehiddentangentkernel_x2_kernel(
@@ -43,355 +47,408 @@ def tile_twotimehiddentangentkernel_x2_kernel(
         psum = ctx.enter_context(tc.psum_pool(name="psum", bufs=1))
         ctx.enter_context(tc.manual_schedule())
 
+        def act_bank(name):
+            return psum.tile([P, BANK], F32, name=name, tag="act", bufs=5)
+
+        def dve_bank(name):
+            return psum.tile([P, BANK], F32, name=name, tag="dve", bufs=3)
+
+        plane_raw = [keep.tile([P, F], U8, name="plane_raw%d" % s, align_bytes=64) for s in (X, Y)]
+        nc.vector.memset(plane_raw[X][:].bitcast(I32), 0)
         warm = keep.tile([P, 1], F32, name="warm")
         nc.vector.memset(warm[:], 0.0)
-        nc.scalar.activation(out=warm[:], in_=warm[:], func=ACT.Tanh)
+        nc.scalar.activation(out=warm[:], in_=warm[:], func=ACT.Sigmoid)
+        nc.vector.memset(plane_raw[Y][:].bitcast(I32), 0)
+        vec16 = keep.tile([P, P], BF16, name="vec16", align_bytes=64)
+        nc.vector.memset(vec16[:], 0.0)
 
         ident = keep.tile([P, P], F32, name="ident", align_bytes=64)
         make_identity(nc, ident[:])
+        ident16 = keep.tile([P, P], BF16, name="ident16", align_bytes=64)
+        nc.vector.tensor_copy(out=ident16[:], in_=ident[:])
 
         raw = {}
-        for s in (0, 1):
-            for h in (0, 1):
-                raw[s, h] = keep.tile([P, 4, D], BF16, name="raw_%d%d" % (s, h), align_bytes=64)
 
-        def load_rows(s, h, j0, j1):
-            src = (x, y)[s][HALF * h : HALF * (h + 1), :]
-            view = src.rearrange("(p t) k -> p t k", t=4) if s == 0 else src.rearrange("(t p) k -> p t k", t=4)
-            nc.sync.dma_start(out=raw[s, h][:, j0:j1, :], in_=view[:, j0:j1, :])
+        def load_rows(side, chunk):
+            raw[side, chunk] = keep.tile([P, 2, D], BF16, name="raw_%d%d" % (side, chunk), align_bytes=64)
+            if side == X:
+                group = x[BANK * (chunk // 2) : BANK * (chunk // 2 + 1), :].rearrange("(p t) k -> p t k", t=4)
+                view = group[:, 2 * (chunk % 2) : 2 * (chunk % 2) + 2, :]
+            else:
+                view = y[CHUNK * chunk : CHUNK * (chunk + 1), :].rearrange("(j p) k -> p j k", j=2)
+            nc.sync.dma_start(out=raw[side, chunk][:], in_=view)
 
-        w_raw = [keep.tile([P, 2 * F], U8, name="w_raw%d" % s, align_bytes=64) for s in (0, 1)]
-        w_perm = [keep.tile([P, 2 * F], U8, name="w_perm%d" % s, align_bytes=64) for s in (0, 1)]
-        wp_raw = [keep.tile([P, F], U8, name="wp_raw%d" % s, align_bytes=64) for s in (0, 1)]
-        wp_perm = [keep.tile([P, F], U8, name="wp_perm%d" % s, align_bytes=64) for s in (0, 1)]
-        for s in (0, 1):
-            nc.vector.memset(wp_raw[s][:].bitcast(I32), 0)
+        w_raw = [keep.tile([P, 2 * F], U8, name="w_raw%d" % s, align_bytes=64) for s in (X, Y)]
+        w_perm = [keep.tile([P, 2 * F], U8, name="w_perm%d" % s, align_bytes=64) for s in (X, Y)]
+        plane_perm = [keep.tile([P, F], U8, name="plane_perm%d" % s, align_bytes=64) for s in (X, Y)]
 
-        def load_words(s):
-            nc.sync.dma_start(out=w_raw[s][:].bitcast(I32), in_=(wa_words, wb_words)[s][0].bitcast(I32))
-
-        def load_scales(s):
+        def load_weight(side):
             for q in range(4):
-                nc.scalar.dma_start(
-                    out=wp_raw[s][32 * q : 32 * q + 4, :].bitcast(I32),
-                    in_=(wa_scales, wb_scales)[s][0][4 * q : 4 * q + 4, :].bitcast(I32),
+                nc.sync.dma_start(
+                    out=plane_raw[side][32 * q : 32 * q + 4, :].bitcast(I32),
+                    in_=(wa_scales, wb_scales)[side][0][4 * q : 4 * q + 4, :].bitcast(I32),
                 )
+            nc.sync.dma_start(out=w_raw[side][:].bitcast(I32), in_=(wa_words, wb_words)[side][0].bitcast(I32))
 
-        vec16 = keep.tile([24, P], BF16, name="vec16")
-        vec32 = keep.tile([P, P], F32, name="vec32", align_bytes=64)
-        nc.vector.memset(vec32[:], 0.0)
-
-        load_rows(0, 0, 0, 2)
-        load_scales(0)
-        load_words(0)
-        load_rows(0, 0, 2, 4)
-        for j, v in enumerate((b, va, vb)):
-            nc.gpsimd.dma_start(
+        def load_vector(j, v):
+            nc.sync.dma_start(
                 out=vec16[8 * j : 8 * j + 8, :].rearrange("r (q i) -> r q i", i=8),
                 in_=v.rearrange("(q r i) -> r q i", r=8, i=8),
             )
-        load_rows(1, 0, 0, 4)
-        load_words(1)
-        load_scales(1)
-        load_rows(1, 1, 0, 4)
-        load_rows(0, 1, 0, 4)
 
-        def permute(s):
-            nc.vector.tensor_copy(
-                out=w_perm[s][:].bitcast(I32).rearrange("p (r q i) -> p r q i", r=8, q=16),
-                in_=w_raw[s][:].bitcast(I32).rearrange("p (q r i) -> p r q i", r=8, q=16),
-            )
-            nc.vector.tensor_copy(
-                out=wp_perm[s][:].bitcast(I32).rearrange("p (r q i) -> p r q i", r=8, q=16),
-                in_=wp_raw[s][:].bitcast(I32).rearrange("p (q r i) -> p r q i", r=8, q=16),
-            )
+        load_rows(X, 0)
+        load_weight(X)
+        load_rows(X, 1)
+        for j, v in enumerate((b, va, vb)):
+            load_vector(j, v)
+        load_rows(X, 2)
+        load_rows(X, 3)
+        load_rows(Y, 0)
+        load_weight(Y)
+        for chunk in (1, 2, 3):
+            load_rows(Y, chunk)
 
-        grouped, codes, planes = {}, {}, {}
+        def permute(side):
+            for dst, src in ((w_perm, w_raw), (plane_perm, plane_raw)):
+                nc.vector.tensor_copy(
+                    out=dst[side][:].bitcast(I32).rearrange("p (r q i) -> p r q i", r=8, q=16),
+                    in_=src[side][:].bitcast(I32).rearrange("p (q r i) -> p r q i", r=8, q=16),
+                )
 
-        def turn(s, h, pair, on_act):
-            if (s, h) not in grouped:
-                grouped[s, h] = keep.tile([P, HALF, 4], BF16, name="grouped_%d%d" % (s, h), align_bytes=64)
-                codes[s, h] = keep.tile([P, HALF], U32, name="codes_%d%d" % (s, h), align_bytes=64)
-                planes[s, h] = keep.tile([P, HALF], U8, name="planes_%d%d" % (s, h), align_bytes=64)
-            xt = psum.tile([P, 2, 2, P], F32, name="xt", tag="z", bufs=4)
+        grouped, turned = {}, {}
+        codes = [keep.tile([P, N], U32, name="codes%d" % s, align_bytes=64) for s in (X, Y)]
+        planes = [keep.tile([P, N], U8, name="planes%d" % s, align_bytes=64) for s in (X, Y)]
+
+        def transposes(side, chunk, bank):
+            turned[side, chunk] = bank
             for j in (0, 1):
-                words = raw[s, h][:, 2 * pair + j, :].bitcast(F32)
+                words = raw[side, chunk][:, j, :].bitcast(F32)
                 for u in (0, 1):
-                    nc.tensor.transpose(xt[:, j, u, :], words[:, u : D // 2 : 2], ident[:])
-            flat = grouped[s, h][:].rearrange("p n t -> p (n t)")[:, 1024 * pair : 1024 * (pair + 1)]
-            dst = flat.bitcast(F32).rearrange("p (j r u) -> p j r u", j=2, u=2)
-            src = xt[:].rearrange("p j u r -> p j r u")
+                    col = P * (2 * j + u)
+                    nc.tensor.transpose(bank[:, col : col + P], words[:, u : D // 2 : 2], ident[:])
+
+        def turn_out(side, chunk, on_act):
+            g16 = keep.tile([P, 4 * CHUNK], BF16, name="grouped_%d%d" % (side, chunk), align_bytes=64)
+            grouped[side, chunk] = g16
+            dst = g16[:].bitcast(F32).rearrange("p (j r u) -> p j r u", j=2, u=2)
+            src = turned[side, chunk][:].rearrange("p (j u r) -> p j r u", j=2, u=2)
             if on_act:
                 nc.scalar.copy(out=dst, in_=src)
             else:
                 nc.vector.tensor_copy(out=dst, in_=src)
 
-        def quant_in(s, h, c0, c1):
+        def quant_in(side, chunk):
+            cols = slice(CHUNK * chunk, CHUNK * (chunk + 1))
             nc.vector.quantize_mx(
-                out=codes[s, h][:, c0:c1].bitcast(FP8X4),
-                scales=planes[s, h][:, c0:c1],
-                in_=grouped[s, h][:, c0:c1, :].rearrange("p n t -> p (n t)"),
+                out=codes[side][:, cols].bitcast(FP8X4), scales=planes[side][:, cols], in_=grouped[side, chunk][:]
             )
 
-        z_tiles, t_tiles, r_tiles, d16_tiles, dq, dpl = {}, {}, {}, {}, {}, {}
-        vcol = keep.tile([P, 24], F32, name="vcol")
-        nvcol = keep.tile([P, 24], F32, name="nvcol")
+        vcol = keep.tile([P, 40], F32, name="vcol")
 
-        def z_mm(u, t):
-            s, h, g, c0, c1 = UNITS[u]
-            r = 4 * g + t
-            z = psum.tile([P, c1 - c0], F32, name="z", tag="z", bufs=4)
-            z_tiles[u, t] = z
-            nc.tensor.matmul_mx(
-                out=z[:],
-                lhsT=w_perm[s][:, 256 * r : 256 * (r + 1)].bitcast(FP4X4),
-                lhsT_scale=wp_perm[s][:, P * r : P * (r + 1)],
-                rhs=codes[s, h][:, c0:c1].bitcast(FP8X4),
-                rhs_scale=planes[s, h][:, c0:c1],
-                start=True,
-                stop=True,
-            )
+        def turn_vectors():
+            bank = psum.tile([P, 2 * BANK], BF16, name="vbank", tag="dve", bufs=3)
+            nc.tensor.transpose(bank[:, 0:P], vec16[:], ident16[:])
+            return bank
 
-        def tanh(u, t):
-            s, h, g, c0, c1 = UNITS[u]
-            r = 4 * g + t
-            if t == 0:
-                t_tiles[u] = work.tile([P, 4, c1 - c0], F32, name="th", tag="th", bufs=3, align_bytes=64)
-                r_tiles[u] = work.tile([P, 4, c1 - c0], F32, name="rr", tag="rr", bufs=3, align_bytes=64)
-            nc.scalar.activation(
-                out=t_tiles[u][:, t, :], in_=z_tiles[u, t][:], func=ACT.Tanh, bias=vcol[:, r : r + 1]
-            )
-
-        def factor(u, t):
-            s, h, g = UNITS[u][:3]
-            if u in SQUARE_ON_ACT:
-                if t % 2 == 1:
-                    nc.scalar.activation(
-                        out=r_tiles[u][:, t - 1 : t + 1, :].rearrange("p t n -> p (t n)"),
-                        in_=t_tiles[u][:, t - 1 : t + 1, :].rearrange("p t n -> p (t n)"),
-                        func=ACT.Square,
-                    )
-            else:
-                c = 8 * (s + 1) + 4 * g + t
+        def vectors_out(bank):
+            for dst, src, factor in ((0, 0, 2.0), (8, 8, -4.0), (24, 8, 4.0)):
+                width = 8 if src == 0 else 16
                 nc.vector.tensor_scalar(
-                    out=r_tiles[u][:, t, :],
-                    in0=t_tiles[u][:, t, :],
-                    scalar1=1.0,
-                    scalar2=nvcol[:, c : c + 1],
-                    op0=ALU.subtract,
-                    op1=ALU.mult,
+                    out=vcol[:, dst : dst + width], in0=bank[:, src : src + width],
+                    scalar1=factor, scalar2=None, op0=ALU.mult,
                 )
 
-        def product(u, part):
-            s, h, g, c0, c1 = UNITS[u]
-            w = c1 - c0
-            if part == 0:
-                d16_tiles[u] = work.tile([P, w, 4], BF16, name="d16", tag="d16", bufs=2, align_bytes=64)
-            c = slice(w // 2 * part, w // 2 * (part + 1))
-            rr = r_tiles[u][:, :, c].rearrange("p t n -> p n t")
-            if u in SQUARE_ON_ACT:
-                col = 8 * (s + 1) + 4 * g
-                nc.vector.scalar_tensor_tensor(
-                    out=d16_tiles[u][:, c, :],
-                    in0=rr,
-                    scalar=1.0,
-                    in1=nvcol[:, col : col + 4].unsqueeze(1).to_broadcast([P, w // 2, 4]),
-                    op0=ALU.subtract,
-                    op1=ALU.mult,
-                )
-            else:
-                nc.vector.scalar_tensor_tensor(
-                    out=d16_tiles[u][:, c, :],
-                    in0=t_tiles[u][:, :, c].rearrange("p t n -> p n t"),
-                    scalar=1.0,
-                    in1=rr,
-                    op0=ALU.add,
-                    op1=ALU.mult,
-                )
+        z_banks, sig, fac, d16, d_codes, d_planes, d_at = {}, {}, {}, {}, {}, {}, {}
 
-        def quant_d(u):
-            s, h, g, c0, c1 = UNITS[u]
-            if c0 == 0:
-                dq[s, h, g] = keep.tile([P, HALF], U32, name="dq_%d%d%d" % (s, h, g), align_bytes=64)
-                dpl[s, h, g] = keep.tile([P, HALF], U8, name="dpl_%d%d%d" % (s, h, g), align_bytes=64)
-            nc.vector.quantize_mx(
-                out=dq[s, h, g][:, c0:c1].bitcast(FP8X4),
-                scales=dpl[s, h, g][:, c0:c1],
-                in_=d16_tiles[u][:].rearrange("p n t -> p (n t)"),
-            )
+        def segments(u):
+            col = 0
+            found = []
+            for side, g, chunk, chunks in UNITS[u]:
+                found.append((side, g, CHUNK * chunk, slice(col, col + CHUNK * chunks)))
+                col = col + CHUNK * chunks
+            return found
 
-        gram_ps, base_sb, o_tiles, o16_tiles = {}, {}, {}, {}
-        oq, opl = {}, {}
+        def pieces(u, k):
+            parts = [(seg, t) for seg in segments(u) for t in range(4)]
+            each = len(parts) // 4
+            width = BANK // each
+            return [(parts[each * k + i], slice(width * i, width * (i + 1))) for i in range(each)]
 
-        def base(j):
-            q, t = STEPS[j]
-            ha, hb = QUADS[q]
-            bp = psum.tile([P, HALF], F32, name="bp", tag="bp", bufs=2)
-            nc.tensor.matmul_mx(
-                out=bp[:],
-                lhsT=codes[0, ha][:, P * t : P * (t + 1)].bitcast(FP8X4),
-                lhsT_scale=planes[0, ha][:, P * t : P * (t + 1)],
-                rhs=codes[1, hb][:].bitcast(FP8X4),
-                rhs_scale=planes[1, hb][:],
-                start=True,
-                stop=True,
-            )
-            bs = work.tile([P, HALF], F32, name="bs", tag="bs", bufs=16, align_bytes=64)
-            base_sb[j] = bs
-            nc.scalar.activation(out=bs[:], in_=bp[:], func=ACT.Copy, scale=SCALE)
-
-        def gram(j):
-            q, t = STEPS[j]
-            ha, hb = QUADS[q]
-            if j >= 12:
-                gp = psum.tile([P, HALF], F32, name="gz", tag="z", bufs=4)
-            else:
-                gp = psum.tile([P, HALF], F32, name="gp", tag="gp", bufs=2)
-            gram_ps[j] = gp
-            for g in (0, 1):
+        def z_mm(u, k):
+            z = act_bank("z")
+            z_banks[u, k] = z
+            for ((side, g, tok, cols), t), at in pieces(u, k):
+                r = 4 * g + t
+                toks = slice(tok, tok + cols.stop - cols.start)
                 nc.tensor.matmul_mx(
-                    out=gp[:],
-                    lhsT=dq[0, ha, g][:, P * t : P * (t + 1)].bitcast(FP8X4),
-                    lhsT_scale=dpl[0, ha, g][:, P * t : P * (t + 1)],
-                    rhs=dq[1, hb, g][:].bitcast(FP8X4),
-                    rhs_scale=dpl[1, hb, g][:],
-                    start=(g == 0),
-                    stop=(g == 1),
+                    out=z[:, at],
+                    lhsT=w_perm[side][:, 2 * P * r : 2 * P * (r + 1)].bitcast(FP4X4),
+                    lhsT_scale=plane_perm[side][:, P * r : P * (r + 1)],
+                    rhs=codes[side][:, toks].bitcast(FP8X4),
+                    rhs_scale=planes[side][:, toks],
+                    start=True,
+                    stop=True,
                 )
 
-        def hadamard(j):
-            q, t = STEPS[j]
-            if t == 0:
-                o_tiles[q] = work.tile([P, 4, HALF], F32, name="o32", tag="o32", bufs=3, align_bytes=64)
-                o16_tiles[q] = work.tile([P, HALF, 4], BF16, name="o16", tag="o16", bufs=2, align_bytes=64)
-                oq[q] = keep.tile([P, HALF], U32, name="oq%d" % q, align_bytes=64)
-                opl[q] = keep.tile([P, HALF], U8, name="opl%d" % q, align_bytes=64)
-            nc.vector.tensor_tensor(out=o_tiles[q][:, t, :], in0=gram_ps[j][:], in1=base_sb[j][:], op=ALU.mult)
-
-        def store_out(q, t0, t1):
-            ha, hb = QUADS[q]
-            rows = out_0[HALF * ha : HALF * (ha + 1), HALF * hb : HALF * (hb + 1)]
-            nc.sync.dma_start(out=rows.rearrange("(p t) m -> p t m", t=4)[:, t0:t1, :], in_=o_tiles[q][:, t0:t1, :])
-
-        def cast(q, on_act, c0=0, c1=HALF):
-            dst = o16_tiles[q][:, c0:c1, :].rearrange("p (c i) t -> p c t i", i=4)
-            src = o_tiles[q][:, :, c0:c1].rearrange("p t (c i) -> p c t i", i=4)
-            if on_act:
-                nc.scalar.copy(out=dst, in_=src)
-            else:
-                nc.vector.tensor_copy(out=dst, in_=src)
-
-        def quant_o(q, c0=0, c1=HALF):
-            nc.vector.quantize_mx(
-                out=oq[q][:, c0:c1].bitcast(FP8X4),
-                scales=opl[q][:, c0:c1],
-                in_=o16_tiles[q][:, c0:c1, :].rearrange("p n t -> p (n t)"),
-            )
-
-        def store_planes(q, c0=0, c1=HALF):
-            ha, hb = QUADS[q]
-            cols = slice(HALF * hb + c0, HALF * hb + c1)
-            nc.sync.dma_start(
-                out=out_1[ha][:, cols, :].rearrange("p m t -> p (m t)").bitcast(I32),
-                in_=oq[q][:, c0:c1].bitcast(I32),
-            )
-            for k in range(4):
-                nc.sync.dma_start(
-                    out=out_2[ha][4 * k : 4 * k + 4, cols].bitcast(I32),
-                    in_=opl[q][32 * k : 32 * k + 4, c0:c1].bitcast(I32),
-                )
-
-        turn(0, 0, 0, True)
-        permute(0)
-        turn(0, 0, 1, False)
-        quant_in(0, 0, 0, 256)
-        quant_in(0, 0, 256, 512)
-        nc.vector.tensor_copy(out=vec32[0:24, :], in_=vec16[:])
-        vps = psum.tile([P, P], F32, name="vps", tag="bp", bufs=2)
-        nc.tensor.transpose(vps[:], vec32[:], ident[:])
-        nc.vector.tensor_copy(out=vcol[:], in_=vps[:, 0:24])
-        nc.vector.tensor_scalar(
-            out=nvcol[:, 8:24], in0=vcol[:, 8:24], scalar1=-1.0, scalar2=None, op0=ALU.mult
-        )
-
-        tiles = [(u, t) for u in range(len(UNITS)) for t in range(4)]
-        ahead = {"z": 0, "g": 0, "had": 0}
-
-        def z_ahead(k):
-            while ahead["z"] < min(k, len(tiles)):
-                z_mm(*tiles[ahead["z"]])
-                ahead["z"] += 1
-
-        def gram_ahead(j):
-            while ahead["g"] < min(j, 16):
-                gram(ahead["g"])
-                ahead["g"] += 1
-
-        def next_hadamard():
-            j = ahead["had"]
-            hadamard(j)
-            q, t = STEPS[j]
-            if t % 2 == 1:
-                store_out(q, t - 1, t + 1)
-            ahead["had"] += 1
-
-        for k, (u, t) in enumerate(tiles):
-            z_ahead(k + 3)
-            tanh(u, t)
+        def sigmoid(u, k):
             if k == 0:
-                turn(1, 0, 0, False)
-                turn(1, 0, 1, False)
-                permute(1)
-            if k == 1:
-                quant_in(1, 0, 0, 512)
-                turn(1, 1, 0, False)
-            if k == 2:
-                turn(1, 1, 1, False)
-            if k == 3:
-                quant_in(1, 1, 0, 512)
-            if k == 5:
-                turn(0, 1, 0, False)
-            if k == 8:
-                turn(0, 1, 1, False)
-            if k == 10:
-                quant_in(0, 1, 0, 512)
-            if k > 0:
-                factor(*tiles[k - 1])
-            for j, at in enumerate(BASE_AT):
-                if at == k:
-                    base(j)
-            if u > 0 and t in (1, 2):
-                product(u - 1, t - 1)
-            if k in HAD_AT:
-                next_hadamard()
-            if u > 0 and t == 3:
-                quant_d(u - 1)
-            if k + 1 in HAD_AT:
-                gram_ahead(HAD_AT.index(k + 1) + 1)
-            if k == 26:
-                cast(0, True)
-            if k == 29:
-                quant_o(0)
-                store_planes(0)
-            if k == 35:
-                cast(1, True)
-            if k == 39:
-                quant_o(1)
-                store_planes(1)
-        factor(*tiles[39])
-        product(9, 0)
-        product(9, 1)
-        quant_d(9)
-        for j in range(12, 16):
-            gram_ahead(j + 3)
-            next_hadamard()
-            if j == 13:
-                cast(2, True)
-        quant_o(2)
-        store_planes(2)
-        cast(3, True, 0, 256)
-        cast(3, False, 256, 512)
-        quant_o(3, 256, 512)
-        store_planes(3, 256, 512)
-        quant_o(3, 0, 256)
-        store_planes(3, 0, 256)
+                sig[u] = work.tile([P, 4, BANK], F32, name="sig", tag="sig", bufs=3, align_bytes=64)
+                fac[u] = work.tile([P, 4, BANK], F32, name="fac", tag="fac", bufs=3, align_bytes=64)
+            for ((side, g, tok, cols), t), at in pieces(u, k):
+                r = 4 * g + t
+                nc.scalar.activation(
+                    out=sig[u][:, t, cols], in_=z_banks[u, k][:, at], func=ACT.Sigmoid,
+                    bias=vcol[:, r : r + 1], scale=2.0,
+                )
+
+        def factor(u, k, on_act):
+            for ((side, g, tok, cols), t), at in pieces(u, k):
+                c = 8 + 8 * side + 4 * g + t
+                if on_act:
+                    nc.scalar.activation(
+                        out=fac[u][:, t, cols], in_=sig[u][:, t, cols], func=ACT.Identity,
+                        bias=vcol[:, c + 16 : c + 17], scale=vcol[:, c : c + 1],
+                    )
+                else:
+                    nc.vector.tensor_scalar(
+                        out=fac[u][:, t, cols], in0=sig[u][:, t, cols],
+                        scalar1=1.0, scalar2=vcol[:, c : c + 1], op0=ALU.subtract, op1=ALU.mult,
+                    )
+
+        def by_runs(tile4, cols):
+            return tile4[:, :, cols].rearrange("p t (c i) -> p c t i", i=RUN)
+
+        def into_words(tile16, cols):
+            return tile16[:, cols, :].rearrange("p (c i) t -> p c t i", i=RUN)
+
+        def product(u, cols):
+            if cols.start == 0:
+                d16[u] = work.tile([P, BANK, 4], BF16, name="d16", tag="d16", bufs=2, align_bytes=64)
+            nc.vector.tensor_tensor(
+                out=into_words(d16[u], cols), in0=by_runs(sig[u], cols), in1=by_runs(fac[u], cols), op=ALU.mult
+            )
+
+        def quant_d(u, cols):
+            if cols.start == 0:
+                d_codes[u] = keep.tile([P, BANK], U32, name="d_codes%d" % u, align_bytes=64)
+                d_planes[u] = keep.tile([P, BANK], U8, name="d_planes%d" % u, align_bytes=64)
+                for side, g, tok, seg in segments(u):
+                    for k in range(0, seg.stop - seg.start, P):
+                        d_at[side, g, tok + k] = (u, seg.start + k)
+            nc.vector.quantize_mx(
+                out=d_codes[u][:, cols].bitcast(FP8X4),
+                scales=d_planes[u][:, cols],
+                in_=d16[u][:, cols, :].rearrange("p n t -> p (n t)"),
+            )
+
+        base_banks, gram_banks, base_sb, o32, o16 = {}, {}, {}, {}, {}
+
+        def tiles_of(k):
+            return [(k // 2, 2 * (k % 2) + i, slice(CHUNK * i, CHUNK * (i + 1))) for i in (0, 1)]
+
+        def base_mm(j, k):
+            bank = act_bank("base")
+            base_banks[j, k] = bank
+            toks = slice(CHUNK * j, CHUNK * (j + 1))
+            for h, t, cols in tiles_of(k):
+                rows = slice(BANK * h + P * t, BANK * h + P * (t + 1))
+                nc.tensor.matmul_mx(
+                    out=bank[:, cols],
+                    lhsT=codes[X][:, rows].bitcast(FP8X4),
+                    lhsT_scale=planes[X][:, rows],
+                    rhs=codes[Y][:, toks].bitcast(FP8X4),
+                    rhs_scale=planes[Y][:, toks],
+                    start=True,
+                    stop=True,
+                )
+
+        def base_out(j, k):
+            base_sb[j, k] = work.tile([P, BANK], F32, name="base_sb", tag="base_sb", bufs=8, align_bytes=64)
+            nc.scalar.activation(out=base_sb[j, k][:], in_=base_banks[j, k][:], func=ACT.Copy, scale=SCALE)
+
+        def gram_mm(j, k, g, bank=None):
+            if bank is not None:
+                gram_banks[j, k] = bank
+            for i, (h, t, cols) in enumerate(tiles_of(k)):
+                ux, cx = d_at[X, g, BANK * h + P * t]
+                uy, cy = d_at[Y, g, CHUNK * j]
+                nc.tensor.matmul_mx(
+                    out=gram_banks[j, k][:, cols],
+                    lhsT=d_codes[ux][:, cx : cx + P].bitcast(FP8X4),
+                    lhsT_scale=d_planes[ux][:, cx : cx + P],
+                    rhs=d_codes[uy][:, cy : cy + CHUNK].bitcast(FP8X4),
+                    rhs_scale=d_planes[uy][:, cy : cy + CHUNK],
+                    start=(g == 0 and i == 0),
+                    stop=(g == 1 and i == 1),
+                )
+
+        def gram(j, k):
+            gram_mm(j, k, 0, dve_bank("gram"))
+            gram_mm(j, k, 1)
+
+        def half(h):
+            return slice(CHUNK * h, CHUNK * (h + 1))
+
+        def hadamard(j, k):
+            if k == 0:
+                o32[j] = work.tile([P, 4, BANK], F32, name="o32", tag="o32", bufs=3, align_bytes=64)
+                o16[j] = work.tile([P, BANK, 4], BF16, name="o16", tag="o16", bufs=2, align_bytes=64)
+            h, t0 = k // 2, 2 * (k % 2)
+            nc.vector.tensor_tensor(
+                out=o32[j][:, t0 : t0 + 2, half(h)],
+                in0=gram_banks[j, k][:].rearrange("p (t c) -> p t c", t=2),
+                in1=base_sb[j, k][:].rearrange("p (t c) -> p t c", t=2),
+                op=ALU.mult,
+            )
+            rows = out_0[BANK * h : BANK * (h + 1), CHUNK * j : CHUNK * (j + 1)].rearrange("(p t) m -> p t m", t=4)
+            nc.sync.dma_start(out=rows[:, t0 : t0 + 2, :], in_=o32[j][:, t0 : t0 + 2, half(h)])
+
+        def cast(j, cols, on_act):
+            if on_act:
+                nc.scalar.copy(out=into_words(o16[j], cols), in_=by_runs(o32[j], cols))
+            else:
+                nc.vector.tensor_copy(out=into_words(o16[j], cols), in_=by_runs(o32[j], cols))
+
+        o_codes = keep.tile([P, 2, M], U32, name="o_codes", align_bytes=64)
+        o_planes = keep.tile([P, 2, M], U8, name="o_planes", align_bytes=64)
+
+        def quant_o(j, h):
+            toks = slice(CHUNK * j, CHUNK * (j + 1))
+            nc.vector.quantize_mx(
+                out=o_codes[:, h, toks].bitcast(FP8X4),
+                scales=o_planes[:, h, toks],
+                in_=o16[j][:, half(h), :].rearrange("p n t -> p (n t)"),
+            )
+
+        def store_words(j, h0, h1, queue):
+            toks = slice(CHUNK * j, CHUNK * (j + 1))
+            queue.dma_start(
+                out=out_1[h0:h1, :, toks, :].rearrange("h p m t -> p h (m t)").bitcast(I32),
+                in_=o_codes[:, h0:h1, toks].bitcast(I32),
+            )
+
+        def store_scales(j0, j1, queues):
+            toks = slice(CHUNK * j0, CHUNK * j1)
+            for q in range(4):
+                queues[q % len(queues)].dma_start(
+                    out=out_2[:, 4 * q : 4 * q + 4, toks].rearrange("h r m -> r h m").bitcast(I32),
+                    in_=o_planes[32 * q : 32 * q + 4, :, toks].bitcast(I32),
+                )
+
+        whole = slice(0, BANK)
+
+        def shared(u):
+            return ACT_BANKS if u in SHARED else ()
+
+        def act_unit(u, staged):
+            for k in range(4):
+                if k + staged < 4:
+                    z_mm(u, k + staged)
+                sigmoid(u, k)
+                if k - 1 in shared(u):
+                    factor(u, k - 1, True)
+
+        def dve_factors(u, banks):
+            for k in banks:
+                if k not in shared(u):
+                    factor(u, k, False)
+
+        transposes(X, 0, act_bank("turn"))
+        transposes(X, 1, act_bank("turn"))
+        vbank = turn_vectors()
+        turn_out(X, 0, True)
+        permute(X)
+        quant_in(X, 0)
+        turn_out(X, 1, True)
+        vectors_out(vbank)
+        quant_in(X, 1)
+        for k in range(2):
+            z_mm(0, k)
+        transposes(X, 2, dve_bank("turn"))
+        act_unit(0, 2)
+        dve_factors(0, (0,))
+        turn_out(X, 2, False)
+        dve_factors(0, (1,))
+        quant_in(X, 2)
+        product(0, half(0))
+        z_mm(1, 0)
+        transposes(X, 3, dve_bank("turn"))
+        dve_factors(0, (2, 3))
+        turn_out(X, 3, False)
+        act_unit(1, 1)
+        product(0, half(1))
+        quant_in(X, 3)
+        permute(Y)
+
+        for u in range(1, X_UNITS):
+            transposes(Y, u - 1, act_bank("turn"))
+            if u + 1 < X_UNITS:
+                z_mm(u + 1, 0)
+            turn_out(Y, u - 1, True)
+            dve_factors(u, range(4))
+            quant_d(u - 1, whole)
+            product(u, whole)
+            quant_in(Y, u - 1)
+            act_unit(u + 1, 1 if u + 1 < X_UNITS else 0)
+
+        last = len(UNITS) - 1
+        for u in range(X_UNITS, last + 1):
+            j = u - X_UNITS - 1
+            if u == X_UNITS:
+                transposes(Y, 3, act_bank("turn"))
+                turn_out(Y, 3, True)
+            if j > 0:
+                cast(j - 1, whole, True)
+            dve_factors(u, range(4))
+            quant_d(u - 1, whole)
+            if u == X_UNITS + 1:
+                quant_in(Y, 3)
+            if u < last:
+                for k in range(4):
+                    z_mm(u + 1, k)
+            if j >= 0:
+                for k in range(3):
+                    gram(j, k)
+            if u < last:
+                act_unit(u + 1, 4)
+            product(u, half(0))
+            base_mm(j + 1, 0)
+            if j >= 0:
+                hadamard(j, 0)
+                gram(j, 3)
+            for k in range(4):
+                if k < 3:
+                    base_mm(j + 1, k + 1)
+                base_out(j + 1, k)
+            if u == last:
+                quant_d(u, half(0))
+                for k in range(4):
+                    gram_mm(j + 1, k, 0, act_bank("gram"))
+            if j >= 0:
+                hadamard(j, 1)
+            product(u, half(1))
+            if j >= 0:
+                hadamard(j, 2)
+                hadamard(j, 3)
+            if u == last:
+                quant_d(u, half(1))
+            if j > 0:
+                for h in (0, 1):
+                    quant_o(j - 1, h)
+                store_words(j - 1, 0, 2, nc.sync)
+        j = last - X_UNITS
+        store_scales(0, j - 1, [nc.sync])
+        cast(j - 1, whole, True)
+        for k in range(4):
+            gram_mm(j, k, 1)
+            hadamard(j, k)
+        cast(j, half(0), True)
+        for h in (0, 1):
+            quant_o(j - 1, h)
+        store_words(j - 1, 0, 2, nc.sync)
+        cast(j, half(1), False)
+        quant_o(j, 0)
+        store_words(j, 0, 1, nc.sync)
+        quant_o(j, 1)
+        store_scales(j - 1, j + 1, [nc.scalar, nc.sync])
+        store_words(j, 1, 2, nc.scalar)

@@ -24,17 +24,19 @@ X, Y = 0, 1
 
 
 def narrow(side, chunk):
-    return [(side, g, chunk, 1) for g in (0, 1)]
+    return [(side, g, CHUNK * chunk, CHUNK) for g in (0, 1)]
 
 
 def wide(side, chunk, g):
-    return [(side, g, chunk, 2)]
+    return [(side, g, CHUNK * chunk, BANK)]
 
 
 UNITS = [narrow(X, 0), narrow(X, 1), wide(X, 2, 0), wide(X, 2, 1)] + [narrow(Y, j) for j in range(4)]
 X_UNITS = 4
+ACT_LAST = 96
+SIG_BUFS = {CHUNK: 6, BANK: 2}
 ACT_BANKS = (0, 2)
-SHARED = (1, 2, 3, 7)
+SHARED = (1, 2, 3, 6)
 
 
 def tile_twotimehiddentangentkernel_x2_kernel(
@@ -48,10 +50,10 @@ def tile_twotimehiddentangentkernel_x2_kernel(
         ctx.enter_context(tc.manual_schedule())
 
         def act_bank(name):
-            return psum.tile([P, BANK], F32, name=name, tag="act", bufs=5)
+            return psum.tile([P, BANK], F32, name=name, tag="act", bufs=4)
 
         def dve_bank(name):
-            return psum.tile([P, BANK], F32, name=name, tag="dve", bufs=3)
+            return psum.tile([P, BANK], F32, name=name, tag="dve", bufs=4)
 
         plane_raw = [keep.tile([P, F], U8, name="plane_raw%d" % s, align_bytes=64) for s in (X, Y)]
         nc.vector.memset(plane_raw[X][:].bitcast(I32), 0)
@@ -59,8 +61,10 @@ def tile_twotimehiddentangentkernel_x2_kernel(
         nc.vector.memset(warm[:], 0.0)
         nc.scalar.activation(out=warm[:], in_=warm[:], func=ACT.Sigmoid)
         nc.vector.memset(plane_raw[Y][:].bitcast(I32), 0)
-        vec16 = keep.tile([P, P], BF16, name="vec16", align_bytes=64)
-        nc.vector.memset(vec16[:], 0.0)
+        b16 = keep.tile([P, P], BF16, name="b16", align_bytes=64)
+        v16 = keep.tile([P, P], BF16, name="v16", align_bytes=64)
+        nc.vector.memset(b16[:], 0.0)
+        nc.vector.memset(v16[:], 0.0)
 
         ident = keep.tile([P, P], F32, name="ident", align_bytes=64)
         make_identity(nc, ident[:])
@@ -82,29 +86,34 @@ def tile_twotimehiddentangentkernel_x2_kernel(
         w_perm = [keep.tile([P, 2 * F], U8, name="w_perm%d" % s, align_bytes=64) for s in (X, Y)]
         plane_perm = [keep.tile([P, F], U8, name="plane_perm%d" % s, align_bytes=64) for s in (X, Y)]
 
-        def load_weight(side):
+        def load_scales(side):
             for q in range(4):
                 nc.sync.dma_start(
                     out=plane_raw[side][32 * q : 32 * q + 4, :].bitcast(I32),
                     in_=(wa_scales, wb_scales)[side][0][4 * q : 4 * q + 4, :].bitcast(I32),
                 )
+
+        def load_words(side):
             nc.sync.dma_start(out=w_raw[side][:].bitcast(I32), in_=(wa_words, wb_words)[side][0].bitcast(I32))
 
-        def load_vector(j, v):
+        def load_vector(rows, j, v):
             nc.sync.dma_start(
-                out=vec16[8 * j : 8 * j + 8, :].rearrange("r (q i) -> r q i", i=8),
+                out=rows[8 * j : 8 * j + 8, :].rearrange("r (q i) -> r q i", i=8),
                 in_=v.rearrange("(q r i) -> r q i", r=8, i=8),
             )
 
         load_rows(X, 0)
-        load_weight(X)
+        load_scales(X)
         load_rows(X, 1)
-        for j, v in enumerate((b, va, vb)):
-            load_vector(j, v)
+        load_words(X)
+        load_vector(b16, 0, b)
+        load_vector(v16, X, va)
+        load_vector(v16, Y, vb)
         load_rows(X, 2)
         load_rows(X, 3)
         load_rows(Y, 0)
-        load_weight(Y)
+        load_scales(Y)
+        load_words(Y)
         for chunk in (1, 2, 3):
             load_rows(Y, chunk)
 
@@ -143,98 +152,96 @@ def tile_twotimehiddentangentkernel_x2_kernel(
                 out=codes[side][:, cols].bitcast(FP8X4), scales=planes[side][:, cols], in_=grouped[side, chunk][:]
             )
 
-        vcol = keep.tile([P, 40], F32, name="vcol")
+        bias2 = keep.tile([P, 8], F32, name="bias2")
+        minus4v = keep.tile([P, 16], F32, name="minus4v")
+        plus4v = keep.tile([P, 16], F32, name="plus4v")
 
-        def turn_vectors():
-            bank = psum.tile([P, 2 * BANK], BF16, name="vbank", tag="dve", bufs=3)
-            nc.tensor.transpose(bank[:, 0:P], vec16[:], ident16[:])
+        def turn_vector(rows):
+            bank = psum.tile([P, 2 * BANK], BF16, name="vbank", tag="dve", bufs=4)
+            nc.tensor.transpose(bank[:, 0:P], rows[:], ident16[:])
             return bank
 
-        def vectors_out(bank):
-            for dst, src, factor in ((0, 0, 2.0), (8, 8, -4.0), (24, 8, 4.0)):
-                width = 8 if src == 0 else 16
-                nc.vector.tensor_scalar(
-                    out=vcol[:, dst : dst + width], in0=bank[:, src : src + width],
-                    scalar1=factor, scalar2=None, op0=ALU.mult,
-                )
+        def vector_out(bank, dst, times):
+            nc.vector.tensor_scalar(
+                out=dst[:], in0=bank[:, 0 : dst.shape[1]], scalar1=times, scalar2=None, op0=ALU.mult
+            )
 
         z_banks, sig, fac, d16, d_codes, d_planes, d_at = {}, {}, {}, {}, {}, {}, {}
 
-        def segments(u):
-            col = 0
-            found = []
-            for side, g, chunk, chunks in UNITS[u]:
-                found.append((side, g, CHUNK * chunk, slice(col, col + CHUNK * chunks)))
-                col = col + CHUNK * chunks
-            return found
-
         def pieces(u, k):
-            parts = [(seg, t) for seg in segments(u) for t in range(4)]
-            each = len(parts) // 4
+            parts = [(part, t) for part in range(len(UNITS[u])) for t in range(4)]
+            each = len(UNITS[u])
             width = BANK // each
-            return [(parts[each * k + i], slice(width * i, width * (i + 1))) for i in range(each)]
+            return [parts[each * k + i] + (slice(width * i, width * (i + 1)),) for i in range(each)]
 
         def z_mm(u, k):
             z = act_bank("z")
             z_banks[u, k] = z
-            for ((side, g, tok, cols), t), at in pieces(u, k):
+            for part, t, at in pieces(u, k):
+                side, g, tok, width = UNITS[u][part]
                 r = 4 * g + t
-                toks = slice(tok, tok + cols.stop - cols.start)
                 nc.tensor.matmul_mx(
                     out=z[:, at],
                     lhsT=w_perm[side][:, 2 * P * r : 2 * P * (r + 1)].bitcast(FP4X4),
                     lhsT_scale=plane_perm[side][:, P * r : P * (r + 1)],
-                    rhs=codes[side][:, toks].bitcast(FP8X4),
-                    rhs_scale=planes[side][:, toks],
+                    rhs=codes[side][:, tok : tok + width].bitcast(FP8X4),
+                    rhs_scale=planes[side][:, tok : tok + width],
                     start=True,
                     stop=True,
                 )
 
         def sigmoid(u, k):
-            if k == 0:
-                sig[u] = work.tile([P, 4, BANK], F32, name="sig", tag="sig", bufs=3, align_bytes=64)
-                fac[u] = work.tile([P, 4, BANK], F32, name="fac", tag="fac", bufs=3, align_bytes=64)
-            for ((side, g, tok, cols), t), at in pieces(u, k):
+            for part, t, at in pieces(u, k):
+                side, g, tok, width = UNITS[u][part]
+                if t == 0:
+                    tag, bufs = "%d" % width, SIG_BUFS[width]
+                    sig[u, part] = work.tile([P, 4, width], F32, name="sig", tag="sig" + tag, bufs=bufs, align_bytes=64)
+                    fac[u, part] = work.tile([P, 4, width], F32, name="fac", tag="fac" + tag, bufs=bufs, align_bytes=64)
                 r = 4 * g + t
                 nc.scalar.activation(
-                    out=sig[u][:, t, cols], in_=z_banks[u, k][:, at], func=ACT.Sigmoid,
-                    bias=vcol[:, r : r + 1], scale=2.0,
+                    out=sig[u, part][:, t, :], in_=z_banks[u, k][:, at], func=ACT.Sigmoid,
+                    bias=bias2[:, r : r + 1], scale=2.0,
                 )
 
         def factor(u, k, on_act):
-            for ((side, g, tok, cols), t), at in pieces(u, k):
-                c = 8 + 8 * side + 4 * g + t
+            for part, t, at in pieces(u, k):
+                side, g, tok, width = UNITS[u][part]
+                c = 8 * side + 4 * g + t
                 if on_act:
                     nc.scalar.activation(
-                        out=fac[u][:, t, cols], in_=sig[u][:, t, cols], func=ACT.Identity,
-                        bias=vcol[:, c + 16 : c + 17], scale=vcol[:, c : c + 1],
+                        out=fac[u, part][:, t, :], in_=sig[u, part][:, t, :], func=ACT.Identity,
+                        bias=plus4v[:, c : c + 1], scale=minus4v[:, c : c + 1],
                     )
                 else:
                     nc.vector.tensor_scalar(
-                        out=fac[u][:, t, cols], in0=sig[u][:, t, cols],
-                        scalar1=1.0, scalar2=vcol[:, c : c + 1], op0=ALU.subtract, op1=ALU.mult,
+                        out=fac[u, part][:, t, :], in0=sig[u, part][:, t, :],
+                        scalar1=1.0, scalar2=minus4v[:, c : c + 1], op0=ALU.subtract, op1=ALU.mult,
                     )
 
-        def by_runs(tile4, cols):
-            return tile4[:, :, cols].rearrange("p t (c i) -> p c t i", i=RUN)
+        def by_runs(planes4):
+            return planes4.rearrange("p t (c i) -> p c t i", i=RUN)
 
         def into_words(tile16, cols):
             return tile16[:, cols, :].rearrange("p (c i) t -> p c t i", i=RUN)
 
-        def product(u, cols):
-            if cols.start == 0:
+        def product(u, part):
+            width = UNITS[u][part][3]
+            if part == 0:
                 d16[u] = work.tile([P, BANK, 4], BF16, name="d16", tag="d16", bufs=2, align_bytes=64)
             nc.vector.tensor_tensor(
-                out=into_words(d16[u], cols), in0=by_runs(sig[u], cols), in1=by_runs(fac[u], cols), op=ALU.mult
+                out=into_words(d16[u], slice(width * part, width * (part + 1))),
+                in0=by_runs(sig[u, part][:]),
+                in1=by_runs(fac[u, part][:]),
+                op=ALU.mult,
             )
 
         def quant_d(u, cols):
             if cols.start == 0:
                 d_codes[u] = keep.tile([P, BANK], U32, name="d_codes%d" % u, align_bytes=64)
                 d_planes[u] = keep.tile([P, BANK], U8, name="d_planes%d" % u, align_bytes=64)
-                for side, g, tok, seg in segments(u):
-                    for k in range(0, seg.stop - seg.start, P):
-                        d_at[side, g, tok + k] = (u, seg.start + k)
+                for part, (side, g, tok, width) in enumerate(UNITS[u]):
+                    for k in range(0, width, P):
+                        d_at[side, g, tok + k] = (u, width * part + k)
             nc.vector.quantize_mx(
                 out=d_codes[u][:, cols].bitcast(FP8X4),
                 scales=d_planes[u][:, cols],
@@ -290,24 +297,24 @@ def tile_twotimehiddentangentkernel_x2_kernel(
             return slice(CHUNK * h, CHUNK * (h + 1))
 
         def hadamard(j, k):
-            if k == 0:
-                o32[j] = work.tile([P, 4, BANK], F32, name="o32", tag="o32", bufs=3, align_bytes=64)
-                o16[j] = work.tile([P, BANK, 4], BF16, name="o16", tag="o16", bufs=2, align_bytes=64)
             h, t0 = k // 2, 2 * (k % 2)
+            if t0 == 0:
+                o32[j, h] = work.tile([P, 4, CHUNK], F32, name="o32", tag="o32", bufs=6, align_bytes=64)
+            pair = o32[j, h][:, t0 : t0 + 2, :]
             nc.vector.tensor_tensor(
-                out=o32[j][:, t0 : t0 + 2, half(h)],
-                in0=gram_banks[j, k][:].rearrange("p (t c) -> p t c", t=2),
-                in1=base_sb[j, k][:].rearrange("p (t c) -> p t c", t=2),
-                op=ALU.mult,
+                out=pair.rearrange("p t c -> p (t c)"), in0=gram_banks[j, k][:], in1=base_sb[j, k][:], op=ALU.mult
             )
             rows = out_0[BANK * h : BANK * (h + 1), CHUNK * j : CHUNK * (j + 1)].rearrange("(p t) m -> p t m", t=4)
-            nc.sync.dma_start(out=rows[:, t0 : t0 + 2, :], in_=o32[j][:, t0 : t0 + 2, half(h)])
+            nc.sync.dma_start(out=rows[:, t0 : t0 + 2, :], in_=pair)
 
-        def cast(j, cols, on_act):
+        def cast(j, h, on_act, cols=slice(0, CHUNK)):
+            if (j, h) not in o16:
+                o16[j, h] = work.tile([P, CHUNK, 4], BF16, name="o16", tag="o16", bufs=4, align_bytes=64)
+            dst, src = into_words(o16[j, h], cols), by_runs(o32[j, h][:, :, cols])
             if on_act:
-                nc.scalar.copy(out=into_words(o16[j], cols), in_=by_runs(o32[j], cols))
+                nc.scalar.copy(out=dst, in_=src)
             else:
-                nc.vector.tensor_copy(out=into_words(o16[j], cols), in_=by_runs(o32[j], cols))
+                nc.vector.tensor_copy(out=dst, in_=src)
 
         o_codes = keep.tile([P, 2, M], U32, name="o_codes", align_bytes=64)
         o_planes = keep.tile([P, 2, M], U8, name="o_planes", align_bytes=64)
@@ -317,7 +324,7 @@ def tile_twotimehiddentangentkernel_x2_kernel(
             nc.vector.quantize_mx(
                 out=o_codes[:, h, toks].bitcast(FP8X4),
                 scales=o_planes[:, h, toks],
-                in_=o16[j][:, half(h), :].rearrange("p n t -> p (n t)"),
+                in_=o16[j, h][:].rearrange("p n t -> p (n t)"),
             )
 
         def store_words(j, h0, h1, queue):
@@ -355,29 +362,32 @@ def tile_twotimehiddentangentkernel_x2_kernel(
 
         transposes(X, 0, act_bank("turn"))
         transposes(X, 1, act_bank("turn"))
-        vbank = turn_vectors()
+        b_bank = turn_vector(b16)
         turn_out(X, 0, True)
         permute(X)
         quant_in(X, 0)
         turn_out(X, 1, True)
-        vectors_out(vbank)
+        vector_out(b_bank, bias2, 2.0)
         quant_in(X, 1)
-        for k in range(2):
-            z_mm(0, k)
+        z_mm(0, 0)
+        v_bank = turn_vector(v16)
+        vector_out(v_bank, minus4v, -4.0)
+        vector_out(v_bank, plus4v, 4.0)
+        z_mm(0, 1)
         transposes(X, 2, dve_bank("turn"))
         act_unit(0, 2)
         dve_factors(0, (0,))
         turn_out(X, 2, False)
         dve_factors(0, (1,))
         quant_in(X, 2)
-        product(0, half(0))
+        product(0, 0)
         z_mm(1, 0)
         transposes(X, 3, dve_bank("turn"))
-        dve_factors(0, (2, 3))
         turn_out(X, 3, False)
-        act_unit(1, 1)
-        product(0, half(1))
+        dve_factors(0, (2, 3))
         quant_in(X, 3)
+        act_unit(1, 1)
+        product(0, 1)
         permute(Y)
 
         for u in range(1, X_UNITS):
@@ -387,66 +397,84 @@ def tile_twotimehiddentangentkernel_x2_kernel(
             turn_out(Y, u - 1, True)
             dve_factors(u, range(4))
             quant_d(u - 1, whole)
-            product(u, whole)
+            for part in range(len(UNITS[u])):
+                product(u, part)
             quant_in(Y, u - 1)
             act_unit(u + 1, 1 if u + 1 < X_UNITS else 0)
+
+        def finish(j):
+            for h in (0, 1):
+                quant_o(j, h)
+            store_words(j, 0, 2, nc.sync)
 
         last = len(UNITS) - 1
         for u in range(X_UNITS, last + 1):
             j = u - X_UNITS - 1
+
+            def stage(k):
+                if u < last:
+                    z_mm(u + 1, k)
+                else:
+                    base_mm(j + 1, k)
+
             if u == X_UNITS:
                 transposes(Y, 3, act_bank("turn"))
                 turn_out(Y, 3, True)
-            if j > 0:
-                cast(j - 1, whole, True)
-            dve_factors(u, range(4))
-            quant_d(u - 1, whole)
-            if u == X_UNITS + 1:
-                quant_in(Y, 3)
-            if u < last:
-                for k in range(4):
-                    z_mm(u + 1, k)
-            if j >= 0:
-                for k in range(3):
-                    gram(j, k)
-            if u < last:
-                act_unit(u + 1, 4)
-            product(u, half(0))
-            base_mm(j + 1, 0)
-            if j >= 0:
-                hadamard(j, 0)
-                gram(j, 3)
             for k in range(4):
-                if k < 3:
-                    base_mm(j + 1, k + 1)
-                base_out(j + 1, k)
-            if u == last:
-                quant_d(u, half(0))
-                for k in range(4):
-                    gram_mm(j + 1, k, 0, act_bank("gram"))
-            if j >= 0:
-                hadamard(j, 1)
-            product(u, half(1))
-            if j >= 0:
-                hadamard(j, 2)
-                hadamard(j, 3)
-            if u == last:
-                quant_d(u, half(1))
+                if j >= 0:
+                    base_out(j, k)
             if j > 0:
                 for h in (0, 1):
-                    quant_o(j - 1, h)
-                store_words(j - 1, 0, 2, nc.sync)
+                    cast(j - 1, h, True)
+            dve_factors(u, range(4))
+            quant_d(u - 1, whole)
+            before = 2 if j > 0 else 4
+            for k in range(before):
+                stage(k)
+            if j >= 0:
+                for k in range(4):
+                    gram(j, k)
+            for k in range(before, 4):
+                stage(k)
+            if u == last:
+                break
+            act_unit(u + 1, 4)
+            for k in range(4):
+                base_mm(j + 1, k)
+            for part in (0, 1):
+                product(u, part)
+            if u == X_UNITS:
+                quant_in(Y, 3)
+            if j >= 0:
+                for k in range(4):
+                    hadamard(j, k)
+            if j > 0:
+                finish(j - 1)
+
         j = last - X_UNITS
+        for k in range(4):
+            base_out(j, k)
+        product(last, 0)
+        hadamard(j - 1, 0)
+        quant_d(last, half(0))
+        for k in range(4):
+            gram_mm(j, k, 0, act_bank("gram"))
+        hadamard(j - 1, 1)
+        product(last, 1)
+        hadamard(j - 1, 2)
+        hadamard(j - 1, 3)
+        quant_d(last, half(1))
+        finish(j - 2)
         store_scales(0, j - 1, [nc.sync])
-        cast(j - 1, whole, True)
+        for h in (0, 1):
+            cast(j - 1, h, True)
         for k in range(4):
             gram_mm(j, k, 1)
             hadamard(j, k)
-        cast(j, half(0), True)
-        for h in (0, 1):
-            quant_o(j - 1, h)
-        store_words(j - 1, 0, 2, nc.sync)
-        cast(j, half(1), False)
+        cast(j, 0, True)
+        cast(j, 1, True, slice(0, ACT_LAST))
+        finish(j - 1)
+        cast(j, 1, False, slice(ACT_LAST, CHUNK))
         quant_o(j, 0)
         store_words(j, 0, 1, nc.sync)
         quant_o(j, 1)

@@ -36,7 +36,9 @@ X_UNITS = 4
 ACT_LAST = 96
 SIG_BUFS = {CHUNK: 6, BANK: 2}
 ACT_BANKS = (0, 2)
-SHARED = (1, 2, 3, 6)
+SHARED = (1, 2, 3)
+ACT_ALL = (5, 6, 7)
+ACT_TURNS = (0, 1)
 
 
 def tile_twotimehiddentangentkernel_x2_kernel(
@@ -345,15 +347,19 @@ def tile_twotimehiddentangentkernel_x2_kernel(
         whole = slice(0, BANK)
 
         def shared(u):
+            if u in ACT_ALL:
+                return (0, 1, 2, 3)
             return ACT_BANKS if u in SHARED else ()
 
         def act_unit(u, staged):
-            for k in range(4):
-                if k + staged < 4:
-                    z_mm(u, k + staged)
-                sigmoid(u, k)
-                if k - 1 in shared(u):
-                    factor(u, k - 1, True)
+            for pair in (0, 2):
+                for k in (pair, pair + 1):
+                    if k + staged < 4:
+                        z_mm(u, k + staged)
+                    sigmoid(u, k)
+                for k in (pair, pair + 1):
+                    if k in shared(u):
+                        factor(u, k, True)
 
         def dve_factors(u, banks):
             for k in banks:
@@ -391,10 +397,11 @@ def tile_twotimehiddentangentkernel_x2_kernel(
         permute(Y)
 
         for u in range(1, X_UNITS):
-            transposes(Y, u - 1, act_bank("turn"))
+            on_act = u - 1 in ACT_TURNS
+            transposes(Y, u - 1, (act_bank if on_act else dve_bank)("turn"))
             if u + 1 < X_UNITS:
                 z_mm(u + 1, 0)
-            turn_out(Y, u - 1, True)
+            turn_out(Y, u - 1, on_act)
             dve_factors(u, range(4))
             quant_d(u - 1, whole)
             for part in range(len(UNITS[u])):
@@ -418,24 +425,24 @@ def tile_twotimehiddentangentkernel_x2_kernel(
                     base_mm(j + 1, k)
 
             if u == X_UNITS:
-                transposes(Y, 3, act_bank("turn"))
-                turn_out(Y, 3, True)
+                on_act = 3 in ACT_TURNS
+                transposes(Y, 3, (act_bank if on_act else dve_bank)("turn"))
+                turn_out(Y, 3, on_act)
             for k in range(4):
                 if j >= 0:
                     base_out(j, k)
-            if j > 0:
-                for h in (0, 1):
-                    cast(j - 1, h, True)
             dve_factors(u, range(4))
             quant_d(u - 1, whole)
-            before = 2 if j > 0 else 4
-            for k in range(before):
-                stage(k)
-            if j >= 0:
-                for k in range(4):
+            for k in range(4):
+                if j <= 0:
+                    stage(k)
+            for k in range(4):
+                if j >= 0:
                     gram(j, k)
-            for k in range(before, 4):
-                stage(k)
+                if j > 0 and k > 0:
+                    stage(k - 1)
+            if j > 0:
+                stage(3)
             if u == last:
                 break
             act_unit(u + 1, 4)
@@ -445,6 +452,9 @@ def tile_twotimehiddentangentkernel_x2_kernel(
                 product(u, part)
             if u == X_UNITS:
                 quant_in(Y, 3)
+            if j > 0:
+                for h in (0, 1):
+                    cast(j - 1, h, False)
             if j >= 0:
                 for k in range(4):
                     hadamard(j, k)
@@ -455,6 +465,8 @@ def tile_twotimehiddentangentkernel_x2_kernel(
         for k in range(4):
             base_out(j, k)
         product(last, 0)
+        for h in (0, 1):
+            cast(j - 2, h, False)
         hadamard(j - 1, 0)
         quant_d(last, half(0))
         for k in range(4):

@@ -33,10 +33,11 @@ def wide(side, chunk, g):
 
 UNITS = [narrow(X, 0), narrow(X, 1), wide(X, 2, 0), wide(X, 2, 1)] + [narrow(Y, j) for j in range(4)]
 X_UNITS = 4
-ACT_LAST = 96
-SIG_BUFS = {CHUNK: 6, BANK: 2}
+ACT_LAST = 64
+RELAY = (6, 7)
+SIG_BUFS = {CHUNK: 5, BANK: 2}
 ACT_BANKS = (0, 2)
-SHARED = (1, 2, 3)
+SHARED = (2, 3)
 ACT_ALL = (5, 6, 7)
 ACT_TURNS = (0, 1)
 
@@ -59,9 +60,6 @@ def tile_twotimehiddentangentkernel_x2_kernel(
 
         plane_raw = [keep.tile([P, F], U8, name="plane_raw%d" % s, align_bytes=64) for s in (X, Y)]
         nc.vector.memset(plane_raw[X][:].bitcast(I32), 0)
-        warm = keep.tile([P, 1], F32, name="warm")
-        nc.vector.memset(warm[:], 0.0)
-        nc.scalar.activation(out=warm[:], in_=warm[:], func=ACT.Sigmoid)
         nc.vector.memset(plane_raw[Y][:].bitcast(I32), 0)
         b16 = keep.tile([P, P], BF16, name="b16", align_bytes=64)
         v16 = keep.tile([P, P], BF16, name="v16", align_bytes=64)
@@ -112,11 +110,10 @@ def tile_twotimehiddentangentkernel_x2_kernel(
         load_vector(v16, X, va)
         load_vector(v16, Y, vb)
         load_rows(X, 2)
-        load_rows(X, 3)
-        load_rows(Y, 0)
-        load_scales(Y)
         load_words(Y)
-        for chunk in (1, 2, 3):
+        load_scales(Y)
+        load_rows(X, 3)
+        for chunk in range(4):
             load_rows(Y, chunk)
 
         def permute(side):
@@ -198,7 +195,8 @@ def tile_twotimehiddentangentkernel_x2_kernel(
                 if t == 0:
                     tag, bufs = "%d" % width, SIG_BUFS[width]
                     sig[u, part] = work.tile([P, 4, width], F32, name="sig", tag="sig" + tag, bufs=bufs, align_bytes=64)
-                    fac[u, part] = work.tile([P, 4, width], F32, name="fac", tag="fac" + tag, bufs=bufs, align_bytes=64)
+                    fac_tag, fac_bufs = ("relay%d" % u, 1) if u in RELAY and part == 1 else ("fac" + tag, bufs)
+                    fac[u, part] = work.tile([P, 4, width], F32, name="fac", tag=fac_tag, bufs=fac_bufs, align_bytes=64)
                 r = 4 * g + t
                 nc.scalar.activation(
                     out=sig[u, part][:, t, :], in_=z_banks[u, k][:, at], func=ACT.Sigmoid,
@@ -318,6 +316,13 @@ def tile_twotimehiddentangentkernel_x2_kernel(
             else:
                 nc.vector.tensor_copy(out=dst, in_=src)
 
+        def cast_on_pool(j, relay):
+            o16[j, 0] = work.tile([P, CHUNK, 4], BF16, name="o16", tag="relay%d" % relay, bufs=1, align_bytes=64)
+            nc.gpsimd.tensor_scalar(
+                out=o16[j, 0][:], in0=o32[j, 0][:].rearrange("p t c -> p c t"),
+                scalar1=1.0, scalar2=0.0, op0=ALU.mult, op1=ALU.add,
+            )
+
         o_codes = keep.tile([P, 2, M], U32, name="o_codes", align_bytes=64)
         o_planes = keep.tile([P, 2, M], U8, name="o_planes", align_bytes=64)
 
@@ -329,8 +334,8 @@ def tile_twotimehiddentangentkernel_x2_kernel(
                 in_=o16[j, h][:].rearrange("p n t -> p (n t)"),
             )
 
-        def store_words(j, h0, h1, queue):
-            toks = slice(CHUNK * j, CHUNK * (j + 1))
+        def store_words(j0, j1, h0, h1, queue):
+            toks = slice(CHUNK * j0, CHUNK * j1)
             queue.dma_start(
                 out=out_1[h0:h1, :, toks, :].rearrange("h p m t -> p h (m t)").bitcast(I32),
                 in_=o_codes[:, h0:h1, toks].bitcast(I32),
@@ -351,68 +356,79 @@ def tile_twotimehiddentangentkernel_x2_kernel(
                 return (0, 1, 2, 3)
             return ACT_BANKS if u in SHARED else ()
 
+        def act_pair(u, pair):
+            for k in (pair, pair + 1):
+                sigmoid(u, k)
+            for k in (pair, pair + 1):
+                if k in shared(u):
+                    factor(u, k, True)
+
         def act_unit(u, staged):
             for pair in (0, 2):
                 for k in (pair, pair + 1):
-                    if k + staged < 4:
-                        z_mm(u, k + staged)
-                    sigmoid(u, k)
-                for k in (pair, pair + 1):
-                    if k in shared(u):
-                        factor(u, k, True)
+                    if k >= staged:
+                        z_mm(u, k)
+                act_pair(u, pair)
 
         def dve_factors(u, banks):
             for k in banks:
                 if k not in shared(u):
                     factor(u, k, False)
 
-        transposes(X, 0, act_bank("turn"))
-        transposes(X, 1, act_bank("turn"))
+        transposes(X, 0, dve_bank("turn"))
+        transposes(X, 1, dve_bank("turn"))
         b_bank = turn_vector(b16)
-        turn_out(X, 0, True)
+        turn_out(X, 0, False)
         permute(X)
         quant_in(X, 0)
-        turn_out(X, 1, True)
         vector_out(b_bank, bias2, 2.0)
-        quant_in(X, 1)
+        turn_out(X, 1, False)
         z_mm(0, 0)
         v_bank = turn_vector(v16)
+        quant_in(X, 1)
         vector_out(v_bank, minus4v, -4.0)
         vector_out(v_bank, plus4v, 4.0)
-        z_mm(0, 1)
-        transposes(X, 2, dve_bank("turn"))
-        act_unit(0, 2)
+        for k in (1, 2, 3):
+            z_mm(0, k)
+        act_unit(0, 4)
+        transposes(X, 2, act_bank("turn"))
+        turn_out(X, 2, True)
         dve_factors(0, (0,))
-        turn_out(X, 2, False)
-        dve_factors(0, (1,))
-        quant_in(X, 2)
-        product(0, 0)
-        z_mm(1, 0)
-        transposes(X, 3, dve_bank("turn"))
-        turn_out(X, 3, False)
-        dve_factors(0, (2, 3))
-        quant_in(X, 3)
-        act_unit(1, 1)
-        product(0, 1)
         permute(Y)
+        dve_factors(0, (1,))
+        product(0, 0)
+        dve_factors(0, (2, 3))
+        quant_in(X, 2)
+        product(0, 1)
+        z_mm(1, 0)
+        z_mm(1, 1)
+        transposes(X, 3, act_bank("turn"))
+        act_pair(1, 0)
+        turn_out(X, 3, True)
+        z_mm(1, 2)
+        z_mm(1, 3)
+        act_pair(1, 2)
 
         for u in range(1, X_UNITS):
             on_act = u - 1 in ACT_TURNS
             transposes(Y, u - 1, (act_bank if on_act else dve_bank)("turn"))
+            dve_factors(u, (0, 1))
+            if u == 1:
+                quant_in(X, 3)
+            dve_factors(u, (2, 3))
+            quant_d(u - 1, whole)
             if u + 1 < X_UNITS:
                 z_mm(u + 1, 0)
             turn_out(Y, u - 1, on_act)
-            dve_factors(u, range(4))
-            quant_d(u - 1, whole)
             for part in range(len(UNITS[u])):
                 product(u, part)
             quant_in(Y, u - 1)
             act_unit(u + 1, 1 if u + 1 < X_UNITS else 0)
 
         def finish(j):
-            for h in (0, 1):
+            for h in (1, 0):
                 quant_o(j, h)
-            store_words(j, 0, 2, nc.sync)
+            store_words(j, j + 1, 0, 2, nc.sync)
 
         last = len(UNITS) - 1
         for u in range(X_UNITS, last + 1):
@@ -448,47 +464,51 @@ def tile_twotimehiddentangentkernel_x2_kernel(
             act_unit(u + 1, 4)
             for k in range(4):
                 base_mm(j + 1, k)
-            for part in (0, 1):
-                product(u, part)
+            product(u, 0)
+            if j > 0:
+                cast(j - 1, 1, False)
+            product(u, 1)
             if u == X_UNITS:
                 quant_in(Y, 3)
             if j > 0:
-                for h in (0, 1):
-                    cast(j - 1, h, False)
+                cast_on_pool(j - 1, u)
             if j >= 0:
                 for k in range(4):
                     hadamard(j, k)
-            if j > 0:
-                finish(j - 1)
 
         j = last - X_UNITS
         for k in range(4):
             base_out(j, k)
+        cast(j - 2, 1, True)
         product(last, 0)
-        for h in (0, 1):
-            cast(j - 2, h, False)
-        hadamard(j - 1, 0)
+        finish(j - 3)
+        store_scales(0, j - 2, [nc.sync])
         quant_d(last, half(0))
-        for k in range(4):
-            gram_mm(j, k, 0, act_bank("gram"))
-        hadamard(j - 1, 1)
         product(last, 1)
-        hadamard(j - 1, 2)
-        hadamard(j - 1, 3)
+        for k in (0, 1):
+            gram_mm(j, k, 0, act_bank("gram"))
+        cast_on_pool(j - 2, last)
+        for k in range(4):
+            hadamard(j - 1, k)
         quant_d(last, half(1))
-        finish(j - 2)
-        store_scales(0, j - 1, [nc.sync])
-        for h in (0, 1):
-            cast(j - 1, h, True)
+        quant_o(j - 2, 0)
+        store_words(j - 2, j - 1, 0, 1, nc.sync)
+        cast_on_pool(j - 1, last)
+        cast(j - 1, 1, True)
         for k in range(4):
             gram_mm(j, k, 1)
+            if k < 2:
+                gram_mm(j, k + 2, 0, act_bank("gram"))
             hadamard(j, k)
         cast(j, 0, True)
         cast(j, 1, True, slice(0, ACT_LAST))
-        finish(j - 1)
+        quant_o(j - 2, 1)
+        quant_o(j - 1, 1)
+        store_words(j - 2, j, 1, 2, nc.sync)
+        quant_o(j - 1, 0)
         cast(j, 1, False, slice(ACT_LAST, CHUNK))
         quant_o(j, 0)
-        store_words(j, 0, 1, nc.sync)
+        store_words(j - 1, j + 1, 0, 1, nc.sync)
         quant_o(j, 1)
-        store_scales(j - 1, j + 1, [nc.scalar, nc.sync])
-        store_words(j, 1, 2, nc.scalar)
+        store_words(j, j + 1, 1, 2, nc.sync)
+        store_scales(j - 2, j + 1, [nc.scalar, nc.sync])

@@ -31,15 +31,15 @@ def wide(side, chunk, g):
     return [(side, g, CHUNK * chunk, BANK)]
 
 
-UNITS = [narrow(X, 0), narrow(X, 1), wide(X, 2, 0), wide(X, 2, 1)] + [narrow(Y, j) for j in range(4)]
+UNITS = [narrow(X, 0), narrow(X, 1), wide(X, 2, 0), wide(X, 2, 1), wide(Y, 0, 0), wide(Y, 0, 1), narrow(Y, 2), narrow(Y, 3)]
 X_UNITS = 4
-ACT_LAST = 64
-RELAY = (6, 7)
-SIG_BUFS = {CHUNK: 5, BANK: 2}
+ACT_LAST = 96
+RELAY = (7,)
+SIG_BUFS = {CHUNK: 4, BANK: 3}
 ACT_BANKS = (0, 2)
 SHARED = (2, 3)
 ACT_ALL = (5, 6, 7)
-ACT_TURNS = (0, 1)
+ACT_TURNS = (0, 1, 2)
 
 
 def tile_twotimehiddentangentkernel_x2_kernel(
@@ -103,9 +103,9 @@ def tile_twotimehiddentangentkernel_x2_kernel(
             )
 
         load_rows(X, 0)
+        load_words(X)
         load_scales(X)
         load_rows(X, 1)
-        load_words(X)
         load_vector(b16, 0, b)
         load_vector(v16, X, va)
         load_vector(v16, Y, vb)
@@ -116,12 +116,11 @@ def tile_twotimehiddentangentkernel_x2_kernel(
         for chunk in range(4):
             load_rows(Y, chunk)
 
-        def permute(side):
-            for dst, src in ((w_perm, w_raw), (plane_perm, plane_raw)):
-                nc.vector.tensor_copy(
-                    out=dst[side][:].bitcast(I32).rearrange("p (r q i) -> p r q i", r=8, q=16),
-                    in_=src[side][:].bitcast(I32).rearrange("p (q r i) -> p r q i", r=8, q=16),
-                )
+        def permute(dst, src):
+            nc.vector.tensor_copy(
+                out=dst[:].bitcast(I32).rearrange("p (r q i) -> p r q i", r=8, q=16),
+                in_=src[:].bitcast(I32).rearrange("p (q r i) -> p r q i", r=8, q=16),
+            )
 
         grouped, turned = {}, {}
         codes = [keep.tile([P, N], U32, name="codes%d" % s, align_bytes=64) for s in (X, Y)]
@@ -316,10 +315,10 @@ def tile_twotimehiddentangentkernel_x2_kernel(
             else:
                 nc.vector.tensor_copy(out=dst, in_=src)
 
-        def cast_on_pool(j, relay):
-            o16[j, 0] = work.tile([P, CHUNK, 4], BF16, name="o16", tag="relay%d" % relay, bufs=1, align_bytes=64)
+        def cast_on_pool(j, h, tag, bufs):
+            o16[j, h] = work.tile([P, CHUNK, 4], BF16, name="o16", tag=tag, bufs=bufs, align_bytes=64)
             nc.gpsimd.tensor_scalar(
-                out=o16[j, 0][:], in0=o32[j, 0][:].rearrange("p t c -> p c t"),
+                out=o16[j, h][:], in0=o32[j, h][:].rearrange("p t c -> p c t"),
                 scalar1=1.0, scalar2=0.0, op0=ALU.mult, op1=ALU.add,
             )
 
@@ -378,8 +377,9 @@ def tile_twotimehiddentangentkernel_x2_kernel(
         transposes(X, 0, dve_bank("turn"))
         transposes(X, 1, dve_bank("turn"))
         b_bank = turn_vector(b16)
+        permute(w_perm[X], w_raw[X])
         turn_out(X, 0, False)
-        permute(X)
+        permute(plane_perm[X], plane_raw[X])
         quant_in(X, 0)
         vector_out(b_bank, bias2, 2.0)
         turn_out(X, 1, False)
@@ -394,7 +394,8 @@ def tile_twotimehiddentangentkernel_x2_kernel(
         transposes(X, 2, act_bank("turn"))
         turn_out(X, 2, True)
         dve_factors(0, (0,))
-        permute(Y)
+        permute(w_perm[Y], w_raw[Y])
+        permute(plane_perm[Y], plane_raw[Y])
         dve_factors(0, (1,))
         product(0, 0)
         dve_factors(0, (2, 3))
@@ -409,96 +410,93 @@ def tile_twotimehiddentangentkernel_x2_kernel(
         z_mm(1, 3)
         act_pair(1, 2)
 
-        for u in range(1, X_UNITS):
-            on_act = u - 1 in ACT_TURNS
-            transposes(Y, u - 1, (act_bank if on_act else dve_bank)("turn"))
-            dve_factors(u, (0, 1))
-            if u == 1:
-                quant_in(X, 3)
-            dve_factors(u, (2, 3))
+        def turn_y(chunk):
+            on_act = chunk in ACT_TURNS
+            transposes(Y, chunk, (act_bank if on_act else dve_bank)("turn"))
+            turn_out(Y, chunk, on_act)
+
+        quant_in(X, 3)
+        for u in range(1, X_UNITS + 1):
+            if u < X_UNITS:
+                turn_y(u - 1)
+            dve_factors(u, range(4))
             quant_d(u - 1, whole)
-            if u + 1 < X_UNITS:
-                z_mm(u + 1, 0)
-            turn_out(Y, u - 1, on_act)
+            if u < X_UNITS:
+                quant_in(Y, u - 1)
+            act_unit(u + 1, 0)
             for part in range(len(UNITS[u])):
                 product(u, part)
-            quant_in(Y, u - 1)
-            act_unit(u + 1, 1 if u + 1 < X_UNITS else 0)
 
         def finish(j):
             for h in (1, 0):
                 quant_o(j, h)
             store_words(j, j + 1, 0, 2, nc.sync)
 
+        def base_block(j):
+            for k in range(4):
+                base_out(j, k)
+
         last = len(UNITS) - 1
-        for u in range(X_UNITS, last + 1):
-            j = u - X_UNITS - 1
+        j = 3
 
-            def stage(k):
-                if u < last:
-                    z_mm(u + 1, k)
-                else:
-                    base_mm(j + 1, k)
+        turn_y(3)
+        dve_factors(5, range(4))
+        quant_d(4, whole)
+        act_unit(6, 0)
+        product(5, 0)
 
-            if u == X_UNITS:
-                on_act = 3 in ACT_TURNS
-                transposes(Y, 3, (act_bank if on_act else dve_bank)("turn"))
-                turn_out(Y, 3, on_act)
-            for k in range(4):
-                if j >= 0:
-                    base_out(j, k)
-            dve_factors(u, range(4))
-            quant_d(u - 1, whole)
-            for k in range(4):
-                if j <= 0:
-                    stage(k)
-            for k in range(4):
-                if j >= 0:
-                    gram(j, k)
-                if j > 0 and k > 0:
-                    stage(k - 1)
-            if j > 0:
-                stage(3)
-            if u == last:
-                break
-            act_unit(u + 1, 4)
-            for k in range(4):
-                base_mm(j + 1, k)
-            product(u, 0)
-            if j > 0:
-                cast(j - 1, 1, False)
-            product(u, 1)
-            if u == X_UNITS:
-                quant_in(Y, 3)
-            if j > 0:
-                cast_on_pool(j - 1, u)
-            if j >= 0:
-                for k in range(4):
-                    hadamard(j, k)
-
-        j = last - X_UNITS
         for k in range(4):
-            base_out(j, k)
+            base_mm(0, k)
+        base_block(0)
+        quant_in(Y, 3)
+        dve_factors(6, range(4))
+        quant_d(5, whole)
+        for k in range(4):
+            gram(0, k)
+            base_mm(1, k)
+        base_block(1)
+        for part in (0, 1):
+            product(6, part)
+        for k in (0, 1):
+            z_mm(last, k)
+        for k in range(4):
+            hadamard(0, k)
+            gram(1, k)
+            if k >= 2:
+                z_mm(last, k)
+            if k % 2 == 1:
+                cast_on_pool(0, k // 2, "o16", 4)
+        act_unit(last, 4)
+        for k in range(4):
+            hadamard(1, k)
+
+        for k in range(4):
+            base_mm(2, k)
+        base_block(2)
+        dve_factors(last, range(4))
+        quant_d(6, whole)
+        for k in range(4):
+            gram(2, k)
+        for k in range(4):
+            base_mm(j, k)
+        base_block(j)
         cast(j - 2, 1, True)
         product(last, 0)
         finish(j - 3)
         store_scales(0, j - 2, [nc.sync])
         quant_d(last, half(0))
         product(last, 1)
-        for k in (0, 1):
-            gram_mm(j, k, 0, act_bank("gram"))
-        cast_on_pool(j - 2, last)
+        cast_on_pool(j - 2, 0, "relay%d" % last, 1)
         for k in range(4):
             hadamard(j - 1, k)
+            gram_mm(j, k, 0, dve_bank("gram"))
         quant_d(last, half(1))
         quant_o(j - 2, 0)
         store_words(j - 2, j - 1, 0, 1, nc.sync)
-        cast_on_pool(j - 1, last)
+        cast_on_pool(j - 1, 0, "relay%d" % last, 1)
         cast(j - 1, 1, True)
         for k in range(4):
             gram_mm(j, k, 1)
-            if k < 2:
-                gram_mm(j, k + 2, 0, act_bank("gram"))
             hadamard(j, k)
         cast(j, 0, True)
         cast(j, 1, True, slice(0, ACT_LAST))

@@ -31,15 +31,15 @@ def wide(side, chunk, g):
     return [(side, g, CHUNK * chunk, BANK)]
 
 
-UNITS = [narrow(X, 0), narrow(X, 1), wide(X, 2, 0), wide(X, 2, 1), wide(Y, 0, 0), wide(Y, 0, 1), narrow(Y, 2), narrow(Y, 3)]
-X_UNITS = 4
+UNITS = [narrow(X, 0), narrow(X, 1), wide(Y, 0, 0), wide(Y, 0, 1), wide(X, 2, 0), wide(X, 2, 1), narrow(Y, 2), narrow(Y, 3)]
+BLOCKS = [[(0, 0), (0, 1)], [(1, 0), (1, 1)], [(0, 2), (1, 2)], [(0, 3), (1, 3)]]
+LAST_ON_ACT = (0, 1, 2, 3)
 ACT_LAST = 96
-RELAY = (7,)
+RELAY = (6, 7)
 SIG_BUFS = {CHUNK: 4, BANK: 3}
 ACT_BANKS = (0, 2)
-SHARED = (2, 3)
-ACT_ALL = (5, 6, 7)
-ACT_TURNS = (0, 1, 2)
+SHARED = (2, 3, 4, 5)
+ACT_ALL = (6,)
 
 
 def tile_twotimehiddentangentkernel_x2_kernel(
@@ -109,17 +109,16 @@ def tile_twotimehiddentangentkernel_x2_kernel(
         load_vector(b16, 0, b)
         load_vector(v16, X, va)
         load_vector(v16, Y, vb)
-        load_rows(X, 2)
-        load_words(Y)
+        load_rows(Y, 0)
         load_scales(Y)
-        load_rows(X, 3)
-        for chunk in range(4):
-            load_rows(Y, chunk)
+        load_words(Y)
+        for side, chunk in ((Y, 1), (X, 2), (X, 3), (Y, 2), (Y, 3)):
+            load_rows(side, chunk)
 
-        def permute(dst, src):
+        def permute(dst, src, r0, r1):
             nc.vector.tensor_copy(
-                out=dst[:].bitcast(I32).rearrange("p (r q i) -> p r q i", r=8, q=16),
-                in_=src[:].bitcast(I32).rearrange("p (q r i) -> p r q i", r=8, q=16),
+                out=dst[:].bitcast(I32).rearrange("p (r q i) -> p r q i", r=8, q=16)[:, r0:r1, :, :],
+                in_=src[:].bitcast(I32).rearrange("p (q r i) -> p r q i", r=8, q=16)[:, r0:r1, :, :],
             )
 
         grouped, turned = {}, {}
@@ -249,15 +248,16 @@ def tile_twotimehiddentangentkernel_x2_kernel(
 
         base_banks, gram_banks, base_sb, o32, o16 = {}, {}, {}, {}, {}
 
-        def tiles_of(k):
-            return [(k // 2, 2 * (k % 2) + i, slice(CHUNK * i, CHUNK * (i + 1))) for i in (0, 1)]
+        def tiles_of(n, k):
+            h, j = BLOCKS[n][k // 2]
+            return [(h, 2 * (k % 2) + i, j, slice(CHUNK * i, CHUNK * (i + 1))) for i in (0, 1)]
 
-        def base_mm(j, k):
+        def base_mm(n, k):
             bank = act_bank("base")
-            base_banks[j, k] = bank
-            toks = slice(CHUNK * j, CHUNK * (j + 1))
-            for h, t, cols in tiles_of(k):
+            base_banks[n, k] = bank
+            for h, t, j, cols in tiles_of(n, k):
                 rows = slice(BANK * h + P * t, BANK * h + P * (t + 1))
+                toks = slice(CHUNK * j, CHUNK * (j + 1))
                 nc.tensor.matmul_mx(
                     out=bank[:, cols],
                     lhsT=codes[X][:, rows].bitcast(FP8X4),
@@ -268,18 +268,18 @@ def tile_twotimehiddentangentkernel_x2_kernel(
                     stop=True,
                 )
 
-        def base_out(j, k):
-            base_sb[j, k] = work.tile([P, BANK], F32, name="base_sb", tag="base_sb", bufs=8, align_bytes=64)
-            nc.scalar.activation(out=base_sb[j, k][:], in_=base_banks[j, k][:], func=ACT.Copy, scale=SCALE)
+        def base_out(n, k):
+            base_sb[n, k] = work.tile([P, BANK], F32, name="base_sb", tag="base_sb", bufs=8, align_bytes=64)
+            nc.scalar.activation(out=base_sb[n, k][:], in_=base_banks[n, k][:], func=ACT.Copy, scale=SCALE)
 
-        def gram_mm(j, k, g, bank=None):
-            if bank is not None:
-                gram_banks[j, k] = bank
-            for i, (h, t, cols) in enumerate(tiles_of(k)):
+        def gram_mm(n, k, g):
+            if g == 0:
+                gram_banks[n, k] = dve_bank("gram")
+            for i, (h, t, j, cols) in enumerate(tiles_of(n, k)):
                 ux, cx = d_at[X, g, BANK * h + P * t]
                 uy, cy = d_at[Y, g, CHUNK * j]
                 nc.tensor.matmul_mx(
-                    out=gram_banks[j, k][:, cols],
+                    out=gram_banks[n, k][:, cols],
                     lhsT=d_codes[ux][:, cx : cx + P].bitcast(FP8X4),
                     lhsT_scale=d_planes[ux][:, cx : cx + P],
                     rhs=d_codes[uy][:, cy : cy + CHUNK].bitcast(FP8X4),
@@ -288,69 +288,66 @@ def tile_twotimehiddentangentkernel_x2_kernel(
                     stop=(g == 1 and i == 1),
                 )
 
-        def gram(j, k):
-            gram_mm(j, k, 0, dve_bank("gram"))
-            gram_mm(j, k, 1)
+        def half(i):
+            return slice(CHUNK * i, CHUNK * (i + 1))
 
-        def half(h):
-            return slice(CHUNK * h, CHUNK * (h + 1))
-
-        def hadamard(j, k):
-            h, t0 = k // 2, 2 * (k % 2)
+        def hadamard(n, k):
+            h, j = BLOCKS[n][k // 2]
+            t0 = 2 * (k % 2)
             if t0 == 0:
-                o32[j, h] = work.tile([P, 4, CHUNK], F32, name="o32", tag="o32", bufs=6, align_bytes=64)
-            pair = o32[j, h][:, t0 : t0 + 2, :]
+                o32[h, j] = work.tile([P, 4, CHUNK], F32, name="o32", tag="o32", bufs=6, align_bytes=64)
+            pair = o32[h, j][:, t0 : t0 + 2, :]
             nc.vector.tensor_tensor(
-                out=pair.rearrange("p t c -> p (t c)"), in0=gram_banks[j, k][:], in1=base_sb[j, k][:], op=ALU.mult
+                out=pair.rearrange("p t c -> p (t c)"), in0=gram_banks[n, k][:], in1=base_sb[n, k][:], op=ALU.mult
             )
-            rows = out_0[BANK * h : BANK * (h + 1), CHUNK * j : CHUNK * (j + 1)].rearrange("(p t) m -> p t m", t=4)
+            rows = out_0[BANK * h : BANK * (h + 1), half(j)].rearrange("(p t) m -> p t m", t=4)
             nc.sync.dma_start(out=rows[:, t0 : t0 + 2, :], in_=pair)
 
-        def cast(j, h, on_act, cols=slice(0, CHUNK)):
-            if (j, h) not in o16:
-                o16[j, h] = work.tile([P, CHUNK, 4], BF16, name="o16", tag="o16", bufs=4, align_bytes=64)
-            dst, src = into_words(o16[j, h], cols), by_runs(o32[j, h][:, :, cols])
+        def cast(h, j, on_act, cols=slice(0, CHUNK)):
+            if (h, j) not in o16:
+                o16[h, j] = work.tile([P, CHUNK, 4], BF16, name="o16", tag="o16", bufs=4, align_bytes=64)
+            dst, src = into_words(o16[h, j], cols), by_runs(o32[h, j][:, :, cols])
             if on_act:
                 nc.scalar.copy(out=dst, in_=src)
             else:
                 nc.vector.tensor_copy(out=dst, in_=src)
 
-        def cast_on_pool(j, h, tag, bufs):
-            o16[j, h] = work.tile([P, CHUNK, 4], BF16, name="o16", tag=tag, bufs=bufs, align_bytes=64)
+        def cast_on_pool(h, j, tag, bufs):
+            o16[h, j] = work.tile([P, CHUNK, 4], BF16, name="o16", tag=tag, bufs=bufs, align_bytes=64)
             nc.gpsimd.tensor_scalar(
-                out=o16[j, h][:], in0=o32[j, h][:].rearrange("p t c -> p c t"),
+                out=o16[h, j][:], in0=o32[h, j][:].rearrange("p t c -> p c t"),
                 scalar1=1.0, scalar2=0.0, op0=ALU.mult, op1=ALU.add,
             )
 
         o_codes = keep.tile([P, 2, M], U32, name="o_codes", align_bytes=64)
         o_planes = keep.tile([P, 2, M], U8, name="o_planes", align_bytes=64)
 
-        def quant_o(j, h):
-            toks = slice(CHUNK * j, CHUNK * (j + 1))
+        def quant_o(h, j):
             nc.vector.quantize_mx(
-                out=o_codes[:, h, toks].bitcast(FP8X4),
-                scales=o_planes[:, h, toks],
-                in_=o16[j, h][:].rearrange("p n t -> p (n t)"),
+                out=o_codes[:, h, half(j)].bitcast(FP8X4),
+                scales=o_planes[:, h, half(j)],
+                in_=o16[h, j][:].rearrange("p n t -> p (n t)"),
             )
 
-        def store_words(j0, j1, h0, h1, queue):
+        def store_words(h, j0, j1):
             toks = slice(CHUNK * j0, CHUNK * j1)
-            queue.dma_start(
-                out=out_1[h0:h1, :, toks, :].rearrange("h p m t -> p h (m t)").bitcast(I32),
-                in_=o_codes[:, h0:h1, toks].bitcast(I32),
+            nc.sync.dma_start(
+                out=out_1[h][:, toks, :].rearrange("p m t -> p (m t)").bitcast(I32),
+                in_=o_codes[:, h, toks].bitcast(I32),
             )
 
-        def store_scales(j0, j1, queues):
-            toks = slice(CHUNK * j0, CHUNK * j1)
+        def store_scales():
             for q in range(4):
-                queues[q % len(queues)].dma_start(
-                    out=out_2[:, 4 * q : 4 * q + 4, toks].rearrange("h r m -> r h m").bitcast(I32),
-                    in_=o_planes[32 * q : 32 * q + 4, :, toks].bitcast(I32),
+                (nc.scalar, nc.sync)[q % 2].dma_start(
+                    out=out_2[:, 4 * q : 4 * q + 4, :].rearrange("h r m -> r h m").bitcast(I32),
+                    in_=o_planes[32 * q : 32 * q + 4, :, :].bitcast(I32),
                 )
 
         whole = slice(0, BANK)
 
         def shared(u):
+            if u == 7:
+                return LAST_ON_ACT
             if u in ACT_ALL:
                 return (0, 1, 2, 3)
             return ACT_BANKS if u in SHARED else ()
@@ -377,136 +374,144 @@ def tile_twotimehiddentangentkernel_x2_kernel(
         transposes(X, 0, dve_bank("turn"))
         transposes(X, 1, dve_bank("turn"))
         b_bank = turn_vector(b16)
-        permute(w_perm[X], w_raw[X])
+        permute(w_perm[X], w_raw[X], 0, 4)
         turn_out(X, 0, False)
-        permute(plane_perm[X], plane_raw[X])
+        permute(plane_perm[X], plane_raw[X], 0, 8)
         quant_in(X, 0)
+        permute(w_perm[X], w_raw[X], 4, 8)
         vector_out(b_bank, bias2, 2.0)
         turn_out(X, 1, False)
-        z_mm(0, 0)
+        for k in (0, 1):
+            z_mm(0, k)
         v_bank = turn_vector(v16)
+        permute(plane_perm[Y], plane_raw[Y], 0, 8)
         quant_in(X, 1)
         vector_out(v_bank, minus4v, -4.0)
         vector_out(v_bank, plus4v, 4.0)
-        for k in (1, 2, 3):
+        for k in (2, 3):
             z_mm(0, k)
         act_unit(0, 4)
-        transposes(X, 2, act_bank("turn"))
-        turn_out(X, 2, True)
-        dve_factors(0, (0,))
-        permute(w_perm[Y], w_raw[Y])
-        permute(plane_perm[Y], plane_raw[Y])
-        dve_factors(0, (1,))
+        def turn(side, chunk, on_act):
+            transposes(side, chunk, (act_bank if on_act else dve_bank)("turn"))
+            turn_out(side, chunk, on_act)
+
+        def base_block(n):
+            for k in range(4):
+                base_out(n, k)
+
+        def grams(n, g):
+            for k in range(4):
+                gram_mm(n, k, g)
+
+        turn(Y, 0, True)
+        dve_factors(0, (0, 1))
+        permute(w_perm[Y], w_raw[Y], 0, 8)
         product(0, 0)
         dve_factors(0, (2, 3))
-        quant_in(X, 2)
+        quant_in(Y, 0)
         product(0, 1)
         z_mm(1, 0)
         z_mm(1, 1)
-        transposes(X, 3, act_bank("turn"))
+        transposes(Y, 1, act_bank("turn"))
         act_pair(1, 0)
-        turn_out(X, 3, True)
+        turn_out(Y, 1, True)
         z_mm(1, 2)
         z_mm(1, 3)
         act_pair(1, 2)
+        quant_in(Y, 1)
 
-        def turn_y(chunk):
-            on_act = chunk in ACT_TURNS
-            transposes(Y, chunk, (act_bank if on_act else dve_bank)("turn"))
-            turn_out(Y, chunk, on_act)
-
-        quant_in(X, 3)
-        for u in range(1, X_UNITS + 1):
-            if u < X_UNITS:
-                turn_y(u - 1)
+        for u in (1, 2, 3):
+            side, chunk = ((X, 2), (X, 3), (Y, 2))[u - 1]
+            turn(side, chunk, True)
             dve_factors(u, range(4))
             quant_d(u - 1, whole)
-            if u < X_UNITS:
-                quant_in(Y, u - 1)
+            quant_in(side, chunk)
             act_unit(u + 1, 0)
+            if u == 3:
+                for k in range(4):
+                    base_mm(0, k)
+                grams(0, 0)
             for part in range(len(UNITS[u])):
                 product(u, part)
 
-        def finish(j):
-            for h in (1, 0):
-                quant_o(j, h)
-            store_words(j, j + 1, 0, 2, nc.sync)
+        base_block(0)
+        dve_factors(4, range(4))
+        quant_d(3, whole)
+        for k in (0, 1):
+            z_mm(5, k)
+        grams(0, 1)
+        act_unit(5, 2)
+        for k in (0, 1):
+            z_mm(6, k)
+        product(4, 0)
+        for k in range(4):
+            hadamard(0, k)
+            if k == 1:
+                cast_on_pool(0, 0, "o16", 4)
+        turn(Y, 3, False)
 
-        def base_block(j):
-            for k in range(4):
-                base_out(j, k)
-
-        last = len(UNITS) - 1
-        j = 3
-
-        turn_y(3)
         dve_factors(5, range(4))
         quant_d(4, whole)
-        act_unit(6, 0)
+        act_unit(6, 2)
+        for k in (0, 1):
+            base_mm(1, k)
+        grams(1, 0)
         product(5, 0)
 
-        for k in range(4):
-            base_mm(0, k)
-        base_block(0)
+        for k in (2, 3):
+            base_mm(1, k)
+        base_block(1)
         quant_in(Y, 3)
         dve_factors(6, range(4))
         quant_d(5, whole)
-        for k in range(4):
-            gram(0, k)
-            base_mm(1, k)
-        base_block(1)
-        for part in (0, 1):
-            product(6, part)
-        for k in (0, 1):
-            z_mm(last, k)
-        for k in range(4):
-            hadamard(0, k)
-            gram(1, k)
-            if k >= 2:
-                z_mm(last, k)
-            if k % 2 == 1:
-                cast_on_pool(0, k // 2, "o16", 4)
-        act_unit(last, 4)
+        grams(1, 1)
+        act_unit(7, 0)
+        product(6, 0)
+        quant_o(0, 0)
+        product(6, 1)
+        cast_on_pool(0, 1, "relay6", 1)
         for k in range(4):
             hadamard(1, k)
 
-        for k in range(4):
+        for k in (0, 1):
             base_mm(2, k)
-        base_block(2)
-        dve_factors(last, range(4))
         quant_d(6, whole)
         for k in range(4):
-            gram(2, k)
+            for g in (0, 1):
+                gram_mm(2, k, g)
+            if k % 2 == 1:
+                base_mm(2, 2 + k // 2)
+        base_block(2)
+        product(7, 0)
+        quant_o(0, 1)
+        store_words(0, 0, 2)
+        dve_factors(7, range(4))
+        quant_d(7, half(0))
+        product(7, 1)
+        cast_on_pool(1, 0, "relay7", 1)
         for k in range(4):
-            base_mm(j, k)
-        base_block(j)
-        cast(j - 2, 1, True)
-        product(last, 0)
-        finish(j - 3)
-        store_scales(0, j - 2, [nc.sync])
-        quant_d(last, half(0))
-        product(last, 1)
-        cast_on_pool(j - 2, 0, "relay%d" % last, 1)
+            base_mm(3, k)
+            base_out(3, k)
+            hadamard(2, k)
+            gram_mm(3, k, 0)
+        cast(1, 1, True)
+        quant_d(7, half(1))
+        quant_o(1, 0)
+        store_words(1, 0, 1)
+        cast_on_pool(0, 2, "relay7", 1)
+        cast(1, 2, True)
         for k in range(4):
-            hadamard(j - 1, k)
-            gram_mm(j, k, 0, dve_bank("gram"))
-        quant_d(last, half(1))
-        quant_o(j - 2, 0)
-        store_words(j - 2, j - 1, 0, 1, nc.sync)
-        cast_on_pool(j - 1, 0, "relay%d" % last, 1)
-        cast(j - 1, 1, True)
-        for k in range(4):
-            gram_mm(j, k, 1)
-            hadamard(j, k)
-        cast(j, 0, True)
-        cast(j, 1, True, slice(0, ACT_LAST))
-        quant_o(j - 2, 1)
-        quant_o(j - 1, 1)
-        store_words(j - 2, j, 1, 2, nc.sync)
-        quant_o(j - 1, 0)
-        cast(j, 1, False, slice(ACT_LAST, CHUNK))
-        quant_o(j, 0)
-        store_words(j - 1, j + 1, 0, 1, nc.sync)
-        quant_o(j, 1)
-        store_words(j, j + 1, 1, 2, nc.sync)
-        store_scales(j - 2, j + 1, [nc.scalar, nc.sync])
+            gram_mm(3, k, 1)
+            hadamard(3, k)
+        cast(0, 3, True)
+        cast(1, 3, True, slice(0, ACT_LAST))
+        quant_o(1, 1)
+        quant_o(1, 2)
+        store_words(1, 1, 3)
+        quant_o(0, 2)
+        cast(1, 3, False, slice(ACT_LAST, CHUNK))
+        quant_o(0, 3)
+        store_words(0, 2, 4)
+        quant_o(1, 3)
+        store_words(1, 3, 4)
+        store_scales()

@@ -33,9 +33,9 @@ def wide(side, chunk, g):
 
 UNITS = [narrow(X, 0), narrow(X, 1), wide(Y, 0, 0), wide(Y, 0, 1), wide(X, 2, 0), wide(X, 2, 1), narrow(Y, 2), narrow(Y, 3)]
 BLOCKS = [[(0, 0), (0, 1)], [(1, 0), (1, 1)], [(0, 2), (1, 2)], [(0, 3), (1, 3)]]
-LAST_ON_ACT = (0, 1, 2, 3)
-ACT_LAST = 96
-RELAY = (6, 7)
+Y2_ON_ACT = True
+LAST_ON_ACT = (0, 1, 2)
+RELAY = (6,)
 SIG_BUFS = {CHUNK: 4, BANK: 3}
 ACT_BANKS = (0, 2)
 SHARED = (2, 3, 4, 5)
@@ -225,7 +225,8 @@ def tile_twotimehiddentangentkernel_x2_kernel(
         def product(u, part):
             width = UNITS[u][part][3]
             if part == 0:
-                d16[u] = work.tile([P, BANK, 4], BF16, name="d16", tag="d16", bufs=2, align_bytes=64)
+                tag, bufs = ("relay7", 1) if u == 7 else ("d16", 2)
+                d16[u] = work.tile([P, BANK, 4], BF16, name="d16", tag=tag, bufs=bufs, align_bytes=64)
             nc.vector.tensor_tensor(
                 out=into_words(d16[u], slice(width * part, width * (part + 1))),
                 in0=by_runs(sig[u, part][:]),
@@ -274,7 +275,7 @@ def tile_twotimehiddentangentkernel_x2_kernel(
 
         def gram_mm(n, k, g):
             if g == 0:
-                gram_banks[n, k] = dve_bank("gram")
+                gram_banks[n, k] = (act_bank if n == 3 else dve_bank)("gram")
             for i, (h, t, j, cols) in enumerate(tiles_of(n, k)):
                 ux, cx = d_at[X, g, BANK * h + P * t]
                 uy, cy = d_at[Y, g, CHUNK * j]
@@ -303,14 +304,9 @@ def tile_twotimehiddentangentkernel_x2_kernel(
             rows = out_0[BANK * h : BANK * (h + 1), half(j)].rearrange("(p t) m -> p t m", t=4)
             nc.sync.dma_start(out=rows[:, t0 : t0 + 2, :], in_=pair)
 
-        def cast(h, j, on_act, cols=slice(0, CHUNK)):
-            if (h, j) not in o16:
-                o16[h, j] = work.tile([P, CHUNK, 4], BF16, name="o16", tag="o16", bufs=4, align_bytes=64)
-            dst, src = into_words(o16[h, j], cols), by_runs(o32[h, j][:, :, cols])
-            if on_act:
-                nc.scalar.copy(out=dst, in_=src)
-            else:
-                nc.vector.tensor_copy(out=dst, in_=src)
+        def cast(h, j):
+            o16[h, j] = work.tile([P, CHUNK, 4], BF16, name="o16", tag="o16", bufs=5, align_bytes=64)
+            nc.scalar.copy(out=into_words(o16[h, j], slice(0, CHUNK)), in_=by_runs(o32[h, j][:]))
 
         def cast_on_pool(h, j, tag, bufs):
             o16[h, j] = work.tile([P, CHUNK, 4], BF16, name="o16", tag=tag, bufs=bufs, align_bytes=64)
@@ -378,13 +374,12 @@ def tile_twotimehiddentangentkernel_x2_kernel(
         turn_out(X, 0, False)
         permute(plane_perm[X], plane_raw[X], 0, 8)
         quant_in(X, 0)
-        permute(w_perm[X], w_raw[X], 4, 8)
         vector_out(b_bank, bias2, 2.0)
         turn_out(X, 1, False)
         for k in (0, 1):
             z_mm(0, k)
         v_bank = turn_vector(v16)
-        permute(plane_perm[Y], plane_raw[Y], 0, 8)
+        permute(w_perm[X], w_raw[X], 4, 8)
         quant_in(X, 1)
         vector_out(v_bank, minus4v, -4.0)
         vector_out(v_bank, plus4v, 4.0)
@@ -404,7 +399,9 @@ def tile_twotimehiddentangentkernel_x2_kernel(
                 gram_mm(n, k, g)
 
         turn(Y, 0, True)
-        dve_factors(0, (0, 1))
+        dve_factors(0, (0,))
+        permute(plane_perm[Y], plane_raw[Y], 0, 8)
+        dve_factors(0, (1,))
         permute(w_perm[Y], w_raw[Y], 0, 8)
         product(0, 0)
         dve_factors(0, (2, 3))
@@ -422,7 +419,7 @@ def tile_twotimehiddentangentkernel_x2_kernel(
 
         for u in (1, 2, 3):
             side, chunk = ((X, 2), (X, 3), (Y, 2))[u - 1]
-            turn(side, chunk, True)
+            turn(side, chunk, side == X or Y2_ON_ACT)
             dve_factors(u, range(4))
             quant_d(u - 1, whole)
             quant_in(side, chunk)
@@ -447,7 +444,7 @@ def tile_twotimehiddentangentkernel_x2_kernel(
         for k in range(4):
             hadamard(0, k)
             if k == 1:
-                cast_on_pool(0, 0, "o16", 4)
+                cast_on_pool(0, 0, "o16", 5)
         turn(Y, 3, False)
 
         dve_factors(5, range(4))
@@ -466,15 +463,15 @@ def tile_twotimehiddentangentkernel_x2_kernel(
         quant_d(5, whole)
         grams(1, 1)
         act_unit(7, 0)
-        product(6, 0)
-        quant_o(0, 0)
-        product(6, 1)
+        for part in (0, 1):
+            product(6, part)
         cast_on_pool(0, 1, "relay6", 1)
         for k in range(4):
             hadamard(1, k)
 
         for k in (0, 1):
             base_mm(2, k)
+        dve_factors(7, (0, 1))
         quant_d(6, whole)
         for k in range(4):
             for g in (0, 1):
@@ -482,35 +479,34 @@ def tile_twotimehiddentangentkernel_x2_kernel(
             if k % 2 == 1:
                 base_mm(2, 2 + k // 2)
         base_block(2)
-        product(7, 0)
-        quant_o(0, 1)
-        store_words(0, 0, 2)
-        dve_factors(7, range(4))
-        quant_d(7, half(0))
-        product(7, 1)
-        cast_on_pool(1, 0, "relay7", 1)
         for k in range(4):
             base_mm(3, k)
-            base_out(3, k)
-            hadamard(2, k)
-            gram_mm(3, k, 0)
-        cast(1, 1, True)
-        quant_d(7, half(1))
-        quant_o(1, 0)
-        store_words(1, 0, 1)
-        cast_on_pool(0, 2, "relay7", 1)
-        cast(1, 2, True)
+        base_block(3)
+        product(7, 0)
+        dve_factors(7, (2, 3))
+        quant_o(0, 0)
+        product(7, 1)
+        quant_o(0, 1)
+        store_words(0, 0, 2)
+        quant_d(7, whole)
+        cast_on_pool(1, 0, "relay7", 1)
+        cast_on_pool(1, 1, "o16", 5)
         for k in range(4):
-            gram_mm(3, k, 1)
+            for g in (0, 1):
+                gram_mm(3, k, g)
+            hadamard(2, k)
+            if k == 1:
+                cast_on_pool(0, 2, "o16", 5)
+        cast(1, 2)
+        for k in range(4):
             hadamard(3, k)
-        cast(0, 3, True)
-        cast(1, 3, True, slice(0, ACT_LAST))
-        quant_o(1, 1)
-        quant_o(1, 2)
-        store_words(1, 1, 3)
-        quant_o(0, 2)
-        cast(1, 3, False, slice(ACT_LAST, CHUNK))
-        quant_o(0, 3)
+        for h in (0, 1):
+            cast(h, 3)
+        for j in range(3):
+            quant_o(1, j)
+        store_words(1, 0, 3)
+        for j in (2, 3):
+            quant_o(0, j)
         store_words(0, 2, 4)
         quant_o(1, 3)
         store_words(1, 3, 4)

@@ -19,27 +19,34 @@ BANK = 512
 CHUNK = 256
 RUN = 4
 FLOPS = 2 * (N * D * F + M * D * F + N * D * M + N * F * M)
-SCALE = 1.0 / (32.0 * 512.0 ** 0.5)
+SCALE = 1.0 / (F ** 0.5 * D ** 0.5)
 X, Y = 0, 1
+BANKS = range(4)
 
 
-def narrow(side, chunk):
-    return [(side, g, CHUNK * chunk, CHUNK) for g in (0, 1)]
+def wide(side, token, g):
+    return [(side, g, token, BANK)]
 
 
-def wide(side, chunk, g):
-    return [(side, g, CHUNK * chunk, BANK)]
+def narrow(side, token):
+    return [(side, g, token, CHUNK) for g in (0, 1)]
 
 
-UNITS = [narrow(X, 0), narrow(X, 1), wide(Y, 0, 0), wide(Y, 0, 1), wide(X, 2, 0), wide(X, 2, 1), narrow(Y, 2), narrow(Y, 3)]
+UNITS = [
+    [(X, 0, 0, CHUNK), (X, 0, CHUNK, CHUNK)],
+    wide(X, 0, 1),
+    wide(Y, 0, 0),
+    wide(Y, 0, 1),
+    wide(X, BANK, 0),
+    wide(X, BANK, 1),
+    narrow(Y, 2 * CHUNK),
+    narrow(Y, 3 * CHUNK),
+]
 BLOCKS = [[(0, 0), (0, 1)], [(1, 0), (1, 1)], [(0, 2), (1, 2)], [(0, 3), (1, 3)]]
-Y2_ON_ACT = True
-LAST_ON_ACT = (0, 1, 2)
-RELAY = (6,)
-SIG_BUFS = {CHUNK: 4, BANK: 3}
-ACT_BANKS = (0, 2)
-SHARED = (2, 3, 4, 5)
-ACT_ALL = (6,)
+LAST_BLOCK = len(BLOCKS) - 1
+SCALAR_FACTORS = [(), (), (0, 2), (0, 2), (0, 2), (0, 2), (0, 1, 2, 3), (0, 1, 2, 3)]
+STAGE_BUFS = {CHUNK: 4, BANK: 3}
+O16_BUFS = 5
 
 
 def tile_twotimehiddentangentkernel_x2_kernel(
@@ -52,19 +59,19 @@ def tile_twotimehiddentangentkernel_x2_kernel(
         psum = ctx.enter_context(tc.psum_pool(name="psum", bufs=1))
         ctx.enter_context(tc.manual_schedule())
 
-        def act_bank(name):
+        def scalar_bank(name):
             return psum.tile([P, BANK], F32, name=name, tag="act", bufs=4)
 
-        def dve_bank(name):
+        def vector_bank(name):
             return psum.tile([P, BANK], F32, name=name, tag="dve", bufs=4)
 
-        plane_raw = [keep.tile([P, F], U8, name="plane_raw%d" % s, align_bytes=64) for s in (X, Y)]
-        nc.vector.memset(plane_raw[X][:].bitcast(I32), 0)
-        nc.vector.memset(plane_raw[Y][:].bitcast(I32), 0)
-        b16 = keep.tile([P, P], BF16, name="b16", align_bytes=64)
-        v16 = keep.tile([P, P], BF16, name="v16", align_bytes=64)
-        nc.vector.memset(b16[:], 0.0)
-        nc.vector.memset(v16[:], 0.0)
+        plane_raw = [keep.tile([P, F], U8, name="plane_raw%d" % side, align_bytes=64) for side in (X, Y)]
+        for side in (X, Y):
+            nc.vector.memset(plane_raw[side][:].bitcast(I32), 0)
+        b_rows = keep.tile([P, P], BF16, name="b_rows", align_bytes=64)
+        v_rows = keep.tile([P, P], BF16, name="v_rows", align_bytes=64)
+        nc.vector.memset(b_rows[:], 0.0)
+        nc.vector.memset(v_rows[:], 0.0)
 
         ident = keep.tile([P, P], F32, name="ident", align_bytes=64)
         make_identity(nc, ident[:])
@@ -82,33 +89,33 @@ def tile_twotimehiddentangentkernel_x2_kernel(
                 view = y[CHUNK * chunk : CHUNK * (chunk + 1), :].rearrange("(j p) k -> p j k", j=2)
             nc.sync.dma_start(out=raw[side, chunk][:], in_=view)
 
-        w_raw = [keep.tile([P, 2 * F], U8, name="w_raw%d" % s, align_bytes=64) for s in (X, Y)]
-        w_perm = [keep.tile([P, 2 * F], U8, name="w_perm%d" % s, align_bytes=64) for s in (X, Y)]
-        plane_perm = [keep.tile([P, F], U8, name="plane_perm%d" % s, align_bytes=64) for s in (X, Y)]
+        w_raw = [keep.tile([P, 2 * F], U8, name="w_raw%d" % side, align_bytes=64) for side in (X, Y)]
+        w_perm = [keep.tile([P, 2 * F], U8, name="w_perm%d" % side, align_bytes=64) for side in (X, Y)]
+        plane_perm = [keep.tile([P, F], U8, name="plane_perm%d" % side, align_bytes=64) for side in (X, Y)]
 
         def load_scales(side):
-            for q in range(4):
+            for quad in range(4):
                 nc.sync.dma_start(
-                    out=plane_raw[side][32 * q : 32 * q + 4, :].bitcast(I32),
-                    in_=(wa_scales, wb_scales)[side][0][4 * q : 4 * q + 4, :].bitcast(I32),
+                    out=plane_raw[side][32 * quad : 32 * quad + 4, :].bitcast(I32),
+                    in_=(wa_scales, wb_scales)[side][0][4 * quad : 4 * quad + 4, :].bitcast(I32),
                 )
 
         def load_words(side):
             nc.sync.dma_start(out=w_raw[side][:].bitcast(I32), in_=(wa_words, wb_words)[side][0].bitcast(I32))
 
-        def load_vector(rows, j, v):
+        def load_vector(rows, first, vec):
             nc.sync.dma_start(
-                out=rows[8 * j : 8 * j + 8, :].rearrange("r (q i) -> r q i", i=8),
-                in_=v.rearrange("(q r i) -> r q i", r=8, i=8),
+                out=rows[first : first + 8, :].rearrange("r (q i) -> r q i", i=8),
+                in_=vec.rearrange("(q r i) -> r q i", r=8, i=8),
             )
 
         load_rows(X, 0)
         load_words(X)
         load_scales(X)
         load_rows(X, 1)
-        load_vector(b16, 0, b)
-        load_vector(v16, X, va)
-        load_vector(v16, Y, vb)
+        load_vector(b_rows, 0, b)
+        load_vector(v_rows, 8 * X, va)
+        load_vector(v_rows, 8 * Y, vb)
         load_rows(Y, 0)
         load_scales(Y)
         load_words(Y)
@@ -121,32 +128,38 @@ def tile_twotimehiddentangentkernel_x2_kernel(
                 in_=src[:].bitcast(I32).rearrange("p (q r i) -> p r q i", r=8, q=16)[:, r0:r1, :, :],
             )
 
-        grouped, turned = {}, {}
-        codes = [keep.tile([P, N], U32, name="codes%d" % s, align_bytes=64) for s in (X, Y)]
-        planes = [keep.tile([P, N], U8, name="planes%d" % s, align_bytes=64) for s in (X, Y)]
+        turned = {}
+        grouped = [keep.tile([P, 4 * N], BF16, name="grouped%d" % side, align_bytes=64) for side in (X, Y)]
+        codes = [keep.tile([P, N], U32, name="codes%d" % side, align_bytes=64) for side in (X, Y)]
+        planes = [keep.tile([P, N], U8, name="planes%d" % side, align_bytes=64) for side in (X, Y)]
 
         def transposes(side, chunk, bank):
             turned[side, chunk] = bank
             for j in (0, 1):
-                words = raw[side, chunk][:, j, :].bitcast(F32)
+                pairs = raw[side, chunk][:, j, :].bitcast(F32)
                 for u in (0, 1):
                     col = P * (2 * j + u)
-                    nc.tensor.transpose(bank[:, col : col + P], words[:, u : D // 2 : 2], ident[:])
+                    nc.tensor.transpose(bank[:, col : col + P], pairs[:, u : D // 2 : 2], ident[:])
 
-        def turn_out(side, chunk, on_act):
-            g16 = keep.tile([P, 4 * CHUNK], BF16, name="grouped_%d%d" % (side, chunk), align_bytes=64)
-            grouped[side, chunk] = g16
-            dst = g16[:].bitcast(F32).rearrange("p (j r u) -> p j r u", j=2, u=2)
+        def turn_out(side, chunk, on_scalar):
+            pairs = grouped[side][:, 4 * CHUNK * chunk : 4 * CHUNK * (chunk + 1)].bitcast(F32)
+            dst = pairs.rearrange("p (j r u) -> p j r u", j=2, u=2)
             src = turned[side, chunk][:].rearrange("p (j u r) -> p j r u", j=2, u=2)
-            if on_act:
+            if on_scalar:
                 nc.scalar.copy(out=dst, in_=src)
             else:
                 nc.vector.tensor_copy(out=dst, in_=src)
 
-        def quant_in(side, chunk):
-            cols = slice(CHUNK * chunk, CHUNK * (chunk + 1))
+        def turn(side, chunk, on_scalar):
+            transposes(side, chunk, (scalar_bank if on_scalar else vector_bank)("turn"))
+            turn_out(side, chunk, on_scalar)
+
+        def quant_in(side, chunk, chunks=1):
+            c0, c1 = CHUNK * chunk, CHUNK * (chunk + chunks)
             nc.vector.quantize_mx(
-                out=codes[side][:, cols].bitcast(FP8X4), scales=planes[side][:, cols], in_=grouped[side, chunk][:]
+                out=codes[side][:, c0:c1].bitcast(FP8X4),
+                scales=planes[side][:, c0:c1],
+                in_=grouped[side][:, 4 * c0 : 4 * c1],
             )
 
         bias2 = keep.tile([P, 8], F32, name="bias2")
@@ -165,150 +178,177 @@ def tile_twotimehiddentangentkernel_x2_kernel(
 
         z_banks, sig, fac, d16, d_codes, d_planes, d_at = {}, {}, {}, {}, {}, {}, {}
 
-        def pieces(u, k):
-            parts = [(part, t) for part in range(len(UNITS[u])) for t in range(4)]
+        def slots_in_bank(u, k):
+            slots = [(part, t) for part in range(len(UNITS[u])) for t in range(4)]
             each = len(UNITS[u])
             width = BANK // each
-            return [parts[each * k + i] + (slice(width * i, width * (i + 1)),) for i in range(each)]
+            return [slots[each * k + i] + (slice(width * i, width * (i + 1)),) for i in range(each)]
 
         def z_mm(u, k):
-            z = act_bank("z")
+            z = scalar_bank("z")
             z_banks[u, k] = z
-            for part, t, at in pieces(u, k):
-                side, g, tok, width = UNITS[u][part]
+            for part, t, at in slots_in_bank(u, k):
+                side, g, token, width = UNITS[u][part]
                 r = 4 * g + t
                 nc.tensor.matmul_mx(
                     out=z[:, at],
                     lhsT=w_perm[side][:, 2 * P * r : 2 * P * (r + 1)].bitcast(FP4X4),
                     lhsT_scale=plane_perm[side][:, P * r : P * (r + 1)],
-                    rhs=codes[side][:, tok : tok + width].bitcast(FP8X4),
-                    rhs_scale=planes[side][:, tok : tok + width],
+                    rhs=codes[side][:, token : token + width].bitcast(FP8X4),
+                    rhs_scale=planes[side][:, token : token + width],
                     start=True,
                     stop=True,
                 )
 
         def sigmoid(u, k):
-            for part, t, at in pieces(u, k):
-                side, g, tok, width = UNITS[u][part]
+            for part, t, at in slots_in_bank(u, k):
+                side, g, token, width = UNITS[u][part]
                 if t == 0:
-                    tag, bufs = "%d" % width, SIG_BUFS[width]
-                    sig[u, part] = work.tile([P, 4, width], F32, name="sig", tag="sig" + tag, bufs=bufs, align_bytes=64)
-                    fac_tag, fac_bufs = ("relay%d" % u, 1) if u in RELAY and part == 1 else ("fac" + tag, bufs)
-                    fac[u, part] = work.tile([P, 4, width], F32, name="fac", tag=fac_tag, bufs=fac_bufs, align_bytes=64)
+                    bufs = STAGE_BUFS[width]
+                    sig[u, part] = work.tile(
+                        [P, 4, width], F32, name="sig", tag="sig%d" % width, bufs=bufs, align_bytes=64
+                    )
+                    tag, bufs = ("relay6", 1) if (u, part) == (6, 1) else ("fac%d" % width, bufs)
+                    fac[u, part] = work.tile([P, 4, width], F32, name="fac", tag=tag, bufs=bufs, align_bytes=64)
                 r = 4 * g + t
                 nc.scalar.activation(
                     out=sig[u, part][:, t, :], in_=z_banks[u, k][:, at], func=ACT.Sigmoid,
                     bias=bias2[:, r : r + 1], scale=2.0,
                 )
 
-        def factor(u, k, on_act):
-            for part, t, at in pieces(u, k):
-                side, g, tok, width = UNITS[u][part]
+        def factor_operands(u, k):
+            for_bank = []
+            for part, t, at in slots_in_bank(u, k):
+                side, g, token, width = UNITS[u][part]
                 c = 8 * side + 4 * g + t
-                if on_act:
-                    nc.scalar.activation(
-                        out=fac[u, part][:, t, :], in_=sig[u, part][:, t, :], func=ACT.Identity,
-                        bias=plus4v[:, c : c + 1], scale=minus4v[:, c : c + 1],
-                    )
-                else:
-                    nc.vector.tensor_scalar(
-                        out=fac[u, part][:, t, :], in0=sig[u, part][:, t, :],
-                        scalar1=1.0, scalar2=minus4v[:, c : c + 1], op0=ALU.subtract, op1=ALU.mult,
-                    )
+                for_bank.append(
+                    (fac[u, part][:, t, :], sig[u, part][:, t, :], minus4v[:, c : c + 1], plus4v[:, c : c + 1])
+                )
+            return for_bank
 
-        def by_runs(planes4):
-            return planes4.rearrange("p t (c i) -> p c t i", i=RUN)
+        def scalar_factor(u, k):
+            for dst, s, minus, plus in factor_operands(u, k):
+                nc.scalar.activation(out=dst, in_=s, func=ACT.Identity, bias=plus, scale=minus)
 
-        def into_words(tile16, cols):
-            return tile16[:, cols, :].rearrange("p (c i) t -> p c t i", i=RUN)
+        def vector_factors(u, banks):
+            for k in banks:
+                if k not in SCALAR_FACTORS[u]:
+                    for dst, s, minus, plus in factor_operands(u, k):
+                        nc.vector.tensor_scalar(
+                            out=dst, in0=s, scalar1=1.0, scalar2=minus, op0=ALU.subtract, op1=ALU.mult
+                        )
 
-        def product(u, part):
-            width = UNITS[u][part][3]
-            if part == 0:
-                tag, bufs = ("relay7", 1) if u == 7 else ("d16", 2)
-                d16[u] = work.tile([P, BANK, 4], BF16, name="d16", tag=tag, bufs=bufs, align_bytes=64)
-            nc.vector.tensor_tensor(
-                out=into_words(d16[u], slice(width * part, width * (part + 1))),
-                in0=by_runs(sig[u, part][:]),
-                in1=by_runs(fac[u, part][:]),
-                op=ALU.mult,
-            )
+        def pool_factor(u, k):
+            for dst, s, minus, plus in factor_operands(u, k):
+                nc.gpsimd.tensor_scalar(out=dst, in0=s, scalar1=minus, scalar2=plus, op0=ALU.mult, op1=ALU.add)
 
-        def quant_d(u, cols):
-            if cols.start == 0:
-                d_codes[u] = keep.tile([P, BANK], U32, name="d_codes%d" % u, align_bytes=64)
-                d_planes[u] = keep.tile([P, BANK], U8, name="d_planes%d" % u, align_bytes=64)
-                for part, (side, g, tok, width) in enumerate(UNITS[u]):
-                    for k in range(0, width, P):
-                        d_at[side, g, tok + k] = (u, width * part + k)
+        def scalar_unit(u, staged):
+            for pair in ((0, 1), (2, 3)):
+                for k in pair:
+                    if k >= staged:
+                        z_mm(u, k)
+                for k in pair:
+                    sigmoid(u, k)
+                for k in pair:
+                    if k in SCALAR_FACTORS[u]:
+                        scalar_factor(u, k)
+
+        def by_runs(slots4):
+            return slots4.rearrange("p t (c i) -> p c t i", i=RUN)
+
+        def into_words(tile16):
+            return tile16.rearrange("p (c i) t -> p c t i", i=RUN)
+
+        def products(u, parts):
+            for part in parts:
+                width = UNITS[u][part][3]
+                if part == 0:
+                    tag, bufs = ("relay7", 1) if u == 7 else ("d16", 2)
+                    d16[u] = work.tile([P, BANK, 4], BF16, name="d16", tag=tag, bufs=bufs, align_bytes=64)
+                nc.vector.tensor_tensor(
+                    out=into_words(d16[u][:, width * part : width * (part + 1), :]),
+                    in0=by_runs(sig[u, part][:]),
+                    in1=by_runs(fac[u, part][:]),
+                    op=ALU.mult,
+                )
+
+        def quant_d(u):
+            d_codes[u] = keep.tile([P, BANK], U32, name="d_codes%d" % u, align_bytes=64)
+            d_planes[u] = keep.tile([P, BANK], U8, name="d_planes%d" % u, align_bytes=64)
+            for part, (side, g, token, width) in enumerate(UNITS[u]):
+                for step in range(0, width, P):
+                    d_at[side, g, token + step] = (u, width * part + step)
             nc.vector.quantize_mx(
-                out=d_codes[u][:, cols].bitcast(FP8X4),
-                scales=d_planes[u][:, cols],
-                in_=d16[u][:, cols, :].rearrange("p n t -> p (n t)"),
+                out=d_codes[u][:].bitcast(FP8X4),
+                scales=d_planes[u][:],
+                in_=d16[u][:].rearrange("p n t -> p (n t)"),
             )
 
         base_banks, gram_banks, base_sb, o32, o16 = {}, {}, {}, {}, {}
 
-        def tiles_of(n, k):
+        def chunk_cols(j):
+            return slice(CHUNK * j, CHUNK * (j + 1))
+
+        def tiles_in_bank(n, k):
             h, j = BLOCKS[n][k // 2]
-            return [(h, 2 * (k % 2) + i, j, slice(CHUNK * i, CHUNK * (i + 1))) for i in (0, 1)]
+            return [(h, 2 * (k % 2) + i, j, chunk_cols(i)) for i in (0, 1)]
 
-        def base_mm(n, k):
-            bank = act_bank("base")
-            base_banks[n, k] = bank
-            for h, t, j, cols in tiles_of(n, k):
-                rows = slice(BANK * h + P * t, BANK * h + P * (t + 1))
-                toks = slice(CHUNK * j, CHUNK * (j + 1))
-                nc.tensor.matmul_mx(
-                    out=bank[:, cols],
-                    lhsT=codes[X][:, rows].bitcast(FP8X4),
-                    lhsT_scale=planes[X][:, rows],
-                    rhs=codes[Y][:, toks].bitcast(FP8X4),
-                    rhs_scale=planes[Y][:, toks],
-                    start=True,
-                    stop=True,
+        def base_mm(n, banks):
+            for k in banks:
+                base_banks[n, k] = scalar_bank("base")
+                for h, t, j, at in tiles_in_bank(n, k):
+                    rows = slice(BANK * h + P * t, BANK * h + P * (t + 1))
+                    nc.tensor.matmul_mx(
+                        out=base_banks[n, k][:, at],
+                        lhsT=codes[X][:, rows].bitcast(FP8X4),
+                        lhsT_scale=planes[X][:, rows],
+                        rhs=codes[Y][:, chunk_cols(j)].bitcast(FP8X4),
+                        rhs_scale=planes[Y][:, chunk_cols(j)],
+                        start=True,
+                        stop=True,
+                    )
+
+        def base_out(n):
+            for k in BANKS:
+                base_sb[n, k] = work.tile([P, BANK], F32, name="base_sb", tag="base_sb", bufs=8, align_bytes=64)
+                nc.scalar.activation(out=base_sb[n, k][:], in_=base_banks[n, k][:], func=ACT.Copy, scale=SCALE)
+
+        def gram_mm(n, banks, passes):
+            for k in banks:
+                for g in passes:
+                    if g == 0:
+                        gram_banks[n, k] = (scalar_bank if n == LAST_BLOCK else vector_bank)("gram")
+                    for i, (h, t, j, at) in enumerate(tiles_in_bank(n, k)):
+                        ux, cx = d_at[X, g, BANK * h + P * t]
+                        uy, cy = d_at[Y, g, CHUNK * j]
+                        nc.tensor.matmul_mx(
+                            out=gram_banks[n, k][:, at],
+                            lhsT=d_codes[ux][:, cx : cx + P].bitcast(FP8X4),
+                            lhsT_scale=d_planes[ux][:, cx : cx + P],
+                            rhs=d_codes[uy][:, cy : cy + CHUNK].bitcast(FP8X4),
+                            rhs_scale=d_planes[uy][:, cy : cy + CHUNK],
+                            start=(g == 0 and i == 0),
+                            stop=(g == 1 and i == 1),
+                        )
+
+        def hadamard(n, banks):
+            for k in banks:
+                h, j = BLOCKS[n][k // 2]
+                t0 = 2 * (k % 2)
+                if t0 == 0:
+                    o32[h, j] = work.tile([P, 4, CHUNK], F32, name="o32", tag="o32", bufs=6, align_bytes=64)
+                pair = o32[h, j][:, t0 : t0 + 2, :]
+                nc.vector.tensor_tensor(
+                    out=pair.rearrange("p t c -> p (t c)"), in0=gram_banks[n, k][:], in1=base_sb[n, k][:], op=ALU.mult
                 )
+                rows = out_0[BANK * h : BANK * (h + 1), chunk_cols(j)].rearrange("(p t) m -> p t m", t=4)
+                nc.sync.dma_start(out=rows[:, t0 : t0 + 2, :], in_=pair)
 
-        def base_out(n, k):
-            base_sb[n, k] = work.tile([P, BANK], F32, name="base_sb", tag="base_sb", bufs=8, align_bytes=64)
-            nc.scalar.activation(out=base_sb[n, k][:], in_=base_banks[n, k][:], func=ACT.Copy, scale=SCALE)
+        def scalar_cast(h, j):
+            o16[h, j] = work.tile([P, CHUNK, 4], BF16, name="o16", tag="o16", bufs=O16_BUFS, align_bytes=64)
+            nc.scalar.copy(out=into_words(o16[h, j][:]), in_=by_runs(o32[h, j][:]))
 
-        def gram_mm(n, k, g):
-            if g == 0:
-                gram_banks[n, k] = (act_bank if n == 3 else dve_bank)("gram")
-            for i, (h, t, j, cols) in enumerate(tiles_of(n, k)):
-                ux, cx = d_at[X, g, BANK * h + P * t]
-                uy, cy = d_at[Y, g, CHUNK * j]
-                nc.tensor.matmul_mx(
-                    out=gram_banks[n, k][:, cols],
-                    lhsT=d_codes[ux][:, cx : cx + P].bitcast(FP8X4),
-                    lhsT_scale=d_planes[ux][:, cx : cx + P],
-                    rhs=d_codes[uy][:, cy : cy + CHUNK].bitcast(FP8X4),
-                    rhs_scale=d_planes[uy][:, cy : cy + CHUNK],
-                    start=(g == 0 and i == 0),
-                    stop=(g == 1 and i == 1),
-                )
-
-        def half(i):
-            return slice(CHUNK * i, CHUNK * (i + 1))
-
-        def hadamard(n, k):
-            h, j = BLOCKS[n][k // 2]
-            t0 = 2 * (k % 2)
-            if t0 == 0:
-                o32[h, j] = work.tile([P, 4, CHUNK], F32, name="o32", tag="o32", bufs=6, align_bytes=64)
-            pair = o32[h, j][:, t0 : t0 + 2, :]
-            nc.vector.tensor_tensor(
-                out=pair.rearrange("p t c -> p (t c)"), in0=gram_banks[n, k][:], in1=base_sb[n, k][:], op=ALU.mult
-            )
-            rows = out_0[BANK * h : BANK * (h + 1), half(j)].rearrange("(p t) m -> p t m", t=4)
-            nc.sync.dma_start(out=rows[:, t0 : t0 + 2, :], in_=pair)
-
-        def cast(h, j):
-            o16[h, j] = work.tile([P, CHUNK, 4], BF16, name="o16", tag="o16", bufs=5, align_bytes=64)
-            nc.scalar.copy(out=into_words(o16[h, j], slice(0, CHUNK)), in_=by_runs(o32[h, j][:]))
-
-        def cast_on_pool(h, j, tag, bufs):
+        def pool_cast(h, j, tag="o16", bufs=O16_BUFS):
             o16[h, j] = work.tile([P, CHUNK, 4], BF16, name="o16", tag=tag, bufs=bufs, align_bytes=64)
             nc.gpsimd.tensor_scalar(
                 out=o16[h, j][:], in0=o32[h, j][:].rearrange("p t c -> p c t"),
@@ -320,56 +360,29 @@ def tile_twotimehiddentangentkernel_x2_kernel(
 
         def quant_o(h, j):
             nc.vector.quantize_mx(
-                out=o_codes[:, h, half(j)].bitcast(FP8X4),
-                scales=o_planes[:, h, half(j)],
+                out=o_codes[:, h, chunk_cols(j)].bitcast(FP8X4),
+                scales=o_planes[:, h, chunk_cols(j)],
                 in_=o16[h, j][:].rearrange("p n t -> p (n t)"),
             )
 
         def store_words(h, j0, j1):
-            toks = slice(CHUNK * j0, CHUNK * j1)
+            cols = slice(CHUNK * j0, CHUNK * j1)
             nc.sync.dma_start(
-                out=out_1[h][:, toks, :].rearrange("p m t -> p (m t)").bitcast(I32),
-                in_=o_codes[:, h, toks].bitcast(I32),
+                out=out_1[h][:, cols, :].rearrange("p m t -> p (m t)").bitcast(I32),
+                in_=o_codes[:, h, cols].bitcast(I32),
             )
 
         def store_scales():
-            for q in range(4):
-                (nc.scalar, nc.sync)[q % 2].dma_start(
-                    out=out_2[:, 4 * q : 4 * q + 4, :].rearrange("h r m -> r h m").bitcast(I32),
-                    in_=o_planes[32 * q : 32 * q + 4, :, :].bitcast(I32),
+            for quad in range(4):
+                (nc.scalar, nc.sync)[quad % 2].dma_start(
+                    out=out_2[:, 4 * quad : 4 * quad + 4, :].rearrange("h r m -> r h m").bitcast(I32),
+                    in_=o_planes[32 * quad : 32 * quad + 4, :, :].bitcast(I32),
                 )
 
-        whole = slice(0, BANK)
 
-        def shared(u):
-            if u == 7:
-                return LAST_ON_ACT
-            if u in ACT_ALL:
-                return (0, 1, 2, 3)
-            return ACT_BANKS if u in SHARED else ()
-
-        def act_pair(u, pair):
-            for k in (pair, pair + 1):
-                sigmoid(u, k)
-            for k in (pair, pair + 1):
-                if k in shared(u):
-                    factor(u, k, True)
-
-        def act_unit(u, staged):
-            for pair in (0, 2):
-                for k in (pair, pair + 1):
-                    if k >= staged:
-                        z_mm(u, k)
-                act_pair(u, pair)
-
-        def dve_factors(u, banks):
-            for k in banks:
-                if k not in shared(u):
-                    factor(u, k, False)
-
-        transposes(X, 0, dve_bank("turn"))
-        transposes(X, 1, dve_bank("turn"))
-        b_bank = turn_vector(b16)
+        for chunk in (0, 1):
+            transposes(X, chunk, vector_bank("turn"))
+        b_bank = turn_vector(b_rows)
         permute(w_perm[X], w_raw[X], 0, 4)
         turn_out(X, 0, False)
         permute(plane_perm[X], plane_raw[X], 0, 8)
@@ -378,130 +391,95 @@ def tile_twotimehiddentangentkernel_x2_kernel(
         turn_out(X, 1, False)
         for k in (0, 1):
             z_mm(0, k)
-        v_bank = turn_vector(v16)
+        v_bank = turn_vector(v_rows)
         permute(w_perm[X], w_raw[X], 4, 8)
         quant_in(X, 1)
         vector_out(v_bank, minus4v, -4.0)
         vector_out(v_bank, plus4v, 4.0)
         for k in (2, 3):
             z_mm(0, k)
-        act_unit(0, 4)
-        def turn(side, chunk, on_act):
-            transposes(side, chunk, (act_bank if on_act else dve_bank)("turn"))
-            turn_out(side, chunk, on_act)
-
-        def base_block(n):
-            for k in range(4):
-                base_out(n, k)
-
-        def grams(n, g):
-            for k in range(4):
-                gram_mm(n, k, g)
-
-        turn(Y, 0, True)
-        dve_factors(0, (0,))
+        scalar_unit(0, 4)
+        for chunk in (0, 1):
+            turn(Y, chunk, True)
+        vector_factors(0, (0,))
         permute(plane_perm[Y], plane_raw[Y], 0, 8)
-        dve_factors(0, (1,))
+        vector_factors(0, (1,))
         permute(w_perm[Y], w_raw[Y], 0, 8)
-        product(0, 0)
-        dve_factors(0, (2, 3))
-        quant_in(Y, 0)
-        product(0, 1)
-        z_mm(1, 0)
-        z_mm(1, 1)
-        transposes(Y, 1, act_bank("turn"))
-        act_pair(1, 0)
-        turn_out(Y, 1, True)
-        z_mm(1, 2)
-        z_mm(1, 3)
-        act_pair(1, 2)
-        quant_in(Y, 1)
+        products(0, (0,))
+        vector_factors(0, (2, 3))
+        quant_in(Y, 0, 2)
+        products(0, (1,))
+        scalar_unit(1, 0)
 
-        for u in (1, 2, 3):
-            side, chunk = ((X, 2), (X, 3), (Y, 2))[u - 1]
-            turn(side, chunk, side == X or Y2_ON_ACT)
-            dve_factors(u, range(4))
-            quant_d(u - 1, whole)
+        for u, (side, chunk) in zip((1, 2, 3), ((X, 2), (X, 3), (Y, 2))):
+            turn(side, chunk, True)
+            vector_factors(u, BANKS)
+            quant_d(u - 1)
             quant_in(side, chunk)
-            act_unit(u + 1, 0)
+            scalar_unit(u + 1, 0)
             if u == 3:
-                for k in range(4):
-                    base_mm(0, k)
-                grams(0, 0)
-            for part in range(len(UNITS[u])):
-                product(u, part)
+                base_mm(0, BANKS)
+                gram_mm(0, BANKS, (0,))
+            products(u, (0,))
 
-        base_block(0)
-        dve_factors(4, range(4))
-        quant_d(3, whole)
+        base_out(0)
+        vector_factors(4, BANKS)
+        quant_d(3)
         for k in (0, 1):
             z_mm(5, k)
-        grams(0, 1)
-        act_unit(5, 2)
+        gram_mm(0, BANKS, (1,))
+        scalar_unit(5, 2)
+        pool_factor(5, 1)
         for k in (0, 1):
             z_mm(6, k)
-        product(4, 0)
-        for k in range(4):
-            hadamard(0, k)
-            if k == 1:
-                cast_on_pool(0, 0, "o16", 5)
+        products(4, (0,))
+        hadamard(0, (0, 1))
+        pool_cast(0, 0)
+        hadamard(0, (2, 3))
         turn(Y, 3, False)
 
-        dve_factors(5, range(4))
-        quant_d(4, whole)
-        act_unit(6, 2)
-        for k in (0, 1):
-            base_mm(1, k)
-        grams(1, 0)
-        product(5, 0)
+        vector_factors(5, (3,))
+        quant_d(4)
+        scalar_unit(6, 2)
+        base_mm(1, (0, 1))
+        gram_mm(1, BANKS, (0,))
+        products(5, (0,))
 
-        for k in (2, 3):
-            base_mm(1, k)
-        base_block(1)
+        base_mm(1, (2, 3))
+        base_out(1)
         quant_in(Y, 3)
-        dve_factors(6, range(4))
-        quant_d(5, whole)
-        grams(1, 1)
-        act_unit(7, 0)
-        for part in (0, 1):
-            product(6, part)
-        cast_on_pool(0, 1, "relay6", 1)
-        for k in range(4):
-            hadamard(1, k)
+        quant_d(5)
+        gram_mm(1, BANKS, (1,))
+        scalar_unit(7, 0)
+        products(6, (0, 1))
+        pool_cast(0, 1, "relay6", 1)
+        hadamard(1, BANKS)
 
-        for k in (0, 1):
-            base_mm(2, k)
-        dve_factors(7, (0, 1))
-        quant_d(6, whole)
-        for k in range(4):
-            for g in (0, 1):
-                gram_mm(2, k, g)
-            if k % 2 == 1:
-                base_mm(2, 2 + k // 2)
-        base_block(2)
-        for k in range(4):
-            base_mm(3, k)
-        base_block(3)
-        product(7, 0)
-        dve_factors(7, (2, 3))
-        quant_o(0, 0)
-        product(7, 1)
-        quant_o(0, 1)
+        base_mm(2, (0, 1))
+        quant_d(6)
+        for pair, k in (((0, 1), 2), ((2, 3), 3)):
+            gram_mm(2, pair, (0, 1))
+            base_mm(2, (k,))
+        base_out(2)
+        base_mm(3, BANKS)
+        base_out(3)
+        for part in (0, 1):
+            products(7, (part,))
+            quant_o(0, part)
         store_words(0, 0, 2)
-        quant_d(7, whole)
-        cast_on_pool(1, 0, "relay7", 1)
-        cast_on_pool(1, 1, "o16", 5)
-        for k in range(4):
-            for g in (0, 1):
-                gram_mm(3, k, g)
-            hadamard(2, k)
+        quant_d(7)
+
+        pool_cast(1, 0, "relay7", 1)
+        pool_cast(1, 1)
+        for k in BANKS:
+            gram_mm(3, (k,), (0, 1))
+            hadamard(2, (k,))
             if k == 1:
-                cast_on_pool(0, 2, "o16", 5)
-        cast(1, 2)
-        for k in range(4):
-            hadamard(3, k)
+                pool_cast(0, 2)
+        scalar_cast(1, 2)
+        hadamard(3, BANKS)
         for h in (0, 1):
-            cast(h, 3)
+            scalar_cast(h, 3)
         for j in range(3):
             quant_o(1, j)
         store_words(1, 0, 3)

@@ -44,7 +44,16 @@ UNITS = [
 ]
 BLOCKS = [[(0, 0), (0, 1)], [(1, 0), (1, 1)], [(0, 2), (1, 2)], [(0, 3), (1, 3)]]
 LAST_BLOCK = len(BLOCKS) - 1
-SCALAR_FACTORS = [(), (), (0, 2), (0, 2), (0, 2), (0, 2), (0, 1, 2, 3), (0, 1, 2, 3)]
+
+
+def scalar_factors(u):
+    if u < 2:
+        return ()
+    if u == 6:
+        return (0, 1, 2, 3)
+    return (0, 2)
+
+
 STAGE_BUFS = {CHUNK: 4, BANK: 3}
 O16_BUFS = 5
 
@@ -232,15 +241,11 @@ def tile_twotimehiddentangentkernel_x2_kernel(
 
         def vector_factors(u, banks):
             for k in banks:
-                if k not in SCALAR_FACTORS[u]:
+                if k not in scalar_factors(u):
                     for dst, s, minus, plus in factor_operands(u, k):
                         nc.vector.tensor_scalar(
                             out=dst, in0=s, scalar1=1.0, scalar2=minus, op0=ALU.subtract, op1=ALU.mult
                         )
-
-        def pool_factor(u, k):
-            for dst, s, minus, plus in factor_operands(u, k):
-                nc.gpsimd.tensor_scalar(out=dst, in0=s, scalar1=minus, scalar2=plus, op0=ALU.mult, op1=ALU.add)
 
         def scalar_unit(u, staged):
             for pair in ((0, 1), (2, 3)):
@@ -250,7 +255,7 @@ def tile_twotimehiddentangentkernel_x2_kernel(
                 for k in pair:
                     sigmoid(u, k)
                 for k in pair:
-                    if k in SCALAR_FACTORS[u]:
+                    if k in scalar_factors(u):
                         scalar_factor(u, k)
 
         def by_runs(slots4):
@@ -429,7 +434,6 @@ def tile_twotimehiddentangentkernel_x2_kernel(
             z_mm(5, k)
         gram_mm(0, BANKS, (1,))
         scalar_unit(5, 2)
-        pool_factor(5, 1)
         for k in (0, 1):
             z_mm(6, k)
         products(4, (0,))
@@ -438,7 +442,7 @@ def tile_twotimehiddentangentkernel_x2_kernel(
         hadamard(0, (2, 3))
         turn(Y, 3, False)
 
-        vector_factors(5, (3,))
+        vector_factors(5, BANKS)
         quant_d(4)
         scalar_unit(6, 2)
         base_mm(1, (0, 1))
@@ -456,6 +460,7 @@ def tile_twotimehiddentangentkernel_x2_kernel(
         hadamard(1, BANKS)
 
         base_mm(2, (0, 1))
+        vector_factors(7, (0, 1))
         quant_d(6)
         for pair, k in (((0, 1), 2), ((2, 3), 3)):
             gram_mm(2, pair, (0, 1))
@@ -463,9 +468,11 @@ def tile_twotimehiddentangentkernel_x2_kernel(
         base_out(2)
         base_mm(3, BANKS)
         base_out(3)
-        for part in (0, 1):
-            products(7, (part,))
-            quant_o(0, part)
+        products(7, (0,))
+        vector_factors(7, (2, 3))
+        quant_o(0, 0)
+        products(7, (1,))
+        quant_o(0, 1)
         store_words(0, 0, 2)
         quant_d(7)
 

@@ -42,6 +42,7 @@ UNITS = [
     narrow(Y, 2 * CHUNK),
     narrow(Y, 3 * CHUNK),
 ]
+FIRST_UNIT_SLOTS = [(0,), (1,), (2, 3), (4, 5), (6, 7)]
 BLOCKS = [[(0, 0), (0, 1)], [(1, 0), (1, 1)], [(0, 2), (1, 2)], [(0, 3), (1, 3)]]
 LAST_BLOCK = len(BLOCKS) - 1
 
@@ -49,9 +50,9 @@ LAST_BLOCK = len(BLOCKS) - 1
 def scalar_factors(u):
     if u < 2:
         return ()
-    if u == 6:
-        return (0, 1, 2, 3)
-    return (0, 2)
+    if u < 6:
+        return (0, 2)
+    return (0, 1, 2, 3)
 
 
 STAGE_BUFS = {CHUNK: 4, BANK: 3}
@@ -89,14 +90,16 @@ def tile_twotimehiddentangentkernel_x2_kernel(
 
         raw = {}
 
-        def load_rows(side, chunk):
-            raw[side, chunk] = keep.tile([P, 2, D], BF16, name="raw_%d%d" % (side, chunk), align_bytes=64)
+        def load_rows(side, chunk, chunks):
+            tiles = keep.tile([P, 2 * chunks, D], BF16, name="raw_%d%d" % (side, chunk), align_bytes=64)
             if side == X:
                 group = x[BANK * (chunk // 2) : BANK * (chunk // 2 + 1), :].rearrange("(p t) k -> p t k", t=4)
-                view = group[:, 2 * (chunk % 2) : 2 * (chunk % 2) + 2, :]
+                view = group[:, 2 * (chunk % 2) : 2 * (chunk % 2 + chunks), :]
             else:
-                view = y[CHUNK * chunk : CHUNK * (chunk + 1), :].rearrange("(j p) k -> p j k", j=2)
-            nc.sync.dma_start(out=raw[side, chunk][:], in_=view)
+                view = y[CHUNK * chunk : CHUNK * (chunk + chunks), :].rearrange("(j p) k -> p j k", p=P)
+            nc.sync.dma_start(out=tiles[:], in_=view)
+            for i in range(chunks):
+                raw[side, chunk + i] = tiles[:, 2 * i : 2 * i + 2, :]
 
         w_raw = [keep.tile([P, 2 * F], U8, name="w_raw%d" % side, align_bytes=64) for side in (X, Y)]
         w_perm = [keep.tile([P, 2 * F], U8, name="w_perm%d" % side, align_bytes=64) for side in (X, Y)]
@@ -118,18 +121,18 @@ def tile_twotimehiddentangentkernel_x2_kernel(
                 in_=vec.rearrange("(q r i) -> r q i", r=8, i=8),
             )
 
-        load_rows(X, 0)
+        load_rows(X, 0, 1)
         load_words(X)
         load_scales(X)
-        load_rows(X, 1)
+        load_rows(X, 1, 1)
         load_vector(b_rows, 0, b)
         load_vector(v_rows, 8 * X, va)
         load_vector(v_rows, 8 * Y, vb)
-        load_rows(Y, 0)
+        load_rows(Y, 0, 2)
         load_scales(Y)
         load_words(Y)
-        for side, chunk in ((Y, 1), (X, 2), (X, 3), (Y, 2), (Y, 3)):
-            load_rows(side, chunk)
+        for side in (X, Y):
+            load_rows(side, 2, 2)
 
         def permute(dst, src, r0, r1):
             nc.vector.tensor_copy(
@@ -191,7 +194,8 @@ def tile_twotimehiddentangentkernel_x2_kernel(
             slots = [(part, t) for part in range(len(UNITS[u])) for t in range(4)]
             each = len(UNITS[u])
             width = BANK // each
-            return [slots[each * k + i] + (slice(width * i, width * (i + 1)),) for i in range(each)]
+            chosen = FIRST_UNIT_SLOTS[k] if u == 0 else range(each * k, each * (k + 1))
+            return [slots[s] + (slice(width * i, width * (i + 1)),) for i, s in enumerate(chosen)]
 
         def z_mm(u, k):
             z = scalar_bank("z")
@@ -394,24 +398,26 @@ def tile_twotimehiddentangentkernel_x2_kernel(
         quant_in(X, 0)
         vector_out(b_bank, bias2, 2.0)
         turn_out(X, 1, False)
-        for k in (0, 1):
+        for k in (0, 1, 2):
             z_mm(0, k)
         v_bank = turn_vector(v_rows)
         permute(w_perm[X], w_raw[X], 4, 8)
         quant_in(X, 1)
         vector_out(v_bank, minus4v, -4.0)
         vector_out(v_bank, plus4v, 4.0)
-        for k in (2, 3):
-            z_mm(0, k)
-        scalar_unit(0, 4)
+        z_mm(0, 3)
+        sigmoid(0, 0)
+        z_mm(0, 4)
+        for k in (1, 2, 3, 4):
+            sigmoid(0, k)
         for chunk in (0, 1):
             turn(Y, chunk, True)
-        vector_factors(0, (0,))
+        vector_factors(0, (0, 1))
         permute(plane_perm[Y], plane_raw[Y], 0, 8)
-        vector_factors(0, (1,))
+        vector_factors(0, (2,))
         permute(w_perm[Y], w_raw[Y], 0, 8)
         products(0, (0,))
-        vector_factors(0, (2, 3))
+        vector_factors(0, (3, 4))
         quant_in(Y, 0, 2)
         products(0, (1,))
         scalar_unit(1, 0)
@@ -460,7 +466,6 @@ def tile_twotimehiddentangentkernel_x2_kernel(
         hadamard(1, BANKS)
 
         base_mm(2, (0, 1))
-        vector_factors(7, (0, 1))
         quant_d(6)
         for pair, k in (((0, 1), 2), ((2, 3), 3)):
             gram_mm(2, pair, (0, 1))
@@ -468,11 +473,9 @@ def tile_twotimehiddentangentkernel_x2_kernel(
         base_out(2)
         base_mm(3, BANKS)
         base_out(3)
-        products(7, (0,))
-        vector_factors(7, (2, 3))
-        quant_o(0, 0)
-        products(7, (1,))
-        quant_o(0, 1)
+        for part in (0, 1):
+            products(7, (part,))
+            quant_o(0, part)
         store_words(0, 0, 2)
         quant_d(7)
 

@@ -24,40 +24,15 @@ X, Y = 0, 1
 BANKS = range(4)
 
 
-def wide(side, token, g):
-    return [(side, g, token, BANK)]
-
-
-def narrow(side, token):
-    return [(side, g, token, CHUNK) for g in (0, 1)]
-
-
-UNITS = [
-    [(X, 0, 0, CHUNK), (X, 0, CHUNK, CHUNK)],
-    wide(X, 0, 1),
-    wide(Y, 0, 0),
-    wide(Y, 0, 1),
-    wide(X, BANK, 0),
-    wide(X, BANK, 1),
-    narrow(Y, 2 * CHUNK),
-    narrow(Y, 3 * CHUNK),
+UNITS = [[(X, 0, 0, CHUNK), (X, 0, CHUNK, CHUNK)], [(X, 1, 0, BANK)]] + [
+    [(side, g, token, BANK)] for side, token in ((Y, 0), (X, BANK), (Y, BANK)) for g in (0, 1)
 ]
-FIRST_UNIT_SLOTS = [(0,), (1,), (2, 3), (4, 5), (6, 7)]
-BLOCKS = [[(0, 0), (0, 1)], [(1, 0), (1, 1)], [(0, 2), (1, 2)], [(0, 3), (1, 3)]]
-LAST_BLOCK = len(BLOCKS) - 1
-
-
-def scalar_factors(u):
-    if u < 2:
-        return ()
-    if u < 6:
-        return (0, 2)
-    return (0, 1, 2, 3)
-
-
-STAGE_BUFS = {CHUNK: 4, BANK: 3}
-O16_BUFS = 5
-
+FIRST_UNIT_BANKS = [
+    [(0, t, P * j, P) for t in slots] for j, slots in ((0, (0,)), (0, (1, 2, 3)), (1, (0, 1)), (1, (2, 3)))
+] + [[(1, t, 0, CHUNK) for t in slots] for slots in ((0,), (1, 2), (3,))]
+BLOCKS = [[(0, 0), (0, 1)], [(1, 0), (1, 1)], [(0, 2), (0, 3)], [(1, 2), (1, 3)]]
+SIG_BUFS = 5
+O16_BUFS = 4
 
 def tile_twotimehiddentangentkernel_x2_kernel(
     tc, x, y, wa_words, wa_scales, wb_words, wb_scales, b, va, vb, out_0, out_1, out_2
@@ -70,10 +45,13 @@ def tile_twotimehiddentangentkernel_x2_kernel(
         ctx.enter_context(tc.manual_schedule())
 
         def scalar_bank(name):
-            return psum.tile([P, BANK], F32, name=name, tag="act", bufs=4)
+            return psum.tile([P, BANK], F32, name=name, tag="act", bufs=3)
 
         def vector_bank(name):
             return psum.tile([P, BANK], F32, name=name, tag="dve", bufs=4)
+
+        def spare_bank(name):
+            return psum.tile([P, BANK], F32, name=name, tag="spare", bufs=1)
 
         plane_raw = [keep.tile([P, F], U8, name="plane_raw%d" % side, align_bytes=64) for side in (X, Y)]
         for side in (X, Y):
@@ -123,8 +101,8 @@ def tile_twotimehiddentangentkernel_x2_kernel(
 
         load_rows(X, 0, 1)
         load_words(X)
-        load_scales(X)
         load_rows(X, 1, 1)
+        load_scales(X)
         load_vector(b_rows, 0, b)
         load_vector(v_rows, 8 * X, va)
         load_vector(v_rows, 8 * Y, vb)
@@ -140,14 +118,15 @@ def tile_twotimehiddentangentkernel_x2_kernel(
                 in_=src[:].bitcast(I32).rearrange("p (q r i) -> p r q i", r=8, q=16)[:, r0:r1, :, :],
             )
 
+        minus_rows = keep.tile([P, P], BF16, name="minus_rows", align_bytes=64)
         turned = {}
         grouped = [keep.tile([P, 4 * N], BF16, name="grouped%d" % side, align_bytes=64) for side in (X, Y)]
         codes = [keep.tile([P, N], U32, name="codes%d" % side, align_bytes=64) for side in (X, Y)]
         planes = [keep.tile([P, N], U8, name="planes%d" % side, align_bytes=64) for side in (X, Y)]
 
-        def transposes(side, chunk, bank):
+        def transposes(side, chunk, bank, tiles=(0, 1)):
             turned[side, chunk] = bank
-            for j in (0, 1):
+            for j in tiles:
                 pairs = raw[side, chunk][:, j, :].bitcast(F32)
                 for u in (0, 1):
                     col = P * (2 * j + u)
@@ -161,6 +140,26 @@ def tile_twotimehiddentangentkernel_x2_kernel(
                 nc.scalar.copy(out=dst, in_=src)
             else:
                 nc.vector.tensor_copy(out=dst, in_=src)
+
+        def first_tile(j):
+            bank = vector_bank("turn")
+            pairs = raw[X, 0][:, j, :].bitcast(F32)
+            for u in (0, 1):
+                nc.tensor.transpose(bank[:, P * u : P * (u + 1)], pairs[:, u : D // 2 : 2], ident[:])
+            return bank
+
+        def first_tile_out(j, bank):
+            pairs = grouped[X][:, 4 * P * j : 4 * P * (j + 1)].bitcast(F32)
+            nc.vector.tensor_copy(
+                out=pairs.rearrange("p (r u) -> p r u", u=2), in_=bank[:, 0 : 2 * P].rearrange("p (u r) -> p r u", u=2)
+            )
+
+        def first_tile_quant(j):
+            nc.vector.quantize_mx(
+                out=codes[X][:, P * j : P * (j + 1)].bitcast(FP8X4),
+                scales=planes[X][:, P * j : P * (j + 1)],
+                in_=grouped[X][:, 4 * P * j : 4 * P * (j + 1)],
+            )
 
         def turn(side, chunk, on_scalar):
             transposes(side, chunk, (scalar_bank if on_scalar else vector_bank)("turn"))
@@ -178,8 +177,8 @@ def tile_twotimehiddentangentkernel_x2_kernel(
         minus4v = keep.tile([P, 16], F32, name="minus4v")
         plus4v = keep.tile([P, 16], F32, name="plus4v")
 
-        def turn_vector(rows):
-            bank = psum.tile([P, 2 * BANK], BF16, name="vbank", tag="dve", bufs=4)
+        def turn_vector(rows, tag, bufs):
+            bank = psum.tile([P, 2 * BANK], BF16, name="vbank", tag=tag, bufs=bufs)
             nc.tensor.transpose(bank[:, 0:P], rows[:], ident16[:])
             return bank
 
@@ -188,79 +187,62 @@ def tile_twotimehiddentangentkernel_x2_kernel(
                 out=dst[:], in0=bank[:, 0 : dst.shape[1]], scalar1=times, scalar2=None, op0=ALU.mult
             )
 
-        z_banks, sig, fac, d16, d_codes, d_planes, d_at = {}, {}, {}, {}, {}, {}, {}
+        z_banks, sig, fac, squares, d16, d_codes, d_planes, d_at = {}, {}, {}, {}, {}, {}, {}, {}
 
         def slots_in_bank(u, k):
-            slots = [(part, t) for part in range(len(UNITS[u])) for t in range(4)]
-            each = len(UNITS[u])
-            width = BANK // each
-            chosen = FIRST_UNIT_SLOTS[k] if u == 0 else range(each * k, each * (k + 1))
-            return [slots[s] + (slice(width * i, width * (i + 1)),) for i, s in enumerate(chosen)]
+            chosen = FIRST_UNIT_BANKS[k] if u == 0 else [(0, k, 0, BANK)]
+            return [(part, t, slice(c, c + w), slice(w * i, w * (i + 1))) for i, (part, t, c, w) in enumerate(chosen)]
 
-        def z_mm(u, k):
-            z = scalar_bank("z")
-            z_banks[u, k] = z
-            for part, t, at in slots_in_bank(u, k):
-                side, g, token, width = UNITS[u][part]
-                r = 4 * g + t
-                nc.tensor.matmul_mx(
-                    out=z[:, at],
-                    lhsT=w_perm[side][:, 2 * P * r : 2 * P * (r + 1)].bitcast(FP4X4),
-                    lhsT_scale=plane_perm[side][:, P * r : P * (r + 1)],
-                    rhs=codes[side][:, token : token + width].bitcast(FP8X4),
-                    rhs_scale=planes[side][:, token : token + width],
-                    start=True,
-                    stop=True,
-                )
+        def planes_of(tile, u, part):
+            width = UNITS[u][part][3]
+            return tile[:, 4 * width * part : 4 * width * (part + 1)].rearrange("p (t n) -> p t n", t=4)
 
-        def sigmoid(u, k):
-            for part, t, at in slots_in_bank(u, k):
-                side, g, token, width = UNITS[u][part]
-                if t == 0:
-                    bufs = STAGE_BUFS[width]
-                    sig[u, part] = work.tile(
-                        [P, 4, width], F32, name="sig", tag="sig%d" % width, bufs=bufs, align_bytes=64
-                    )
-                    tag, bufs = ("relay6", 1) if (u, part) == (6, 1) else ("fac%d" % width, bufs)
-                    fac[u, part] = work.tile([P, 4, width], F32, name="fac", tag=tag, bufs=bufs, align_bytes=64)
-                r = 4 * g + t
-                nc.scalar.activation(
-                    out=sig[u, part][:, t, :], in_=z_banks[u, k][:, at], func=ACT.Sigmoid,
-                    bias=bias2[:, r : r + 1], scale=2.0,
-                )
-
-        def factor_operands(u, k):
-            for_bank = []
-            for part, t, at in slots_in_bank(u, k):
-                side, g, token, width = UNITS[u][part]
-                c = 8 * side + 4 * g + t
-                for_bank.append(
-                    (fac[u, part][:, t, :], sig[u, part][:, t, :], minus4v[:, c : c + 1], plus4v[:, c : c + 1])
-                )
-            return for_bank
-
-        def scalar_factor(u, k):
-            for dst, s, minus, plus in factor_operands(u, k):
-                nc.scalar.activation(out=dst, in_=s, func=ACT.Identity, bias=plus, scale=minus)
-
-        def vector_factors(u, banks):
+        def z_mm(u, banks, bank=scalar_bank):
             for k in banks:
-                if k not in scalar_factors(u):
-                    for dst, s, minus, plus in factor_operands(u, k):
-                        nc.vector.tensor_scalar(
-                            out=dst, in0=s, scalar1=1.0, scalar2=minus, op0=ALU.subtract, op1=ALU.mult
-                        )
+                z = bank("z")
+                z_banks[u, k] = z
+                for part, t, cols, at in slots_in_bank(u, k):
+                    side, g, token, width = UNITS[u][part]
+                    tokens = slice(token + cols.start, token + cols.stop)
+                    r = 4 * g + t
+                    nc.tensor.matmul_mx(
+                        out=z[:, at],
+                        lhsT=w_perm[side][:, 2 * P * r : 2 * P * (r + 1)].bitcast(FP4X4),
+                        lhsT_scale=plane_perm[side][:, P * r : P * (r + 1)],
+                        rhs=codes[side][:, tokens].bitcast(FP8X4),
+                        rhs_scale=planes[side][:, tokens],
+                        start=True,
+                        stop=True,
+                    )
 
-        def scalar_unit(u, staged):
-            for pair in ((0, 1), (2, 3)):
-                for k in pair:
-                    if k >= staged:
-                        z_mm(u, k)
-                for k in pair:
-                    sigmoid(u, k)
-                for k in pair:
-                    if k in scalar_factors(u):
-                        scalar_factor(u, k)
+        def sigmoid(u, banks):
+            for k in banks:
+                if k == 0:
+                    sig[u] = work.tile([P, 4 * BANK], F32, name="sig", tag="sig", bufs=SIG_BUFS, align_bytes=64)
+                for part, t, cols, at in slots_in_bank(u, k):
+                    r = 4 * UNITS[u][part][1] + t
+                    nc.scalar.activation(
+                        out=planes_of(sig[u], u, part)[:, t, cols], in_=z_banks[u, k][:, at], func=ACT.Sigmoid,
+                        bias=bias2[:, r : r + 1], scale=2.0,
+                    )
+
+        def stage(u, staged=0):
+            for k in BANKS:
+                if k >= staged:
+                    z_mm(u, (k,))
+                sigmoid(u, (k,))
+
+        def factor(engine, u, part, slots):
+            side, g, token, width = UNITS[u][part]
+            if u not in fac:
+                tag = "relay%d" % (u - 2) if u in (5, 7) else "fac%d" % min(u, 1)
+                fac[u] = work.tile([P, 4 * BANK], F32, name="fac", tag=tag, bufs=1, align_bytes=64)
+            for t in slots:
+                c = 8 * side + 4 * g + t
+                engine.tensor_scalar(
+                    out=planes_of(fac[u], u, part)[:, t, :], in0=planes_of(sig[u], u, part)[:, t, :],
+                    scalar1=minus4v[:, c : c + 1], scalar2=plus4v[:, c : c + 1], op0=ALU.mult, op1=ALU.add,
+                )
 
         def by_runs(slots4):
             return slots4.rearrange("p t (c i) -> p c t i", i=RUN)
@@ -268,29 +250,50 @@ def tile_twotimehiddentangentkernel_x2_kernel(
         def into_words(tile16):
             return tile16.rearrange("p (c i) t -> p c t i", i=RUN)
 
-        def products(u, parts):
-            for part in parts:
-                width = UNITS[u][part][3]
-                if part == 0:
-                    tag, bufs = ("relay7", 1) if u == 7 else ("d16", 2)
-                    d16[u] = work.tile([P, BANK, 4], BF16, name="d16", tag=tag, bufs=bufs, align_bytes=64)
-                nc.vector.tensor_tensor(
-                    out=into_words(d16[u][:, width * part : width * (part + 1), :]),
-                    in0=by_runs(sig[u, part][:]),
-                    in1=by_runs(fac[u, part][:]),
-                    op=ALU.mult,
-                )
+        def square(u):
+            squares[u] = work.tile([P, BANK, 4], F32, name="square", tag="sig", bufs=SIG_BUFS, align_bytes=64)
+            nc.scalar.activation(
+                out=into_words(squares[u][:]), in_=by_runs(planes_of(sig[u], u, 0)), func=ACT.Square,
+                bias=-1.0, scale=2.0,
+            )
 
-        def quant_d(u):
-            d_codes[u] = keep.tile([P, BANK], U32, name="d_codes%d" % u, align_bytes=64)
-            d_planes[u] = keep.tile([P, BANK], U8, name="d_planes%d" % u, align_bytes=64)
+        def new_d16(u):
+            tag, bufs = ("relay%d" % u, 1) if u in (3, 5) else ("d16", 3)
+            d16[u] = work.tile([P, BANK, 4], BF16, name="d16", tag=tag, bufs=bufs, align_bytes=64)
+
+        def product(u, part=0):
+            width = UNITS[u][part][3]
+            if part == 0:
+                new_d16(u)
+            nc.vector.tensor_tensor(
+                out=into_words(d16[u][:, width * part : width * (part + 1), :]),
+                in0=by_runs(planes_of(sig[u], u, part)),
+                in1=by_runs(planes_of(fac[u], u, part)),
+                op=ALU.mult,
+            )
+
+        def product_of_square(u, minus_v):
+            side, g, token, width = UNITS[u][0]
+            c = 8 * side + 4 * g
+            new_d16(u)
+            nc.vector.scalar_tensor_tensor(
+                out=d16[u][:], in0=squares[u][:], scalar=1.0,
+                in1=minus_v[:, c : c + 4].unsqueeze(1).to_broadcast([P, BANK, 4]),
+                op0=ALU.subtract, op1=ALU.mult,
+            )
+
+        def quant_d(u, halves=(0, 1)):
+            if u not in d_codes:
+                d_codes[u] = keep.tile([P, BANK], U32, name="d_codes%d" % u, align_bytes=64)
+                d_planes[u] = keep.tile([P, BANK], U8, name="d_planes%d" % u, align_bytes=64)
+            cols = slice(CHUNK * halves[0], CHUNK * (halves[-1] + 1))
             for part, (side, g, token, width) in enumerate(UNITS[u]):
                 for step in range(0, width, P):
                     d_at[side, g, token + step] = (u, width * part + step)
             nc.vector.quantize_mx(
-                out=d_codes[u][:].bitcast(FP8X4),
-                scales=d_planes[u][:],
-                in_=d16[u][:].rearrange("p n t -> p (n t)"),
+                out=d_codes[u][:, cols].bitcast(FP8X4),
+                scales=d_planes[u][:, cols],
+                in_=d16[u][:, cols, :].rearrange("p n t -> p (n t)"),
             )
 
         base_banks, gram_banks, base_sb, o32, o16 = {}, {}, {}, {}, {}
@@ -302,9 +305,9 @@ def tile_twotimehiddentangentkernel_x2_kernel(
             h, j = BLOCKS[n][k // 2]
             return [(h, 2 * (k % 2) + i, j, chunk_cols(i)) for i in (0, 1)]
 
-        def base_mm(n, banks):
+        def base_mm(n, banks, bank=scalar_bank):
             for k in banks:
-                base_banks[n, k] = scalar_bank("base")
+                base_banks[n, k] = bank("base")
                 for h, t, j, at in tiles_in_bank(n, k):
                     rows = slice(BANK * h + P * t, BANK * h + P * (t + 1))
                     nc.tensor.matmul_mx(
@@ -317,16 +320,16 @@ def tile_twotimehiddentangentkernel_x2_kernel(
                         stop=True,
                     )
 
-        def base_out(n):
-            for k in BANKS:
+        def base_out(n, banks):
+            for k in banks:
                 base_sb[n, k] = work.tile([P, BANK], F32, name="base_sb", tag="base_sb", bufs=8, align_bytes=64)
                 nc.scalar.activation(out=base_sb[n, k][:], in_=base_banks[n, k][:], func=ACT.Copy, scale=SCALE)
 
-        def gram_mm(n, banks, passes):
+        def gram_mm(n, banks, passes, bank=vector_bank):
             for k in banks:
                 for g in passes:
                     if g == 0:
-                        gram_banks[n, k] = (scalar_bank if n == LAST_BLOCK else vector_bank)("gram")
+                        gram_banks[n, k] = bank("gram")
                     for i, (h, t, j, at) in enumerate(tiles_in_bank(n, k)):
                         ux, cx = d_at[X, g, BANK * h + P * t]
                         uy, cy = d_at[Y, g, CHUNK * j]
@@ -354,11 +357,13 @@ def tile_twotimehiddentangentkernel_x2_kernel(
                 nc.sync.dma_start(out=rows[:, t0 : t0 + 2, :], in_=pair)
 
         def scalar_cast(h, j):
-            o16[h, j] = work.tile([P, CHUNK, 4], BF16, name="o16", tag="o16", bufs=O16_BUFS, align_bytes=64)
+            if (h, j) not in o16:
+                o16[h, j] = work.tile([P, CHUNK, 4], BF16, name="o16", tag="o16", bufs=O16_BUFS, align_bytes=64)
             nc.scalar.copy(out=into_words(o16[h, j][:]), in_=by_runs(o32[h, j][:]))
 
         def pool_cast(h, j, tag="o16", bufs=O16_BUFS):
-            o16[h, j] = work.tile([P, CHUNK, 4], BF16, name="o16", tag=tag, bufs=bufs, align_bytes=64)
+            if (h, j) not in o16:
+                o16[h, j] = work.tile([P, CHUNK, 4], BF16, name="o16", tag=tag, bufs=bufs, align_bytes=64)
             nc.gpsimd.tensor_scalar(
                 out=o16[h, j][:], in0=o32[h, j][:].rearrange("p t c -> p c t"),
                 scalar1=1.0, scalar2=0.0, op0=ALU.mult, op1=ALU.add,
@@ -367,11 +372,17 @@ def tile_twotimehiddentangentkernel_x2_kernel(
         o_codes = keep.tile([P, 2, M], U32, name="o_codes", align_bytes=64)
         o_planes = keep.tile([P, 2, M], U8, name="o_planes", align_bytes=64)
 
-        def quant_o(h, j):
+        def pair_tile(h, j, tag):
+            o16[h, j, 2] = work.tile([P, 2 * CHUNK, 4], BF16, name="o16pair", tag=tag, bufs=1, align_bytes=64)
+            for i in (0, 1):
+                o16[h, j + i] = o16[h, j, 2][:, chunk_cols(i), :]
+
+        def quant_o(h, j, pieces=1):
+            cols = slice(CHUNK * j, CHUNK * (j + pieces))
             nc.vector.quantize_mx(
-                out=o_codes[:, h, chunk_cols(j)].bitcast(FP8X4),
-                scales=o_planes[:, h, chunk_cols(j)],
-                in_=o16[h, j][:].rearrange("p n t -> p (n t)"),
+                out=o_codes[:, h, cols].bitcast(FP8X4),
+                scales=o_planes[:, h, cols],
+                in_=(o16[h, j] if pieces == 1 else o16[h, j, 2])[:].rearrange("p n t -> p (n t)"),
             )
 
         def store_words(h, j0, j1):
@@ -388,114 +399,142 @@ def tile_twotimehiddentangentkernel_x2_kernel(
                     in_=o_planes[32 * quad : 32 * quad + 4, :, :].bitcast(I32),
                 )
 
-
-        for chunk in (0, 1):
-            transposes(X, chunk, vector_bank("turn"))
-        b_bank = turn_vector(b_rows)
+        tile_banks = [first_tile(j) for j in (0, 1)]
+        second_bank = vector_bank("turn")
+        transposes(X, 1, second_bank, (0,))
+        b_bank = turn_vector(b_rows, "dve", 4)
+        transposes(X, 1, second_bank, (1,))
+        first_tile_out(0, tile_banks[0])
         permute(w_perm[X], w_raw[X], 0, 4)
-        turn_out(X, 0, False)
+        first_tile_quant(0)
+        first_tile_out(1, tile_banks[1])
         permute(plane_perm[X], plane_raw[X], 0, 8)
-        quant_in(X, 0)
+        first_tile_quant(1)
         vector_out(b_bank, bias2, 2.0)
         turn_out(X, 1, False)
-        for k in (0, 1, 2):
-            z_mm(0, k)
-        v_bank = turn_vector(v_rows)
+        z_mm(0, (0, 1, 2))
+        z_mm(0, (3,), spare_bank)
+        v_bank = turn_vector(v_rows, "dve", 4)
         permute(w_perm[X], w_raw[X], 4, 8)
         quant_in(X, 1)
+        nc.vector.tensor_scalar(out=minus_rows[:], in0=v_rows[:], scalar1=-1.0, scalar2=None, op0=ALU.mult)
         vector_out(v_bank, minus4v, -4.0)
         vector_out(v_bank, plus4v, 4.0)
-        z_mm(0, 3)
-        sigmoid(0, 0)
-        z_mm(0, 4)
-        for k in (1, 2, 3, 4):
-            sigmoid(0, k)
+        for k in (0, 1, 2):
+            sigmoid(0, (k,))
+            z_mm(0, (4 + k,))
+        sigmoid(0, (3, 4, 5, 6))
         for chunk in (0, 1):
-            turn(Y, chunk, True)
-        vector_factors(0, (0, 1))
+            transposes(Y, chunk, vector_bank("turn"))
+            turn_out(Y, chunk, True)
+        factor(nc.vector, 0, 0, (0, 1))
         permute(plane_perm[Y], plane_raw[Y], 0, 8)
-        vector_factors(0, (2,))
+        factor(nc.vector, 0, 0, (2, 3))
         permute(w_perm[Y], w_raw[Y], 0, 8)
-        products(0, (0,))
-        vector_factors(0, (3, 4))
+        product(0, 0)
+        factor(nc.vector, 0, 1, (0, 1, 2, 3))
         quant_in(Y, 0, 2)
-        products(0, (1,))
-        scalar_unit(1, 0)
+        product(0, 1)
+        z_mm(1, (0, 1, 2))
+        transposes(X, 2, vector_bank("turn"))
+        stage(1, 3)
+        transposes(X, 3, vector_bank("turn"))
+        z_mm(2, (0, 1, 2))
+        transposes(Y, 2, vector_bank("turn"))
+        minus_v = turn_vector(minus_rows, "spare", 1)
+        stage(2, 3)
+        z_mm(3, (0,))
+        transposes(Y, 3, vector_bank("turn"))
+        factor(nc.vector, 1, 0, (0, 1, 2, 3))
+        for chunk in (2, 3):
+            turn_out(X, chunk, False)
+        quant_d(0)
+        quant_in(X, 2, 2)
+        product(1)
 
-        for u, (side, chunk) in zip((1, 2, 3), ((X, 2), (X, 3), (Y, 2))):
-            turn(side, chunk, True)
-            vector_factors(u, BANKS)
-            quant_d(u - 1)
-            quant_in(side, chunk)
-            scalar_unit(u + 1, 0)
-            if u == 3:
-                base_mm(0, BANKS)
-                gram_mm(0, BANKS, (0,))
-            products(u, (0,))
-
-        base_out(0)
-        vector_factors(4, BANKS)
+        sigmoid(3, (0,))
+        square(2)
+        for k in (1, 2, 3):
+            z_mm(3, (k,))
+        sigmoid(3, (1, 2, 3))
+        factor(nc.gpsimd, 3, 0, (0, 1, 2, 3))
+        product_of_square(2, minus_v)
+        for chunk in (2, 3):
+            turn_out(Y, chunk, False)
+        quant_d(1)
+        quant_d(2)
+        stage(4)
+        z_mm(5, (0, 1, 2))
+        gram_mm(0, BANKS, (0,))
+        product(3)
+        quant_in(Y, 2, 2)
         quant_d(3)
-        for k in (0, 1):
-            z_mm(5, k)
-        gram_mm(0, BANKS, (1,))
-        scalar_unit(5, 2)
-        for k in (0, 1):
-            z_mm(6, k)
-        products(4, (0,))
-        hadamard(0, (0, 1))
-        pool_cast(0, 0)
-        hadamard(0, (2, 3))
-        turn(Y, 3, False)
 
-        vector_factors(5, BANKS)
-        quant_d(4)
-        scalar_unit(6, 2)
-        base_mm(1, (0, 1))
+        def window(n, u, casts, passes):
+            sigmoid(u + 1, (0,))
+            base_mm(n, (0,))
+            square(u)
+            sigmoid(u + 1, (1,))
+            base_mm(n, (1,))
+            sigmoid(u + 1, (2,))
+            z_mm(u + 1, (3,))
+            gram_mm(n, (0, 1), passes)
+            base_out(n, (0,))
+            base_mm(n, (2,))
+            base_out(n, (1,))
+            base_mm(n, (3,))
+            gram_mm(n, (2, 3), passes)
+            sigmoid(u + 1, (3,))
+            base_out(n, (2, 3))
+            factor(nc.gpsimd, u + 1, 0, (0,))
+            for piece in casts:
+                pool_cast(*piece)
+            factor(nc.gpsimd, u + 1, 0, (1, 2, 3))
+            product_of_square(u, minus_v)
+            hadamard(n, BANKS)
+
+        window(0, 4, (), (1,))
+        stage(6)
+        z_mm(7, (0, 1, 2))
+        quant_d(4, (0,))
+        product(5)
+        quant_d(4, (1,))
         gram_mm(1, BANKS, (0,))
-        products(5, (0,))
-
-        base_mm(1, (2, 3))
-        base_out(1)
-        quant_in(Y, 3)
         quant_d(5)
-        gram_mm(1, BANKS, (1,))
-        scalar_unit(7, 0)
-        products(6, (0, 1))
-        pool_cast(0, 1, "relay6", 1)
-        hadamard(1, BANKS)
-
-        base_mm(2, (0, 1))
+        window(1, 6, ((0, 0),), (1,))
         quant_d(6)
-        for pair, k in (((0, 1), 2), ((2, 3), 3)):
-            gram_mm(2, pair, (0, 1))
-            base_mm(2, (k,))
-        base_out(2)
-        base_mm(3, BANKS)
-        base_out(3)
-        for part in (0, 1):
-            products(7, (part,))
-            quant_o(0, part)
+        base_mm(2, (0, 1, 2))
+        base_mm(2, (3,), spare_bank)
+        base_out(2, BANKS)
+        o16[0, 1] = work.tile([P, CHUNK, 4], BF16, name="o16", tag="relay7", bufs=1, align_bytes=64)
+        scalar_cast(0, 1)
+        base_mm(3, (0, 1))
+        gram_mm(2, BANKS, (0,))
+        base_mm(3, (2,))
+        base_mm(3, (3,), spare_bank)
+        base_out(3, BANKS)
+        product(7)
+        quant_o(0, 0)
+        for half in (0, 1):
+            quant_d(7, (half,))
+        quant_o(0, 1)
         store_words(0, 0, 2)
-        quant_d(7)
-
-        pool_cast(1, 0, "relay7", 1)
+        pair_tile(1, 0, "relay7")
+        pair_tile(0, 2, "pair")
+        pool_cast(1, 0)
         pool_cast(1, 1)
-        for k in BANKS:
-            gram_mm(3, (k,), (0, 1))
-            hadamard(2, (k,))
-            if k == 1:
-                pool_cast(0, 2)
-        scalar_cast(1, 2)
-        hadamard(3, BANKS)
-        for h in (0, 1):
-            scalar_cast(h, 3)
-        for j in range(3):
-            quant_o(1, j)
-        store_words(1, 0, 3)
-        for j in (2, 3):
-            quant_o(0, j)
+        gram_mm(2, BANKS, (1,))
+        gram_mm(3, (0, 1, 2), (0, 1), scalar_bank)
+        gram_mm(3, (3,), (0, 1), spare_bank)
+        for n in (2, 3):
+            for half in (0, 1):
+                hadamard(n, (2 * half, 2 * half + 1))
+                scalar_cast(*BLOCKS[n][half])
+        quant_o(1, 0, 2)
+        quant_o(0, 2, 2)
         store_words(0, 2, 4)
+        quant_o(1, 2)
+        store_words(1, 0, 3)
         quant_o(1, 3)
         store_words(1, 3, 4)
         store_scales()

@@ -438,13 +438,13 @@ def tile_twotimehiddentangentkernel_x2_kernel(
         z_mm(1, (0, 1, 2))
         transposes(X, 2, vector_bank("turn"))
         stage(1, 3)
-        transposes(X, 3, vector_bank("turn"))
-        z_mm(2, (0, 1, 2))
-        transposes(Y, 2, vector_bank("turn"))
         minus_v = turn_vector(minus_rows, "spare", 1)
-        stage(2, 3)
-        z_mm(3, (0,))
-        transposes(Y, 3, vector_bank("turn"))
+        z_mm(2, (0, 1))
+        transposes(X, 3, vector_bank("turn"))
+        stage(2, 2)
+        z_mm(3, (0, 1, 2))
+        for chunk in (2, 3):
+            transposes(Y, chunk, vector_bank("turn"))
         factor(nc.vector, 1, 0, (0, 1, 2, 3))
         for chunk in (2, 3):
             turn_out(X, chunk, False)
@@ -454,14 +454,14 @@ def tile_twotimehiddentangentkernel_x2_kernel(
 
         sigmoid(3, (0,))
         square(2)
-        for k in (1, 2, 3):
-            z_mm(3, (k,))
+        z_mm(3, (3,))
         sigmoid(3, (1, 2, 3))
-        factor(nc.gpsimd, 3, 0, (0, 1, 2, 3))
+        factor(nc.gpsimd, 3, 0, (0, 1, 2))
         product_of_square(2, minus_v)
         for chunk in (2, 3):
             turn_out(Y, chunk, False)
         quant_d(1)
+        factor(nc.vector, 3, 0, (3,))
         quant_d(2)
         stage(4)
         z_mm(5, (0, 1, 2))
@@ -470,20 +470,21 @@ def tile_twotimehiddentangentkernel_x2_kernel(
         quant_in(Y, 2, 2)
         quant_d(3)
 
-        def window(n, u, casts, passes):
+        def window(n, u, casts, late):
             sigmoid(u + 1, (0,))
             base_mm(n, (0,))
+            gram_mm(n, late, (0,))
             square(u)
             sigmoid(u + 1, (1,))
             base_mm(n, (1,))
             sigmoid(u + 1, (2,))
             z_mm(u + 1, (3,))
-            gram_mm(n, (0, 1), passes)
+            gram_mm(n, (0, 1), (1,))
             base_out(n, (0,))
             base_mm(n, (2,))
             base_out(n, (1,))
             base_mm(n, (3,))
-            gram_mm(n, (2, 3), passes)
+            gram_mm(n, (2, 3), (1,))
             sigmoid(u + 1, (3,))
             base_out(n, (2, 3))
             factor(nc.gpsimd, u + 1, 0, (0,))
@@ -493,19 +494,20 @@ def tile_twotimehiddentangentkernel_x2_kernel(
             product_of_square(u, minus_v)
             hadamard(n, BANKS)
 
-        window(0, 4, (), (1,))
+        window(0, 4, (), ())
         stage(6)
         z_mm(7, (0, 1, 2))
         quant_d(4, (0,))
+        gram_mm(1, (0, 2), (0,))
         product(5)
         quant_d(4, (1,))
-        gram_mm(1, BANKS, (0,))
         quant_d(5)
-        window(1, 6, ((0, 0),), (1,))
+        window(1, 6, (), (1, 3))
         quant_d(6)
         base_mm(2, (0, 1, 2))
         base_mm(2, (3,), spare_bank)
         base_out(2, BANKS)
+        scalar_cast(0, 0)
         o16[0, 1] = work.tile([P, CHUNK, 4], BF16, name="o16", tag="relay7", bufs=1, align_bytes=64)
         scalar_cast(0, 1)
         base_mm(3, (0, 1))

@@ -25,14 +25,14 @@ BANKS = range(4)
 
 
 UNITS = [[(X, 0, 0, CHUNK), (X, 0, CHUNK, CHUNK)], [(X, 1, 0, BANK)]] + [
-    [(side, g, token, BANK)] for side, token in ((Y, 0), (X, BANK), (Y, BANK)) for g in (0, 1)
-]
+    [(side, g, token, BANK)] for side, token in ((Y, 0), (X, BANK)) for g in (0, 1)
+] + [[(Y, g, CHUNK * chunk, CHUNK) for g in (0, 1)] for chunk in (2, 3)]
 FIRST_UNIT_BANKS = [
     [(0, t, P * j, P) for t in slots] for j, slots in ((0, (0,)), (0, (1, 2, 3)), (1, (0, 1)), (1, (2, 3)))
 ] + [[(1, t, 0, CHUNK) for t in slots] for slots in ((0,), (1, 2), (3,))]
-BLOCKS = [[(0, 0), (0, 1)], [(1, 0), (1, 1)], [(0, 2), (0, 3)], [(1, 2), (1, 3)]]
-SIG_BUFS = 5
-O16_BUFS = 4
+BLOCKS = [[(0, 0), (0, 1)], [(1, 0), (1, 1)], [(0, 2), (1, 2)], [(0, 3), (1, 3)]]
+SIG_BUFS = 4
+O16_BUFS = 3
 
 def tile_twotimehiddentangentkernel_x2_kernel(
     tc, x, y, wa_words, wa_scales, wb_words, wb_scales, b, va, vb, out_0, out_1, out_2
@@ -190,12 +190,13 @@ def tile_twotimehiddentangentkernel_x2_kernel(
         z_banks, sig, fac, squares, d16, d_codes, d_planes, d_at = {}, {}, {}, {}, {}, {}, {}, {}
 
         def slots_in_bank(u, k):
-            chosen = FIRST_UNIT_BANKS[k] if u == 0 else [(0, k, 0, BANK)]
+            each = len(UNITS[u])
+            chosen = FIRST_UNIT_BANKS[k] if u == 0 else [divmod(s, 4) + (0, BANK // each) for s in range(each * k, each * (k + 1))]
             return [(part, t, slice(c, c + w), slice(w * i, w * (i + 1))) for i, (part, t, c, w) in enumerate(chosen)]
 
         def planes_of(tile, u, part):
             width = UNITS[u][part][3]
-            return tile[:, 4 * width * part : 4 * width * (part + 1)].rearrange("p (t n) -> p t n", t=4)
+            return tile[:].rearrange("p (t n) -> p t n", t=4)[:, :, width * part : width * (part + 1)]
 
         def z_mm(u, banks, bank=scalar_bank):
             for k in banks:
@@ -232,11 +233,32 @@ def tile_twotimehiddentangentkernel_x2_kernel(
                     z_mm(u, (k,))
                 sigmoid(u, (k,))
 
+        def factor_tile(u):
+            if u not in fac:
+                tag, bufs = ("fac4", 1) if u in (4, 5) else ("fac", 2)
+                fac[u] = work.tile([P, 4 * BANK], F32, name="fac", tag=tag, bufs=bufs, align_bytes=64)
+
+        def scalar_factor(u, t, part=0):
+            side, g, token, width = UNITS[u][part]
+            factor_tile(u)
+            c = 8 * side + 4 * g + t
+            nc.scalar.activation(
+                out=planes_of(fac[u], u, part)[:, t, :], in_=planes_of(sig[u], u, part)[:, t, :], func=ACT.Identity,
+                bias=plus4v[:, c : c + 1], scale=minus4v[:, c : c + 1],
+            )
+
+        def shared_stage(u, scalar_slots):
+            for pair in ((0, 1), (2, 3)):
+                for k in pair:
+                    z_mm(u, (k,), spare_bank if k == 3 else scalar_bank)
+                sigmoid(u, pair)
+                for t in pair:
+                    if t in scalar_slots:
+                        scalar_factor(u, t)
+
         def factor(engine, u, part, slots):
             side, g, token, width = UNITS[u][part]
-            if u not in fac:
-                tag = "relay%d" % (u - 2) if u in (5, 7) else "fac%d" % min(u, 1)
-                fac[u] = work.tile([P, 4 * BANK], F32, name="fac", tag=tag, bufs=1, align_bytes=64)
+            factor_tile(u)
             for t in slots:
                 c = 8 * side + 4 * g + t
                 engine.tensor_scalar(
@@ -250,15 +272,17 @@ def tile_twotimehiddentangentkernel_x2_kernel(
         def into_words(tile16):
             return tile16.rearrange("p (c i) t -> p c t i", i=RUN)
 
-        def square(u):
-            squares[u] = work.tile([P, BANK, 4], F32, name="square", tag="sig", bufs=SIG_BUFS, align_bytes=64)
+        def square(u, part):
+            width = UNITS[u][part][3]
+            if part == 0:
+                squares[u] = work.tile([P, BANK, 4], F32, name="square", tag="square", bufs=2, align_bytes=64)
             nc.scalar.activation(
-                out=into_words(squares[u][:]), in_=by_runs(planes_of(sig[u], u, 0)), func=ACT.Square,
-                bias=-1.0, scale=2.0,
+                out=into_words(squares[u][:, width * part : width * (part + 1), :]),
+                in_=by_runs(planes_of(sig[u], u, part)), func=ACT.Square, bias=-1.0, scale=2.0,
             )
 
         def new_d16(u):
-            tag, bufs = ("relay%d" % u, 1) if u in (3, 5) else ("d16", 3)
+            tag, bufs = ("relay%d" % u, 1) if u in (5, 7) else ("d16", 2)
             d16[u] = work.tile([P, BANK, 4], BF16, name="d16", tag=tag, bufs=bufs, align_bytes=64)
 
         def product(u, part=0):
@@ -273,27 +297,26 @@ def tile_twotimehiddentangentkernel_x2_kernel(
             )
 
         def product_of_square(u, minus_v):
-            side, g, token, width = UNITS[u][0]
-            c = 8 * side + 4 * g
             new_d16(u)
-            nc.vector.scalar_tensor_tensor(
-                out=d16[u][:], in0=squares[u][:], scalar=1.0,
-                in1=minus_v[:, c : c + 4].unsqueeze(1).to_broadcast([P, BANK, 4]),
+            for part, (side, g, token, width) in enumerate(UNITS[u]):
+              c = 8 * side + 4 * g
+              cols = slice(width * part, width * (part + 1))
+              nc.vector.scalar_tensor_tensor(
+                out=d16[u][:, cols, :], in0=squares[u][:, cols, :], scalar=1.0,
+                in1=minus_v[:, c : c + 4].unsqueeze(1).to_broadcast([P, width, 4]),
                 op0=ALU.subtract, op1=ALU.mult,
             )
 
-        def quant_d(u, halves=(0, 1)):
-            if u not in d_codes:
-                d_codes[u] = keep.tile([P, BANK], U32, name="d_codes%d" % u, align_bytes=64)
-                d_planes[u] = keep.tile([P, BANK], U8, name="d_planes%d" % u, align_bytes=64)
-            cols = slice(CHUNK * halves[0], CHUNK * (halves[-1] + 1))
+        def quant_d(u):
+            d_codes[u] = keep.tile([P, BANK], U32, name="d_codes%d" % u, align_bytes=64)
+            d_planes[u] = keep.tile([P, BANK], U8, name="d_planes%d" % u, align_bytes=64)
             for part, (side, g, token, width) in enumerate(UNITS[u]):
                 for step in range(0, width, P):
                     d_at[side, g, token + step] = (u, width * part + step)
             nc.vector.quantize_mx(
-                out=d_codes[u][:, cols].bitcast(FP8X4),
-                scales=d_planes[u][:, cols],
-                in_=d16[u][:, cols, :].rearrange("p n t -> p (n t)"),
+                out=d_codes[u][:].bitcast(FP8X4),
+                scales=d_planes[u][:],
+                in_=d16[u][:].rearrange("p n t -> p (n t)"),
             )
 
         base_banks, gram_banks, base_sb, o32, o16 = {}, {}, {}, {}, {}
@@ -348,7 +371,7 @@ def tile_twotimehiddentangentkernel_x2_kernel(
                 h, j = BLOCKS[n][k // 2]
                 t0 = 2 * (k % 2)
                 if t0 == 0:
-                    o32[h, j] = work.tile([P, 4, CHUNK], F32, name="o32", tag="o32", bufs=6, align_bytes=64)
+                    o32[h, j] = work.tile([P, 4, CHUNK], F32, name="o32", tag="o32", bufs=7, align_bytes=64)
                 pair = o32[h, j][:, t0 : t0 + 2, :]
                 nc.vector.tensor_tensor(
                     out=pair.rearrange("p t c -> p (t c)"), in0=gram_banks[n, k][:], in1=base_sb[n, k][:], op=ALU.mult
@@ -356,16 +379,16 @@ def tile_twotimehiddentangentkernel_x2_kernel(
                 rows = out_0[BANK * h : BANK * (h + 1), chunk_cols(j)].rearrange("(p t) m -> p t m", t=4)
                 nc.sync.dma_start(out=rows[:, t0 : t0 + 2, :], in_=pair)
 
-        def scalar_cast(h, j):
+        def scalar_cast(h, j, cols=slice(0, CHUNK)):
             if (h, j) not in o16:
                 o16[h, j] = work.tile([P, CHUNK, 4], BF16, name="o16", tag="o16", bufs=O16_BUFS, align_bytes=64)
-            nc.scalar.copy(out=into_words(o16[h, j][:]), in_=by_runs(o32[h, j][:]))
+            nc.scalar.copy(out=into_words(o16[h, j][:, cols, :]), in_=by_runs(o32[h, j][:, :, cols]))
 
-        def pool_cast(h, j, tag="o16", bufs=O16_BUFS):
+        def pool_cast(h, j, tag="o16", bufs=O16_BUFS, cols=slice(0, CHUNK)):
             if (h, j) not in o16:
                 o16[h, j] = work.tile([P, CHUNK, 4], BF16, name="o16", tag=tag, bufs=bufs, align_bytes=64)
             nc.gpsimd.tensor_scalar(
-                out=o16[h, j][:], in0=o32[h, j][:].rearrange("p t c -> p c t"),
+                out=o16[h, j][:, cols, :], in0=o32[h, j][:, :, cols].rearrange("p t c -> p c t"),
                 scalar1=1.0, scalar2=0.0, op0=ALU.mult, op1=ALU.add,
             )
 
@@ -435,108 +458,101 @@ def tile_twotimehiddentangentkernel_x2_kernel(
         factor(nc.vector, 0, 1, (0, 1, 2, 3))
         quant_in(Y, 0, 2)
         product(0, 1)
-        z_mm(1, (0, 1, 2))
-        transposes(X, 2, vector_bank("turn"))
-        stage(1, 3)
-        minus_v = turn_vector(minus_rows, "spare", 1)
-        z_mm(2, (0, 1))
-        transposes(X, 3, vector_bank("turn"))
-        stage(2, 2)
-        z_mm(3, (0, 1, 2))
-        for chunk in (2, 3):
-            transposes(Y, chunk, vector_bank("turn"))
-        factor(nc.vector, 1, 0, (0, 1, 2, 3))
-        for chunk in (2, 3):
-            turn_out(X, chunk, False)
-        quant_d(0)
-        quant_in(X, 2, 2)
-        product(1)
+        shared_stage(1, ())
+        for u, (side, chunk) in zip((1, 2, 3), ((X, 2), (X, 3), (Y, 2))):
+            turn(side, chunk, True)
+            factor(nc.vector, u, 0, (0, 1, 2, 3) if u == 1 else (1, 3))
+            quant_d(u - 1)
+            if u > 1:
+                quant_in(side, 2, 2 if side == X else 1)
+            shared_stage(u + 1, (0, 2))
+            if u == 3:
+                base_mm(0, (0, 1, 2))
+                base_mm(0, (3,), spare_bank)
+                gram_mm(0, BANKS, (0,))
+            product(u)
 
-        sigmoid(3, (0,))
-        square(2)
-        z_mm(3, (3,))
-        sigmoid(3, (1, 2, 3))
-        factor(nc.gpsimd, 3, 0, (0, 1, 2))
-        product_of_square(2, minus_v)
-        for chunk in (2, 3):
-            turn_out(Y, chunk, False)
-        quant_d(1)
-        factor(nc.vector, 3, 0, (3,))
-        quant_d(2)
-        stage(4)
-        z_mm(5, (0, 1, 2))
-        gram_mm(0, BANKS, (0,))
-        product(3)
-        quant_in(Y, 2, 2)
+        base_out(0, BANKS)
+        factor(nc.vector, 4, 0, (1, 3))
         quant_d(3)
-
-        def window(n, u, casts, late):
-            sigmoid(u + 1, (0,))
-            base_mm(n, (0,))
-            gram_mm(n, late, (0,))
-            square(u)
-            sigmoid(u + 1, (1,))
-            base_mm(n, (1,))
-            sigmoid(u + 1, (2,))
-            z_mm(u + 1, (3,))
-            gram_mm(n, (0, 1), (1,))
-            base_out(n, (0,))
-            base_mm(n, (2,))
-            base_out(n, (1,))
-            base_mm(n, (3,))
-            gram_mm(n, (2, 3), (1,))
-            sigmoid(u + 1, (3,))
-            base_out(n, (2, 3))
-            factor(nc.gpsimd, u + 1, 0, (0,))
-            for piece in casts:
-                pool_cast(*piece)
-            factor(nc.gpsimd, u + 1, 0, (1, 2, 3))
-            product_of_square(u, minus_v)
-            hadamard(n, BANKS)
-
-        window(0, 4, (), ())
-        stage(6)
-        z_mm(7, (0, 1, 2))
-        quant_d(4, (0,))
-        gram_mm(1, (0, 2), (0,))
+        z_mm(5, (0, 1))
+        gram_mm(0, BANKS, (1,))
+        z_mm(5, (2,))
+        z_mm(5, (3,), spare_bank)
+        product(4)
+        sigmoid(5, BANKS)
+        factor(nc.gpsimd, 5, 0, (0, 1, 2))
+        z_mm(6, (0, 1))
+        hadamard(0, BANKS)
+        turn(Y, 3, False)
+        minus_v = turn_vector(minus_rows, "spare", 1)
+        quant_d(4)
+        quant_in(Y, 3)
+        sigmoid(6, (0,))
+        scalar_factor(5, 3)
+        sigmoid(6, (1,))
+        z_mm(6, (2, 3))
+        sigmoid(6, (2,))
+        square(6, 0)
+        sigmoid(6, (3,))
+        base_mm(1, (0, 1))
         product(5)
-        quant_d(4, (1,))
+
+        base_out(1, (0,))
+        square(6, 1)
+        base_mm(1, (2,))
+        gram_mm(1, BANKS, (0,))
+        base_out(1, (1,))
+        base_mm(1, (3,))
+        base_out(1, (2, 3))
         quant_d(5)
-        window(1, 6, (), (1, 3))
-        quant_d(6)
+        for k in (0, 1, 2):
+            z_mm(7, (k,))
+            gram_mm(1, (k,), (1,))
+        gram_mm(1, (3,), (1,))
+        pair_tile(0, 0, "relay5")
+        pool_cast(0, 0)
+        pool_cast(0, 1, cols=slice(0, P))
+        sigmoid(7, (0,))
+        z_mm(7, (3,))
+        sigmoid(7, (1, 2, 3))
+        factor(nc.gpsimd, 7, 0, (0, 1, 2))
+        scalar_factor(7, 3, 0)
+        for t in BANKS:
+            scalar_factor(7, t, 1)
+        product_of_square(6, minus_v)
+        hadamard(1, BANKS)
         base_mm(2, (0, 1, 2))
         base_mm(2, (3,), spare_bank)
+        quant_d(6)
         base_out(2, BANKS)
-        scalar_cast(0, 0)
-        o16[0, 1] = work.tile([P, CHUNK, 4], BF16, name="o16", tag="relay7", bufs=1, align_bytes=64)
-        scalar_cast(0, 1)
-        base_mm(3, (0, 1))
-        gram_mm(2, BANKS, (0,))
-        base_mm(3, (2,))
+        gram_mm(2, (0, 1), (0, 1))
+        base_mm(3, (0, 1, 2))
+        gram_mm(2, (2, 3), (0, 1))
         base_mm(3, (3,), spare_bank)
         base_out(3, BANKS)
-        product(7)
+        scalar_cast(0, 1, cols=slice(P, 2 * P))
+        for part in (0, 1):
+            product(7, part)
         quant_o(0, 0)
-        for half in (0, 1):
-            quant_d(7, (half,))
-        quant_o(0, 1)
-        store_words(0, 0, 2)
+        quant_d(7)
         pair_tile(1, 0, "relay7")
-        pair_tile(0, 2, "pair")
+        pair_tile(0, 2, "pair0")
         pool_cast(1, 0)
         pool_cast(1, 1)
-        gram_mm(2, BANKS, (1,))
-        gram_mm(3, (0, 1, 2), (0, 1), scalar_bank)
-        gram_mm(3, (3,), (0, 1), spare_bank)
+        for k in BANKS:
+            gram_mm(3, (k,), (0, 1), spare_bank if k == 3 else scalar_bank)
         for n in (2, 3):
             for half in (0, 1):
                 hadamard(n, (2 * half, 2 * half + 1))
-                scalar_cast(*BLOCKS[n][half])
+                (pool_cast if (n, half) == (2, 0) else scalar_cast)(*BLOCKS[n][half])
+        quant_o(0, 1)
+        store_words(0, 0, 2)
+        quant_o(1, 2)
         quant_o(1, 0, 2)
+        store_words(1, 0, 3)
         quant_o(0, 2, 2)
         store_words(0, 2, 4)
-        quant_o(1, 2)
-        store_words(1, 0, 3)
         quant_o(1, 3)
         store_words(1, 3, 4)
         store_scales()

@@ -233,17 +233,22 @@ def tile_twotimehiddentangentkernel_x2_kernel(
                     z_mm(u, (k,))
                 sigmoid(u, (k,))
 
-        def factor_tile(u):
-            if u not in fac:
+        def factor_tile(u, part):
+            if u == 7 and (u, part) not in fac:
+                fac[u, part] = work.tile([P, 4, CHUNK], F32, name="fac", tag="fac7" if part == 0 else "fac7b", bufs=1, align_bytes=64)
+            if u != 7 and u not in fac:
                 tag, bufs = ("fac4", 1) if u in (4, 5) else ("fac", 2)
                 fac[u] = work.tile([P, 4 * BANK], F32, name="fac", tag=tag, bufs=bufs, align_bytes=64)
 
+        def factor_planes(u, part):
+            return fac[u, part][:] if u == 7 else planes_of(fac[u], u, part)
+
         def scalar_factor(u, t, part=0):
             side, g, token, width = UNITS[u][part]
-            factor_tile(u)
+            factor_tile(u, part)
             c = 8 * side + 4 * g + t
             nc.scalar.activation(
-                out=planes_of(fac[u], u, part)[:, t, :], in_=planes_of(sig[u], u, part)[:, t, :], func=ACT.Identity,
+                out=factor_planes(u, part)[:, t, :], in_=planes_of(sig[u], u, part)[:, t, :], func=ACT.Identity,
                 bias=plus4v[:, c : c + 1], scale=minus4v[:, c : c + 1],
             )
 
@@ -258,11 +263,11 @@ def tile_twotimehiddentangentkernel_x2_kernel(
 
         def factor(engine, u, part, slots):
             side, g, token, width = UNITS[u][part]
-            factor_tile(u)
+            factor_tile(u, part)
             for t in slots:
                 c = 8 * side + 4 * g + t
                 engine.tensor_scalar(
-                    out=planes_of(fac[u], u, part)[:, t, :], in0=planes_of(sig[u], u, part)[:, t, :],
+                    out=factor_planes(u, part)[:, t, :], in0=planes_of(sig[u], u, part)[:, t, :],
                     scalar1=minus4v[:, c : c + 1], scalar2=plus4v[:, c : c + 1], op0=ALU.mult, op1=ALU.add,
                 )
 
@@ -275,14 +280,14 @@ def tile_twotimehiddentangentkernel_x2_kernel(
         def square(u, part):
             width = UNITS[u][part][3]
             if part == 0:
-                squares[u] = work.tile([P, BANK, 4], F32, name="square", tag="square", bufs=2, align_bytes=64)
+                squares[u] = work.tile([P, BANK, 4], F32, name="square", tag="square", bufs=1, align_bytes=64)
             nc.scalar.activation(
                 out=into_words(squares[u][:, width * part : width * (part + 1), :]),
                 in_=by_runs(planes_of(sig[u], u, part)), func=ACT.Square, bias=-1.0, scale=2.0,
             )
 
         def new_d16(u):
-            tag, bufs = ("relay%d" % u, 1) if u in (5, 7) else ("d16", 2)
+            tag, bufs = ("relay%d" % u, 1) if u == 5 else ("d16", 2)
             d16[u] = work.tile([P, BANK, 4], BF16, name="d16", tag=tag, bufs=bufs, align_bytes=64)
 
         def product(u, part=0):
@@ -292,7 +297,7 @@ def tile_twotimehiddentangentkernel_x2_kernel(
             nc.vector.tensor_tensor(
                 out=into_words(d16[u][:, width * part : width * (part + 1), :]),
                 in0=by_runs(planes_of(sig[u], u, part)),
-                in1=by_runs(planes_of(fac[u], u, part)),
+                in1=by_runs(factor_planes(u, part)),
                 op=ALU.mult,
             )
 
@@ -307,16 +312,18 @@ def tile_twotimehiddentangentkernel_x2_kernel(
                 op0=ALU.subtract, op1=ALU.mult,
             )
 
-        def quant_d(u):
-            d_codes[u] = keep.tile([P, BANK], U32, name="d_codes%d" % u, align_bytes=64)
-            d_planes[u] = keep.tile([P, BANK], U8, name="d_planes%d" % u, align_bytes=64)
+        def quant_d(u, halves=(0, 1)):
+            if u not in d_codes:
+                d_codes[u] = keep.tile([P, BANK], U32, name="d_codes%d" % u, align_bytes=64)
+                d_planes[u] = keep.tile([P, BANK], U8, name="d_planes%d" % u, align_bytes=64)
+            cols = slice(CHUNK * halves[0], CHUNK * (halves[-1] + 1))
             for part, (side, g, token, width) in enumerate(UNITS[u]):
                 for step in range(0, width, P):
                     d_at[side, g, token + step] = (u, width * part + step)
             nc.vector.quantize_mx(
-                out=d_codes[u][:].bitcast(FP8X4),
-                scales=d_planes[u][:],
-                in_=d16[u][:].rearrange("p n t -> p (n t)"),
+                out=d_codes[u][:, cols].bitcast(FP8X4),
+                scales=d_planes[u][:, cols],
+                in_=d16[u][:, cols, :].rearrange("p n t -> p (n t)"),
             )
 
         base_banks, gram_banks, base_sb, o32, o16 = {}, {}, {}, {}, {}
@@ -384,6 +391,9 @@ def tile_twotimehiddentangentkernel_x2_kernel(
                 o16[h, j] = work.tile([P, CHUNK, 4], BF16, name="o16", tag="o16", bufs=O16_BUFS, align_bytes=64)
             nc.scalar.copy(out=into_words(o16[h, j][:, cols, :]), in_=by_runs(o32[h, j][:, :, cols]))
 
+        def vector_cast(h, j, cols):
+            nc.vector.tensor_copy(out=into_words(o16[h, j][:, cols, :]), in_=by_runs(o32[h, j][:, :, cols]))
+
         def pool_cast(h, j, tag="o16", bufs=O16_BUFS, cols=slice(0, CHUNK)):
             if (h, j) not in o16:
                 o16[h, j] = work.tile([P, CHUNK, 4], BF16, name="o16", tag=tag, bufs=bufs, align_bytes=64)
@@ -440,9 +450,9 @@ def tile_twotimehiddentangentkernel_x2_kernel(
         v_bank = turn_vector(v_rows, "dve", 4)
         permute(w_perm[X], w_raw[X], 4, 8)
         quant_in(X, 1)
-        nc.vector.tensor_scalar(out=minus_rows[:], in0=v_rows[:], scalar1=-1.0, scalar2=None, op0=ALU.mult)
         vector_out(v_bank, minus4v, -4.0)
         vector_out(v_bank, plus4v, 4.0)
+        nc.vector.tensor_scalar(out=minus_rows[:], in0=v_rows[:], scalar1=-1.0, scalar2=None, op0=ALU.mult)
         for k in (0, 1, 2):
             sigmoid(0, (k,))
             z_mm(0, (4 + k,))
@@ -513,46 +523,56 @@ def tile_twotimehiddentangentkernel_x2_kernel(
         pair_tile(0, 0, "relay5")
         pool_cast(0, 0)
         pool_cast(0, 1, cols=slice(0, P))
-        sigmoid(7, (0,))
-        z_mm(7, (3,))
-        sigmoid(7, (1, 2, 3))
+        sigmoid(7, (0, 1))
         factor(nc.gpsimd, 7, 0, (0, 1, 2))
         scalar_factor(7, 3, 0)
+        product_of_square(6, minus_v)
+        base_mm(2, (0, 1))
+        hadamard(1, BANKS)
+        base_mm(2, (2,), spare_bank)
+        quant_d(6)
+        base_out(2, (0,))
+        base_mm(2, (3,))
+        gram_mm(2, (0,), (0, 1))
+        base_out(2, (1,))
+        z_mm(7, (3,))
+        gram_mm(2, (1, 2, 3), (0, 1))
+        base_out(2, (2, 3))
+        sigmoid(7, (2, 3))
         for t in BANKS:
             scalar_factor(7, t, 1)
-        product_of_square(6, minus_v)
-        hadamard(1, BANKS)
-        base_mm(2, (0, 1, 2))
-        base_mm(2, (3,), spare_bank)
-        quant_d(6)
-        base_out(2, BANKS)
-        gram_mm(2, (0, 1), (0, 1))
         base_mm(3, (0, 1, 2))
-        gram_mm(2, (2, 3), (0, 1))
         base_mm(3, (3,), spare_bank)
-        base_out(3, BANKS)
         scalar_cast(0, 1, cols=slice(P, 2 * P))
-        for part in (0, 1):
-            product(7, part)
+        o16[1, 1] = work.tile([P, CHUNK, 4], BF16, name="o16", tag="relay7", bufs=1, align_bytes=64)
+        scalar_cast(1, 1)
+        base_out(3, BANKS)
+        product(7, 0)
+        pool_cast(1, 0, "fac7", 1)
+        hadamard(2, BANKS)
+        quant_d(7, (0,))
+        gram_mm(3, BANKS, (0,))
+        product(7, 1)
+        scalar_cast(0, 2)
         quant_o(0, 0)
-        quant_d(7)
-        pair_tile(1, 0, "relay7")
-        pair_tile(0, 2, "pair0")
-        pool_cast(1, 0)
-        pool_cast(1, 1)
-        for k in BANKS:
-            gram_mm(3, (k,), (0, 1), spare_bank if k == 3 else scalar_bank)
-        for n in (2, 3):
-            for half in (0, 1):
-                hadamard(n, (2 * half, 2 * half + 1))
-                (pool_cast if (n, half) == (2, 0) else scalar_cast)(*BLOCKS[n][half])
+        quant_d(7, (1,))
+        gram_mm(3, BANKS, (1,))
+        quant_o(1, 0)
         quant_o(0, 1)
         store_words(0, 0, 2)
+        quant_o(1, 1)
+        store_words(1, 0, 2)
+        pool_cast(1, 2, "relay7", 1)
+        hadamard(3, (0, 1))
+        scalar_cast(0, 3)
+        hadamard(3, (2,))
+        quant_o(0, 2)
+        hadamard(3, (3,))
+        scalar_cast(1, 3, cols=slice(0, P))
         quant_o(1, 2)
-        quant_o(1, 0, 2)
-        store_words(1, 0, 3)
-        quant_o(0, 2, 2)
+        vector_cast(1, 3, slice(P, 2 * P))
+        quant_o(0, 3)
         store_words(0, 2, 4)
         quant_o(1, 3)
-        store_words(1, 3, 4)
+        store_words(1, 2, 4)
         store_scales()

@@ -32,7 +32,8 @@ FIRST_UNIT_BANKS = [
 ] + [[(1, t, 0, CHUNK) for t in slots] for slots in ((0,), (1, 2), (3,))]
 BLOCKS = [[(0, 0), (0, 1)], [(1, 0), (1, 1)], [(0, 2), (1, 2)], [(0, 3), (1, 3)]]
 SIG_BUFS = 4
-O16_BUFS = 3
+POOL_COLS = 64
+O16_BUFS = 4
 
 def tile_twotimehiddentangentkernel_x2_kernel(
     tc, x, y, wa_words, wa_scales, wb_words, wb_scales, b, va, vb, out_0, out_1, out_2
@@ -301,9 +302,10 @@ def tile_twotimehiddentangentkernel_x2_kernel(
                 op=ALU.mult,
             )
 
-        def product_of_square(u, minus_v):
-            new_d16(u)
-            for part, (side, g, token, width) in enumerate(UNITS[u]):
+        def product_of_square(u, minus_v, part):
+            if part == 0:
+                new_d16(u)
+            for side, g, token, width in UNITS[u][part : part + 1]:
               c = 8 * side + 4 * g
               cols = slice(width * part, width * (part + 1))
               nc.vector.scalar_tensor_tensor(
@@ -332,20 +334,22 @@ def tile_twotimehiddentangentkernel_x2_kernel(
             return slice(CHUNK * j, CHUNK * (j + 1))
 
         def tiles_in_bank(n, k):
+            if n < 2:
+                return [(n, k, 0, BANK)]
             h, j = BLOCKS[n][k // 2]
-            return [(h, 2 * (k % 2) + i, j, chunk_cols(i)) for i in (0, 1)]
+            return [(h, 2 * (k % 2) + i, CHUNK * j, CHUNK) for i in (0, 1)]
 
         def base_mm(n, banks, bank=scalar_bank):
             for k in banks:
                 base_banks[n, k] = bank("base")
-                for h, t, j, at in tiles_in_bank(n, k):
+                for i, (h, t, col, width) in enumerate(tiles_in_bank(n, k)):
                     rows = slice(BANK * h + P * t, BANK * h + P * (t + 1))
                     nc.tensor.matmul_mx(
-                        out=base_banks[n, k][:, at],
+                        out=base_banks[n, k][:, width * i : width * (i + 1)],
                         lhsT=codes[X][:, rows].bitcast(FP8X4),
                         lhsT_scale=planes[X][:, rows],
-                        rhs=codes[Y][:, chunk_cols(j)].bitcast(FP8X4),
-                        rhs_scale=planes[Y][:, chunk_cols(j)],
+                        rhs=codes[Y][:, col : col + width].bitcast(FP8X4),
+                        rhs_scale=planes[Y][:, col : col + width],
                         start=True,
                         stop=True,
                     )
@@ -357,34 +361,38 @@ def tile_twotimehiddentangentkernel_x2_kernel(
 
         def gram_mm(n, banks, passes, bank=vector_bank):
             for k in banks:
+                tiles = tiles_in_bank(n, k)
                 for g in passes:
                     if g == 0:
                         gram_banks[n, k] = bank("gram")
-                    for i, (h, t, j, at) in enumerate(tiles_in_bank(n, k)):
+                    for i, (h, t, col, width) in enumerate(tiles):
                         ux, cx = d_at[X, g, BANK * h + P * t]
-                        uy, cy = d_at[Y, g, CHUNK * j]
+                        uy, cy = d_at[Y, g, col]
                         nc.tensor.matmul_mx(
-                            out=gram_banks[n, k][:, at],
+                            out=gram_banks[n, k][:, width * i : width * (i + 1)],
                             lhsT=d_codes[ux][:, cx : cx + P].bitcast(FP8X4),
                             lhsT_scale=d_planes[ux][:, cx : cx + P],
-                            rhs=d_codes[uy][:, cy : cy + CHUNK].bitcast(FP8X4),
-                            rhs_scale=d_planes[uy][:, cy : cy + CHUNK],
+                            rhs=d_codes[uy][:, cy : cy + width].bitcast(FP8X4),
+                            rhs_scale=d_planes[uy][:, cy : cy + width],
                             start=(g == 0 and i == 0),
-                            stop=(g == 1 and i == 1),
+                            stop=(g == 1 and i == len(tiles) - 1),
                         )
 
         def hadamard(n, banks):
             for k in banks:
-                h, j = BLOCKS[n][k // 2]
-                t0 = 2 * (k % 2)
+                tiles = tiles_in_bank(n, k)
+                h, t0, col, width = tiles[0]
                 if t0 == 0:
-                    o32[h, j] = work.tile([P, 4, CHUNK], F32, name="o32", tag="o32", bufs=7, align_bytes=64)
-                pair = o32[h, j][:, t0 : t0 + 2, :]
+                    whole = work.tile([P, 4, width], F32, name="o32", tag="o32_%d" % width, bufs=2 if n < 2 else 4, align_bytes=64)
+                    o32[h, col, width] = whole
+                    for i in range(width // CHUNK):
+                        o32[h, col // CHUNK + i] = whole[:, :, chunk_cols(i)]
+                slots = o32[h, col, width][:, t0 : t0 + len(tiles), :]
                 nc.vector.tensor_tensor(
-                    out=pair.rearrange("p t c -> p (t c)"), in0=gram_banks[n, k][:], in1=base_sb[n, k][:], op=ALU.mult
+                    out=slots.rearrange("p t c -> p (t c)"), in0=gram_banks[n, k][:], in1=base_sb[n, k][:], op=ALU.mult
                 )
-                rows = out_0[BANK * h : BANK * (h + 1), chunk_cols(j)].rearrange("(p t) m -> p t m", t=4)
-                nc.sync.dma_start(out=rows[:, t0 : t0 + 2, :], in_=pair)
+                rows = out_0[BANK * h : BANK * (h + 1), col : col + width].rearrange("(p t) m -> p t m", t=4)
+                nc.sync.dma_start(out=rows[:, t0 : t0 + len(tiles), :], in_=slots)
 
         def scalar_cast(h, j, cols=slice(0, CHUNK)):
             if (h, j) not in o16:
@@ -423,6 +431,12 @@ def tile_twotimehiddentangentkernel_x2_kernel(
             nc.sync.dma_start(
                 out=out_1[h][:, cols, :].rearrange("p m t -> p (m t)").bitcast(I32),
                 in_=o_codes[:, h, cols].bitcast(I32),
+            )
+
+        def store_both(j):
+            nc.sync.dma_start(
+                out=out_1[:, :, chunk_cols(j), :].rearrange("h p m t -> p h (m t)").bitcast(I32),
+                in_=o_codes[:, :, chunk_cols(j)].bitcast(I32),
             )
 
         def store_scales():
@@ -497,7 +511,6 @@ def tile_twotimehiddentangentkernel_x2_kernel(
         turn(Y, 3, False)
         minus_v = turn_vector(minus_rows, "spare", 1)
         quant_d(4)
-        quant_in(Y, 3)
         sigmoid(6, (0,))
         scalar_factor(5, 3)
         sigmoid(6, (1,))
@@ -505,74 +518,80 @@ def tile_twotimehiddentangentkernel_x2_kernel(
         sigmoid(6, (2,))
         square(6, 0)
         sigmoid(6, (3,))
-        base_mm(1, (0, 1))
+        base_mm(1, (0,))
+        gram_mm(1, (0, 1), (0,))
+        base_mm(1, (1,))
+        gram_mm(1, (2, 3), (0,))
+        base_mm(1, (2,))
         product(5)
+        quant_in(Y, 3)
 
         base_out(1, (0,))
-        square(6, 1)
-        base_mm(1, (2,))
-        gram_mm(1, BANKS, (0,))
-        base_out(1, (1,))
         base_mm(1, (3,))
+        base_out(1, (1,))
+        z_mm(7, (0,))
         base_out(1, (2, 3))
         quant_d(5)
-        for k in (0, 1, 2):
-            z_mm(7, (k,))
-            gram_mm(1, (k,), (1,))
-        gram_mm(1, (3,), (1,))
+        gram_mm(1, (0,), (1,))
+        z_mm(7, (1,))
+        gram_mm(1, (1, 2, 3), (1,))
+        z_mm(7, (2,))
         pair_tile(0, 0, "relay5")
         pool_cast(0, 0)
-        pool_cast(0, 1, cols=slice(0, P))
-        sigmoid(7, (0, 1))
+        pool_cast(0, 1)
+        sigmoid(7, (0,))
+        square(6, 1)
+        sigmoid(7, (1,))
         factor(nc.gpsimd, 7, 0, (0, 1, 2))
         scalar_factor(7, 3, 0)
-        product_of_square(6, minus_v)
+        product_of_square(6, minus_v, 0)
         base_mm(2, (0, 1))
         hadamard(1, BANKS)
-        base_mm(2, (2,), spare_bank)
+        product_of_square(6, minus_v, 1)
+        quant_o(0, 0, 2)
+        store_words(0, 0, 2)
         quant_d(6)
-        base_out(2, (0,))
-        base_mm(2, (3,))
-        gram_mm(2, (0,), (0, 1))
-        base_out(2, (1,))
+        for k in (0, 1):
+            base_out(2, (k,))
+            base_mm(2, (k + 2,))
+        base_out(2, (2,))
         z_mm(7, (3,))
-        gram_mm(2, (1, 2, 3), (0, 1))
-        base_out(2, (2, 3))
+        gram_mm(2, BANKS, (0, 1))
+        base_out(2, (3,))
         sigmoid(7, (2, 3))
         for t in BANKS:
             scalar_factor(7, t, 1)
         base_mm(3, (0, 1, 2))
         base_mm(3, (3,), spare_bank)
-        scalar_cast(0, 1, cols=slice(P, 2 * P))
-        o16[1, 1] = work.tile([P, CHUNK, 4], BF16, name="o16", tag="relay7", bufs=1, align_bytes=64)
-        scalar_cast(1, 1)
-        base_out(3, BANKS)
         product(7, 0)
-        pool_cast(1, 0, "fac7", 1)
+        pair_tile(1, 0, "fac7")
+        scalar_cast(1, 1, cols=slice(POOL_COLS, CHUNK))
+        pool_cast(1, 0)
+        pool_cast(1, 1, cols=slice(0, POOL_COLS))
         hadamard(2, BANKS)
+        o16[0, 2] = work.tile([P, CHUNK, 4], BF16, name="o16", tag="relay7", bufs=1, align_bytes=64)
+        scalar_cast(0, 2)
+        base_out(3, BANKS)
         quant_d(7, (0,))
         gram_mm(3, BANKS, (0,))
         product(7, 1)
-        scalar_cast(0, 2)
-        quant_o(0, 0)
+        quant_o(1, 0)
+        store_words(1, 0, 1)
         quant_d(7, (1,))
         gram_mm(3, BANKS, (1,))
-        quant_o(1, 0)
-        quant_o(0, 1)
-        store_words(0, 0, 2)
         quant_o(1, 1)
-        store_words(1, 0, 2)
+        store_words(1, 1, 2)
+        quant_o(0, 2)
+        store_words(0, 2, 3)
         pool_cast(1, 2, "relay7", 1)
         hadamard(3, (0, 1))
         scalar_cast(0, 3)
-        hadamard(3, (2,))
-        quant_o(0, 2)
-        hadamard(3, (3,))
+        hadamard(3, (2, 3))
         scalar_cast(1, 3, cols=slice(0, P))
         quant_o(1, 2)
         vector_cast(1, 3, slice(P, 2 * P))
         quant_o(0, 3)
-        store_words(0, 2, 4)
+        store_words(0, 3, 4)
         quant_o(1, 3)
         store_words(1, 2, 4)
         store_scales()

@@ -46,13 +46,10 @@ def tile_twotimehiddentangentkernel_x2_kernel(
         ctx.enter_context(tc.manual_schedule())
 
         def scalar_bank(name):
-            return psum.tile([P, BANK], F32, name=name, tag="act", bufs=3)
+            return psum.tile([P, BANK], F32, name=name, tag="act", bufs=4)
 
         def vector_bank(name):
             return psum.tile([P, BANK], F32, name=name, tag="dve", bufs=4)
-
-        def spare_bank(name):
-            return psum.tile([P, BANK], F32, name=name, tag="spare", bufs=1)
 
         plane_raw = [keep.tile([P, F], U8, name="plane_raw%d" % side, align_bytes=64) for side in (X, Y)]
         for side in (X, Y):
@@ -119,7 +116,6 @@ def tile_twotimehiddentangentkernel_x2_kernel(
                 in_=src[:].bitcast(I32).rearrange("p (q r i) -> p r q i", r=8, q=16)[:, r0:r1, :, :],
             )
 
-        minus_rows = keep.tile([P, P], BF16, name="minus_rows", align_bytes=64)
         turned = {}
         grouped = [keep.tile([P, 4 * N], BF16, name="grouped%d" % side, align_bytes=64) for side in (X, Y)]
         codes = [keep.tile([P, N], U32, name="codes%d" % side, align_bytes=64) for side in (X, Y)]
@@ -238,7 +234,7 @@ def tile_twotimehiddentangentkernel_x2_kernel(
             if u == 7 and (u, part) not in fac:
                 fac[u, part] = work.tile([P, 4, CHUNK], F32, name="fac", tag="fac7" if part == 0 else "fac7b", bufs=1, align_bytes=64)
             if u != 7 and u not in fac:
-                tag, bufs = ("fac4", 1) if u in (4, 5) else ("fac", 2)
+                tag, bufs = ("fac4", 1) if u in (4, 5) else ("fac6", 1) if u == 6 else ("fac", 2)
                 fac[u] = work.tile([P, 4 * BANK], F32, name="fac", tag=tag, bufs=bufs, align_bytes=64)
 
         def factor_planes(u, part):
@@ -256,11 +252,16 @@ def tile_twotimehiddentangentkernel_x2_kernel(
         def shared_stage(u, scalar_slots):
             for pair in ((0, 1), (2, 3)):
                 for k in pair:
-                    z_mm(u, (k,), spare_bank if k == 3 else scalar_bank)
+                    z_mm(u, (k,), scalar_bank)
                 sigmoid(u, pair)
                 for t in pair:
                     if t in scalar_slots:
                         scalar_factor(u, t)
+
+        def narrow_stage(u, part):
+            sigmoid(u, (2 * part, 2 * part + 1))
+            for t in range(4):
+                scalar_factor(u, t, part)
 
         def factor(engine, u, part, slots):
             side, g, token, width = UNITS[u][part]
@@ -278,15 +279,6 @@ def tile_twotimehiddentangentkernel_x2_kernel(
         def into_words(tile16):
             return tile16.rearrange("p (c i) t -> p c t i", i=RUN)
 
-        def square(u, part):
-            width = UNITS[u][part][3]
-            if part == 0:
-                squares[u] = work.tile([P, BANK, 4], F32, name="square", tag="square", bufs=1, align_bytes=64)
-            nc.scalar.activation(
-                out=into_words(squares[u][:, width * part : width * (part + 1), :]),
-                in_=by_runs(planes_of(sig[u], u, part)), func=ACT.Square, bias=-1.0, scale=2.0,
-            )
-
         def new_d16(u):
             tag, bufs = ("relay%d" % u, 1) if u == 5 else ("d16", 2)
             d16[u] = work.tile([P, BANK, 4], BF16, name="d16", tag=tag, bufs=bufs, align_bytes=64)
@@ -302,16 +294,11 @@ def tile_twotimehiddentangentkernel_x2_kernel(
                 op=ALU.mult,
             )
 
-        def product_of_square(u, minus_v, part):
-            if part == 0:
-                new_d16(u)
-            for side, g, token, width in UNITS[u][part : part + 1]:
-              c = 8 * side + 4 * g
-              cols = slice(width * part, width * (part + 1))
-              nc.vector.scalar_tensor_tensor(
-                out=d16[u][:, cols, :], in0=squares[u][:, cols, :], scalar=1.0,
-                in1=minus_v[:, c : c + 4].unsqueeze(1).to_broadcast([P, width, 4]),
-                op0=ALU.subtract, op1=ALU.mult,
+        def whole_product(u):
+            new_d16(u)
+            nc.vector.tensor_tensor(
+                out=into_words(d16[u][:]), in0=by_runs(sig[u][:].rearrange("p (t n) -> p t n", t=4)),
+                in1=by_runs(fac[u][:].rearrange("p (t n) -> p t n", t=4)), op=ALU.mult,
             )
 
         def quant_d(u, halves=(0, 1)):
@@ -399,8 +386,9 @@ def tile_twotimehiddentangentkernel_x2_kernel(
                 o16[h, j] = work.tile([P, CHUNK, 4], BF16, name="o16", tag="o16", bufs=O16_BUFS, align_bytes=64)
             nc.scalar.copy(out=into_words(o16[h, j][:, cols, :]), in_=by_runs(o32[h, j][:, :, cols]))
 
-        def vector_cast(h, j, cols):
-            nc.vector.tensor_copy(out=into_words(o16[h, j][:, cols, :]), in_=by_runs(o32[h, j][:, :, cols]))
+        def vector_cast(h, j):
+            o16[h, j] = work.tile([P, CHUNK, 4], BF16, name="o16", tag="o16", bufs=O16_BUFS, align_bytes=64)
+            nc.vector.tensor_copy(out=into_words(o16[h, j][:]), in_=by_runs(o32[h, j][:]))
 
         def pool_cast(h, j, tag="o16", bufs=O16_BUFS, cols=slice(0, CHUNK)):
             if (h, j) not in o16:
@@ -460,13 +448,12 @@ def tile_twotimehiddentangentkernel_x2_kernel(
         vector_out(b_bank, bias2, 2.0)
         turn_out(X, 1, False)
         z_mm(0, (0, 1, 2))
-        z_mm(0, (3,), spare_bank)
+        z_mm(0, (3,))
         v_bank = turn_vector(v_rows, "dve", 4)
         permute(w_perm[X], w_raw[X], 4, 8)
         quant_in(X, 1)
         vector_out(v_bank, minus4v, -4.0)
         vector_out(v_bank, plus4v, 4.0)
-        nc.vector.tensor_scalar(out=minus_rows[:], in0=v_rows[:], scalar1=-1.0, scalar2=None, op0=ALU.mult)
         for k in (0, 1, 2):
             sigmoid(0, (k,))
             z_mm(0, (4 + k,))
@@ -492,7 +479,7 @@ def tile_twotimehiddentangentkernel_x2_kernel(
             shared_stage(u + 1, (0, 2))
             if u == 3:
                 base_mm(0, (0, 1, 2))
-                base_mm(0, (3,), spare_bank)
+                base_mm(0, (3,))
                 gram_mm(0, BANKS, (0,))
             product(u)
 
@@ -501,77 +488,54 @@ def tile_twotimehiddentangentkernel_x2_kernel(
         quant_d(3)
         z_mm(5, (0, 1))
         gram_mm(0, BANKS, (1,))
-        z_mm(5, (2,))
-        z_mm(5, (3,), spare_bank)
+        z_mm(5, (2, 3))
         product(4)
         sigmoid(5, BANKS)
-        factor(nc.gpsimd, 5, 0, (0, 1, 2))
+        factor(nc.gpsimd, 5, 0, (0, 1))
         z_mm(6, (0, 1))
         hadamard(0, BANKS)
         turn(Y, 3, False)
-        minus_v = turn_vector(minus_rows, "spare", 1)
+        factor(nc.vector, 5, 0, (2, 3))
         quant_d(4)
-        sigmoid(6, (0,))
-        scalar_factor(5, 3)
-        sigmoid(6, (1,))
+        narrow_stage(6, 0)
         z_mm(6, (2, 3))
-        sigmoid(6, (2,))
-        square(6, 0)
-        sigmoid(6, (3,))
-        base_mm(1, (0,))
-        gram_mm(1, (0, 1), (0,))
-        base_mm(1, (1,))
-        gram_mm(1, (2, 3), (0,))
-        base_mm(1, (2,))
+        base_mm(1, (0, 1))
+        gram_mm(1, BANKS, (0,))
+        narrow_stage(6, 1)
         product(5)
         quant_in(Y, 3)
-
-        base_out(1, (0,))
-        base_mm(1, (3,))
-        base_out(1, (1,))
-        z_mm(7, (0,))
-        base_out(1, (2, 3))
+        base_mm(1, (2, 3))
+        base_out(1, BANKS)
         quant_d(5)
-        gram_mm(1, (0,), (1,))
+        z_mm(7, (0,))
+        gram_mm(1, (0, 1), (1,))
         z_mm(7, (1,))
-        gram_mm(1, (1, 2, 3), (1,))
-        z_mm(7, (2,))
-        pair_tile(0, 0, "relay5")
+        gram_mm(1, (2, 3), (1,))
+        z_mm(7, (2, 3))
+        whole_product(6)
+        pair_tile(0, 0, "fac6")
         pool_cast(0, 0)
-        pool_cast(0, 1)
-        sigmoid(7, (0,))
-        square(6, 1)
-        sigmoid(7, (1,))
-        factor(nc.gpsimd, 7, 0, (0, 1, 2))
-        scalar_factor(7, 3, 0)
-        product_of_square(6, minus_v, 0)
+        narrow_stage(7, 0)
         base_mm(2, (0, 1))
         hadamard(1, BANKS)
-        product_of_square(6, minus_v, 1)
-        quant_o(0, 0, 2)
-        store_words(0, 0, 2)
         quant_d(6)
+        quant_o(0, 0)
+        store_words(0, 0, 1)
         for k in (0, 1):
             base_out(2, (k,))
             base_mm(2, (k + 2,))
-        base_out(2, (2,))
-        z_mm(7, (3,))
         gram_mm(2, BANKS, (0, 1))
-        base_out(2, (3,))
-        sigmoid(7, (2, 3))
-        for t in BANKS:
-            scalar_factor(7, t, 1)
-        base_mm(3, (0, 1, 2))
-        base_mm(3, (3,), spare_bank)
+        base_out(2, (2, 3))
+        narrow_stage(7, 1)
+        base_mm(3, BANKS)
         product(7, 0)
         pair_tile(1, 0, "fac7")
-        scalar_cast(1, 1, cols=slice(POOL_COLS, CHUNK))
         pool_cast(1, 0)
-        pool_cast(1, 1, cols=slice(0, POOL_COLS))
         hadamard(2, BANKS)
-        o16[0, 2] = work.tile([P, CHUNK, 4], BF16, name="o16", tag="relay7", bufs=1, align_bytes=64)
-        scalar_cast(0, 2)
+        for h in (0, 1):
+            scalar_cast(h, 1)
         base_out(3, BANKS)
+        scalar_cast(0, 2)
         quant_d(7, (0,))
         gram_mm(3, BANKS, (0,))
         product(7, 1)
@@ -579,19 +543,18 @@ def tile_twotimehiddentangentkernel_x2_kernel(
         store_words(1, 0, 1)
         quant_d(7, (1,))
         gram_mm(3, BANKS, (1,))
-        quant_o(1, 1)
-        store_words(1, 1, 2)
-        quant_o(0, 2)
-        store_words(0, 2, 3)
-        pool_cast(1, 2, "relay7", 1)
+        for h in (0, 1):
+            quant_o(h, 1)
+            store_words(h, 1, 2)
+        pool_cast(1, 2, "fac7", 1)
         hadamard(3, (0, 1))
         scalar_cast(0, 3)
         hadamard(3, (2, 3))
-        scalar_cast(1, 3, cols=slice(0, P))
         quant_o(1, 2)
-        vector_cast(1, 3, slice(P, 2 * P))
-        quant_o(0, 3)
-        store_words(0, 3, 4)
+        vector_cast(1, 3)
+        quant_o(0, 2)
         quant_o(1, 3)
         store_words(1, 2, 4)
+        quant_o(0, 3)
+        store_words(0, 2, 4)
         store_scales()

@@ -145,11 +145,14 @@ def tile_twotimehiddentangentkernel_x2_kernel(
                 nc.tensor.transpose(bank[:, P * u : P * (u + 1)], pairs[:, u : D // 2 : 2], ident[:])
             return bank
 
-        def first_tile_out(j, bank):
+        def first_tile_out(j, bank, on_scalar):
             pairs = grouped[X][:, 4 * P * j : 4 * P * (j + 1)].bitcast(F32)
-            nc.vector.tensor_copy(
-                out=pairs.rearrange("p (r u) -> p r u", u=2), in_=bank[:, 0 : 2 * P].rearrange("p (u r) -> p r u", u=2)
-            )
+            dst = pairs.rearrange("p (r u) -> p r u", u=2)
+            src = bank[:, 0 : 2 * P].rearrange("p (u r) -> p r u", u=2)
+            if on_scalar:
+                nc.scalar.copy(out=dst, in_=src)
+            else:
+                nc.vector.tensor_copy(out=dst, in_=src)
 
         def first_tile_quant(j):
             nc.vector.quantize_mx(
@@ -434,23 +437,24 @@ def tile_twotimehiddentangentkernel_x2_kernel(
                     in_=o_planes[32 * quad : 32 * quad + 4, :, :].bitcast(I32),
                 )
 
+        warm = keep.tile([P, 8], F32, name="warm")
+        nc.scalar.activation(out=warm[:, 0:1], in_=ident[:, 0:1], func=ACT.Sigmoid)
         tile_banks = [first_tile(j) for j in (0, 1)]
         second_bank = vector_bank("turn")
         transposes(X, 1, second_bank, (0,))
         b_bank = turn_vector(b_rows, "dve", 4)
         transposes(X, 1, second_bank, (1,))
-        first_tile_out(0, tile_banks[0])
-        permute(w_perm[X], w_raw[X], 0, 4)
+        for j in (0, 1):
+            first_tile_out(j, tile_banks[j], True)
+        permute(w_perm[X], w_raw[X], 0, 8)
         first_tile_quant(0)
-        first_tile_out(1, tile_banks[1])
         permute(plane_perm[X], plane_raw[X], 0, 8)
         first_tile_quant(1)
         vector_out(b_bank, bias2, 2.0)
-        turn_out(X, 1, False)
+        turn_out(X, 1, True)
         z_mm(0, (0, 1, 2))
         z_mm(0, (3,))
         v_bank = turn_vector(v_rows, "dve", 4)
-        permute(w_perm[X], w_raw[X], 4, 8)
         quant_in(X, 1)
         vector_out(v_bank, minus4v, -4.0)
         vector_out(v_bank, plus4v, 4.0)

@@ -98,8 +98,8 @@ def tile_twotimehiddentangentkernel_x2_kernel(
             )
 
         load_rows(X, 0, 1)
-        load_words(X)
         load_rows(X, 1, 1)
+        load_words(X)
         load_scales(X)
         load_vector(b_rows, 0, b)
         load_vector(v_rows, 8 * X, va)
@@ -440,10 +440,14 @@ def tile_twotimehiddentangentkernel_x2_kernel(
         warm = keep.tile([P, 8], F32, name="warm")
         nc.scalar.activation(out=warm[:, 0:1], in_=ident[:, 0:1], func=ACT.Sigmoid)
         tile_banks = [first_tile(j) for j in (0, 1)]
-        second_bank = vector_bank("turn")
-        transposes(X, 1, second_bank, (0,))
+        dealt = keep.tile([P, 2, 2, P], I32, name="dealt", align_bytes=64)
+        nc.vector.tensor_copy(out=dealt[:], in_=raw[X, 1].bitcast(I32).rearrange("p j (r u) -> p j u r", u=2))
+        turned[X, 1] = vector_bank("turn")
+        for j in (0, 1):
+            for u in (0, 1):
+                col = P * (2 * j + u)
+                nc.tensor.transpose(turned[X, 1][:, col : col + P], dealt[:, j, u, :].bitcast(F32), ident[:])
         b_bank = turn_vector(b_rows, "dve", 4)
-        transposes(X, 1, second_bank, (1,))
         for j in (0, 1):
             first_tile_out(j, tile_banks[j], True)
         permute(w_perm[X], w_raw[X], 0, 8)
@@ -495,11 +499,11 @@ def tile_twotimehiddentangentkernel_x2_kernel(
         z_mm(5, (2, 3))
         product(4)
         sigmoid(5, BANKS)
-        factor(nc.gpsimd, 5, 0, (0, 1))
+        factor(nc.gpsimd, 5, 0, (0, 1, 2))
         z_mm(6, (0, 1))
         hadamard(0, BANKS)
         turn(Y, 3, False)
-        factor(nc.vector, 5, 0, (2, 3))
+        factor(nc.vector, 5, 0, (3,))
         quant_d(4)
         narrow_stage(6, 0)
         z_mm(6, (2, 3))

@@ -23,17 +23,20 @@ SCALE = 1.0 / (F ** 0.5 * D ** 0.5)
 X, Y = 0, 1
 BANKS = range(4)
 
-
-UNITS = [[(X, 0, 0, CHUNK), (X, 0, CHUNK, CHUNK)], [(X, 1, 0, BANK)]] + [
-    [(side, g, token, BANK)] for side, token in ((Y, 0), (X, BANK)) for g in (0, 1)
-] + [[(Y, g, CHUNK * chunk, CHUNK) for g in (0, 1)] for chunk in (2, 3)]
+UNITS = (
+    [[(X, 0, 0, CHUNK), (X, 0, CHUNK, CHUNK)], [(X, 1, 0, BANK)]]
+    + [[(side, g, token, BANK)] for side, token in ((Y, 0), (X, BANK)) for g in (0, 1)]
+    + [[(Y, g, CHUNK * chunk, CHUNK) for g in (0, 1)] for chunk in (2, 3)]
+)
 FIRST_UNIT_BANKS = [
     [(0, t, P * j, P) for t in slots] for j, slots in ((0, (0,)), (0, (1, 2, 3)), (1, (0, 1)), (1, (2, 3)))
 ] + [[(1, t, 0, CHUNK) for t in slots] for slots in ((0,), (1, 2), (3,))]
 BLOCKS = [[(0, 0), (0, 1)], [(1, 0), (1, 1)], [(0, 2), (1, 2)], [(0, 3), (1, 3)]]
+SCALAR_SLOTS, VECTOR_SLOTS = (0, 2), (1, 3)
+POOL_SLOTS = (1, 2, 3)
 SIG_BUFS = 4
-POOL_COLS = 64
 O16_BUFS = 4
+
 
 def tile_twotimehiddentangentkernel_x2_kernel(
     tc, x, y, wa_words, wa_scales, wb_words, wb_scales, b, va, vb, out_0, out_1, out_2
@@ -51,18 +54,23 @@ def tile_twotimehiddentangentkernel_x2_kernel(
         def vector_bank(name):
             return psum.tile([P, BANK], F32, name=name, tag="dve", bufs=4)
 
+        warm = keep.tile([P, 8], F32, name="warm")
+        nc.vector.memset(warm[:, 0:1], 0.0)
+        nc.scalar.activation(out=warm[:, 1:2], in_=warm[:, 0:1], func=ACT.Sigmoid)
+
         plane_raw = [keep.tile([P, F], U8, name="plane_raw%d" % side, align_bytes=64) for side in (X, Y)]
-        for side in (X, Y):
-            nc.vector.memset(plane_raw[side][:].bitcast(I32), 0)
+        nc.vector.memset(plane_raw[X][:].bitcast(I32), 0)
         b_rows = keep.tile([P, P], BF16, name="b_rows", align_bytes=64)
         v_rows = keep.tile([P, P], BF16, name="v_rows", align_bytes=64)
         nc.vector.memset(b_rows[:], 0.0)
         nc.vector.memset(v_rows[:], 0.0)
 
         ident = keep.tile([P, P], F32, name="ident", align_bytes=64)
-        make_identity(nc, ident[:])
+        nc.vector.memset(ident[:], 0.0)
+        make_identity(nc, ident[:], nomemset=True)
         ident16 = keep.tile([P, P], BF16, name="ident16", align_bytes=64)
         nc.vector.tensor_copy(out=ident16[:], in_=ident[:])
+        nc.vector.memset(plane_raw[Y][:].bitcast(I32), 0)
 
         raw = {}
 
@@ -110,10 +118,10 @@ def tile_twotimehiddentangentkernel_x2_kernel(
         for side in (X, Y):
             load_rows(side, 2, 2)
 
-        def permute(dst, src, r0, r1):
+        def permute(dst, src):
             nc.vector.tensor_copy(
-                out=dst[:].bitcast(I32).rearrange("p (r q i) -> p r q i", r=8, q=16)[:, r0:r1, :, :],
-                in_=src[:].bitcast(I32).rearrange("p (q r i) -> p r q i", r=8, q=16)[:, r0:r1, :, :],
+                out=dst[:].bitcast(I32).rearrange("p (r q i) -> p r q i", r=8, q=16),
+                in_=src[:].bitcast(I32).rearrange("p (q r i) -> p r q i", r=8, q=16),
             )
 
         turned = {}
@@ -121,9 +129,9 @@ def tile_twotimehiddentangentkernel_x2_kernel(
         codes = [keep.tile([P, N], U32, name="codes%d" % side, align_bytes=64) for side in (X, Y)]
         planes = [keep.tile([P, N], U8, name="planes%d" % side, align_bytes=64) for side in (X, Y)]
 
-        def transposes(side, chunk, bank, tiles=(0, 1)):
+        def transposes(side, chunk, bank):
             turned[side, chunk] = bank
-            for j in tiles:
+            for j in (0, 1):
                 pairs = raw[side, chunk][:, j, :].bitcast(F32)
                 for u in (0, 1):
                     col = P * (2 * j + u)
@@ -145,14 +153,11 @@ def tile_twotimehiddentangentkernel_x2_kernel(
                 nc.tensor.transpose(bank[:, P * u : P * (u + 1)], pairs[:, u : D // 2 : 2], ident[:])
             return bank
 
-        def first_tile_out(j, bank, on_scalar):
+        def first_tile_out(j, bank):
             pairs = grouped[X][:, 4 * P * j : 4 * P * (j + 1)].bitcast(F32)
-            dst = pairs.rearrange("p (r u) -> p r u", u=2)
-            src = bank[:, 0 : 2 * P].rearrange("p (u r) -> p r u", u=2)
-            if on_scalar:
-                nc.scalar.copy(out=dst, in_=src)
-            else:
-                nc.vector.tensor_copy(out=dst, in_=src)
+            nc.scalar.copy(
+                out=pairs.rearrange("p (r u) -> p r u", u=2), in_=bank[:, 0 : 2 * P].rearrange("p (u r) -> p r u", u=2)
+            )
 
         def first_tile_quant(j):
             nc.vector.quantize_mx(
@@ -160,6 +165,15 @@ def tile_twotimehiddentangentkernel_x2_kernel(
                 scales=planes[X][:, P * j : P * (j + 1)],
                 in_=grouped[X][:, 4 * P * j : 4 * P * (j + 1)],
             )
+
+        def dealt_transposes(side, chunk):
+            dealt = keep.tile([P, 2, 2, P], I32, name="dealt", align_bytes=64)
+            nc.vector.tensor_copy(out=dealt[:], in_=raw[side, chunk].bitcast(I32).rearrange("p j (r u) -> p j u r", u=2))
+            turned[side, chunk] = vector_bank("turn")
+            for j in (0, 1):
+                for u in (0, 1):
+                    col = P * (2 * j + u)
+                    nc.tensor.transpose(turned[side, chunk][:, col : col + P], dealt[:, j, u, :].bitcast(F32), ident[:])
 
         def turn(side, chunk, on_scalar):
             transposes(side, chunk, (scalar_bank if on_scalar else vector_bank)("turn"))
@@ -177,8 +191,8 @@ def tile_twotimehiddentangentkernel_x2_kernel(
         minus4v = keep.tile([P, 16], F32, name="minus4v")
         plus4v = keep.tile([P, 16], F32, name="plus4v")
 
-        def turn_vector(rows, tag, bufs):
-            bank = psum.tile([P, 2 * BANK], BF16, name="vbank", tag=tag, bufs=bufs)
+        def turn_vector(rows):
+            bank = psum.tile([P, 2 * BANK], BF16, name="vbank", tag="dve", bufs=4)
             nc.tensor.transpose(bank[:, 0:P], rows[:], ident16[:])
             return bank
 
@@ -187,20 +201,26 @@ def tile_twotimehiddentangentkernel_x2_kernel(
                 out=dst[:], in0=bank[:, 0 : dst.shape[1]], scalar1=times, scalar2=None, op0=ALU.mult
             )
 
-        z_banks, sig, fac, squares, d16, d_codes, d_planes, d_at = {}, {}, {}, {}, {}, {}, {}, {}
+        z_banks, sig, fac, d16, d_codes, d_planes, d_at = {}, {}, {}, {}, {}, {}, {}
 
         def slots_in_bank(u, k):
-            each = len(UNITS[u])
-            chosen = FIRST_UNIT_BANKS[k] if u == 0 else [divmod(s, 4) + (0, BANK // each) for s in range(each * k, each * (k + 1))]
+            if u == 0:
+                chosen = FIRST_UNIT_BANKS[k]
+            else:
+                each = len(UNITS[u])
+                chosen = [divmod(s, 4) + (0, BANK // each) for s in range(each * k, each * (k + 1))]
             return [(part, t, slice(c, c + w), slice(w * i, w * (i + 1))) for i, (part, t, c, w) in enumerate(chosen)]
 
-        def planes_of(tile, u, part):
-            width = UNITS[u][part][3]
-            return tile[:].rearrange("p (t n) -> p t n", t=4)[:, :, width * part : width * (part + 1)]
+        def four_slots(tile):
+            return tile[:].rearrange("p (t n) -> p t n", t=4)
 
-        def z_mm(u, banks, bank=scalar_bank):
+        def part_of(tile, u, part):
+            width = UNITS[u][part][3]
+            return four_slots(tile)[:, :, width * part : width * (part + 1)]
+
+        def z_mm(u, banks):
             for k in banks:
-                z = bank("z")
+                z = scalar_bank("z")
                 z_banks[u, k] = z
                 for part, t, cols, at in slots_in_bank(u, k):
                     side, g, token, width = UNITS[u][part]
@@ -223,39 +243,36 @@ def tile_twotimehiddentangentkernel_x2_kernel(
                 for part, t, cols, at in slots_in_bank(u, k):
                     r = 4 * UNITS[u][part][1] + t
                     nc.scalar.activation(
-                        out=planes_of(sig[u], u, part)[:, t, cols], in_=z_banks[u, k][:, at], func=ACT.Sigmoid,
+                        out=part_of(sig[u], u, part)[:, t, cols], in_=z_banks[u, k][:, at], func=ACT.Sigmoid,
                         bias=bias2[:, r : r + 1], scale=2.0,
                     )
 
-        def stage(u, staged=0):
-            for k in BANKS:
-                if k >= staged:
-                    z_mm(u, (k,))
-                sigmoid(u, (k,))
+        run0 = keep.tile([P, 5 * BANK], F32, name="run0", align_bytes=64)
 
-        def factor_tile(u, part):
-            if u == 7 and (u, part) not in fac:
-                fac[u, part] = work.tile([P, 4, CHUNK], F32, name="fac", tag="fac7" if part == 0 else "fac7b", bufs=1, align_bytes=64)
-            if u != 7 and u not in fac:
-                tag, bufs = ("fac4", 1) if u in (4, 5) else ("fac6", 1) if u == 6 else ("fac", 2)
+        def factor_part(u, part):
+            if u == 7:
+                if (u, part) not in fac:
+                    tag = ("run2", "fac_last")[part]
+                    fac[u, part] = work.tile([P, 4, CHUNK], F32, name="fac", tag=tag, bufs=1, align_bytes=64)
+                return fac[u, part][:]
+            if u in (4, 5):
+                fac[u] = run0[:, BANK * (5 - u) : BANK * (9 - u)]
+            if u not in fac:
+                tag, bufs = ("fac", 2) if u < 4 else ("run1", 1)
                 fac[u] = work.tile([P, 4 * BANK], F32, name="fac", tag=tag, bufs=bufs, align_bytes=64)
-
-        def factor_planes(u, part):
-            return fac[u, part][:] if u == 7 else planes_of(fac[u], u, part)
+            return part_of(fac[u], u, part)
 
         def scalar_factor(u, t, part=0):
             side, g, token, width = UNITS[u][part]
-            factor_tile(u, part)
             c = 8 * side + 4 * g + t
             nc.scalar.activation(
-                out=factor_planes(u, part)[:, t, :], in_=planes_of(sig[u], u, part)[:, t, :], func=ACT.Identity,
+                out=factor_part(u, part)[:, t, :], in_=part_of(sig[u], u, part)[:, t, :], func=ACT.Identity,
                 bias=plus4v[:, c : c + 1], scale=minus4v[:, c : c + 1],
             )
 
-        def shared_stage(u, scalar_slots):
+        def wide_stage(u, scalar_slots):
             for pair in ((0, 1), (2, 3)):
-                for k in pair:
-                    z_mm(u, (k,), scalar_bank)
+                z_mm(u, pair)
                 sigmoid(u, pair)
                 for t in pair:
                     if t in scalar_slots:
@@ -268,11 +285,10 @@ def tile_twotimehiddentangentkernel_x2_kernel(
 
         def factor(engine, u, part, slots):
             side, g, token, width = UNITS[u][part]
-            factor_tile(u, part)
             for t in slots:
                 c = 8 * side + 4 * g + t
                 engine.tensor_scalar(
-                    out=factor_planes(u, part)[:, t, :], in0=planes_of(sig[u], u, part)[:, t, :],
+                    out=factor_part(u, part)[:, t, :], in0=part_of(sig[u], u, part)[:, t, :],
                     scalar1=minus4v[:, c : c + 1], scalar2=plus4v[:, c : c + 1], op0=ALU.mult, op1=ALU.add,
                 )
 
@@ -283,7 +299,7 @@ def tile_twotimehiddentangentkernel_x2_kernel(
             return tile16.rearrange("p (c i) t -> p c t i", i=RUN)
 
         def new_d16(u):
-            tag, bufs = ("relay%d" % u, 1) if u == 5 else ("d16", 2)
+            tag, bufs = ("d16_extra", 1) if u == 5 else ("d16", 2)
             d16[u] = work.tile([P, BANK, 4], BF16, name="d16", tag=tag, bufs=bufs, align_bytes=64)
 
         def product(u, part=0):
@@ -292,16 +308,9 @@ def tile_twotimehiddentangentkernel_x2_kernel(
                 new_d16(u)
             nc.vector.tensor_tensor(
                 out=into_words(d16[u][:, width * part : width * (part + 1), :]),
-                in0=by_runs(planes_of(sig[u], u, part)),
-                in1=by_runs(factor_planes(u, part)),
+                in0=by_runs(part_of(sig[u], u, part)),
+                in1=by_runs(factor_part(u, part)),
                 op=ALU.mult,
-            )
-
-        def whole_product(u):
-            new_d16(u)
-            nc.vector.tensor_tensor(
-                out=into_words(d16[u][:]), in0=by_runs(sig[u][:].rearrange("p (t n) -> p t n", t=4)),
-                in1=by_runs(fac[u][:].rearrange("p (t n) -> p t n", t=4)), op=ALU.mult,
             )
 
         def quant_d(u, halves=(0, 1)):
@@ -329,9 +338,9 @@ def tile_twotimehiddentangentkernel_x2_kernel(
             h, j = BLOCKS[n][k // 2]
             return [(h, 2 * (k % 2) + i, CHUNK * j, CHUNK) for i in (0, 1)]
 
-        def base_mm(n, banks, bank=scalar_bank):
+        def base_mm(n, banks):
             for k in banks:
-                base_banks[n, k] = bank("base")
+                base_banks[n, k] = scalar_bank("base")
                 for i, (h, t, col, width) in enumerate(tiles_in_bank(n, k)):
                     rows = slice(BANK * h + P * t, BANK * h + P * (t + 1))
                     nc.tensor.matmul_mx(
@@ -349,12 +358,12 @@ def tile_twotimehiddentangentkernel_x2_kernel(
                 base_sb[n, k] = work.tile([P, BANK], F32, name="base_sb", tag="base_sb", bufs=8, align_bytes=64)
                 nc.scalar.activation(out=base_sb[n, k][:], in_=base_banks[n, k][:], func=ACT.Copy, scale=SCALE)
 
-        def gram_mm(n, banks, passes, bank=vector_bank):
+        def gram_mm(n, banks, passes):
             for k in banks:
                 tiles = tiles_in_bank(n, k)
                 for g in passes:
                     if g == 0:
-                        gram_banks[n, k] = bank("gram")
+                        gram_banks[n, k] = vector_bank("gram")
                     for i, (h, t, col, width) in enumerate(tiles):
                         ux, cx = d_at[X, g, BANK * h + P * t]
                         uy, cy = d_at[Y, g, col]
@@ -373,7 +382,9 @@ def tile_twotimehiddentangentkernel_x2_kernel(
                 tiles = tiles_in_bank(n, k)
                 h, t0, col, width = tiles[0]
                 if t0 == 0:
-                    whole = work.tile([P, 4, width], F32, name="o32", tag="o32_%d" % width, bufs=2 if n < 2 else 4, align_bytes=64)
+                    whole = work.tile(
+                        [P, 4, width], F32, name="o32", tag="o32_%d" % width, bufs=2 if n < 2 else 4, align_bytes=64
+                    )
                     o32[h, col, width] = whole
                     for i in range(width // CHUNK):
                         o32[h, col // CHUNK + i] = whole[:, :, chunk_cols(i)]
@@ -384,37 +395,36 @@ def tile_twotimehiddentangentkernel_x2_kernel(
                 rows = out_0[BANK * h : BANK * (h + 1), col : col + width].rearrange("(p t) m -> p t m", t=4)
                 nc.sync.dma_start(out=rows[:, t0 : t0 + len(tiles), :], in_=slots)
 
-        def scalar_cast(h, j, cols=slice(0, CHUNK)):
-            if (h, j) not in o16:
-                o16[h, j] = work.tile([P, CHUNK, 4], BF16, name="o16", tag="o16", bufs=O16_BUFS, align_bytes=64)
-            nc.scalar.copy(out=into_words(o16[h, j][:, cols, :]), in_=by_runs(o32[h, j][:, :, cols]))
-
-        def vector_cast(h, j):
-            o16[h, j] = work.tile([P, CHUNK, 4], BF16, name="o16", tag="o16", bufs=O16_BUFS, align_bytes=64)
-            nc.vector.tensor_copy(out=into_words(o16[h, j][:]), in_=by_runs(o32[h, j][:]))
-
-        def pool_cast(h, j, tag="o16", bufs=O16_BUFS, cols=slice(0, CHUNK)):
+        def o16_tile(h, j, tag="o16", bufs=O16_BUFS):
             if (h, j) not in o16:
                 o16[h, j] = work.tile([P, CHUNK, 4], BF16, name="o16", tag=tag, bufs=bufs, align_bytes=64)
+            return o16[h, j][:]
+
+        def relay_tile(n, tag):
+            pair = work.tile([P, 2 * CHUNK, 4], BF16, name="o16pair", tag=tag, bufs=1, align_bytes=64)
+            for i, piece in enumerate(BLOCKS[n]):
+                o16[piece] = pair[:, chunk_cols(i), :]
+
+        def scalar_cast(h, j):
+            nc.scalar.copy(out=into_words(o16_tile(h, j)), in_=by_runs(o32[h, j][:]))
+
+        def vector_cast(h, j):
+            nc.vector.tensor_copy(out=into_words(o16_tile(h, j)), in_=by_runs(o32[h, j][:]))
+
+        def pool_cast(h, j, *buffer):
             nc.gpsimd.tensor_scalar(
-                out=o16[h, j][:, cols, :], in0=o32[h, j][:, :, cols].rearrange("p t c -> p c t"),
+                out=o16_tile(h, j, *buffer), in0=o32[h, j][:].rearrange("p t c -> p c t"),
                 scalar1=1.0, scalar2=0.0, op0=ALU.mult, op1=ALU.add,
             )
 
         o_codes = keep.tile([P, 2, M], U32, name="o_codes", align_bytes=64)
-        o_planes = keep.tile([P, 2, M], U8, name="o_planes", align_bytes=64)
+        o_planes = keep.tile([P, M], U8, name="o_planes", align_bytes=64)
 
-        def pair_tile(h, j, tag):
-            o16[h, j, 2] = work.tile([P, 2 * CHUNK, 4], BF16, name="o16pair", tag=tag, bufs=1, align_bytes=64)
-            for i in (0, 1):
-                o16[h, j + i] = o16[h, j, 2][:, chunk_cols(i), :]
-
-        def quant_o(h, j, pieces=1):
-            cols = slice(CHUNK * j, CHUNK * (j + pieces))
+        def quant_o(h, j):
             nc.vector.quantize_mx(
-                out=o_codes[:, h, cols].bitcast(FP8X4),
-                scales=o_planes[:, h, cols],
-                in_=(o16[h, j] if pieces == 1 else o16[h, j, 2])[:].rearrange("p n t -> p (n t)"),
+                out=o_codes[:, h, chunk_cols(j)].bitcast(FP8X4),
+                scales=o_planes[4 * h :, chunk_cols(j)],
+                in_=o16[h, j][:].rearrange("p n t -> p (n t)"),
             )
 
         def store_words(h, j0, j1):
@@ -424,41 +434,27 @@ def tile_twotimehiddentangentkernel_x2_kernel(
                 in_=o_codes[:, h, cols].bitcast(I32),
             )
 
-        def store_both(j):
-            nc.sync.dma_start(
-                out=out_1[:, :, chunk_cols(j), :].rearrange("h p m t -> p h (m t)").bitcast(I32),
-                in_=o_codes[:, :, chunk_cols(j)].bitcast(I32),
-            )
-
         def store_scales():
             for quad in range(4):
-                (nc.scalar, nc.sync)[quad % 2].dma_start(
-                    out=out_2[:, 4 * quad : 4 * quad + 4, :].rearrange("h r m -> r h m").bitcast(I32),
-                    in_=o_planes[32 * quad : 32 * quad + 4, :, :].bitcast(I32),
+                nc.scalar.dma_start(
+                    out=out_2[:, 4 * quad : 4 * quad + 4, :].bitcast(I32),
+                    in_=o_planes[32 * quad : 32 * quad + 8, :].bitcast(I32),
                 )
 
-        warm = keep.tile([P, 8], F32, name="warm")
-        nc.scalar.activation(out=warm[:, 0:1], in_=ident[:, 0:1], func=ACT.Sigmoid)
+
         tile_banks = [first_tile(j) for j in (0, 1)]
-        dealt = keep.tile([P, 2, 2, P], I32, name="dealt", align_bytes=64)
-        nc.vector.tensor_copy(out=dealt[:], in_=raw[X, 1].bitcast(I32).rearrange("p j (r u) -> p j u r", u=2))
-        turned[X, 1] = vector_bank("turn")
+        dealt_transposes(X, 1)
+        b_bank = turn_vector(b_rows)
         for j in (0, 1):
-            for u in (0, 1):
-                col = P * (2 * j + u)
-                nc.tensor.transpose(turned[X, 1][:, col : col + P], dealt[:, j, u, :].bitcast(F32), ident[:])
-        b_bank = turn_vector(b_rows, "dve", 4)
-        for j in (0, 1):
-            first_tile_out(j, tile_banks[j], True)
-        permute(w_perm[X], w_raw[X], 0, 8)
+            first_tile_out(j, tile_banks[j])
+        permute(w_perm[X], w_raw[X])
         first_tile_quant(0)
-        permute(plane_perm[X], plane_raw[X], 0, 8)
+        permute(plane_perm[X], plane_raw[X])
         first_tile_quant(1)
         vector_out(b_bank, bias2, 2.0)
         turn_out(X, 1, True)
-        z_mm(0, (0, 1, 2))
-        z_mm(0, (3,))
-        v_bank = turn_vector(v_rows, "dve", 4)
+        z_mm(0, BANKS)
+        v_bank = turn_vector(v_rows)
         quant_in(X, 1)
         vector_out(v_bank, minus4v, -4.0)
         vector_out(v_bank, plus4v, 4.0)
@@ -469,42 +465,45 @@ def tile_twotimehiddentangentkernel_x2_kernel(
         for chunk in (0, 1):
             transposes(Y, chunk, vector_bank("turn"))
             turn_out(Y, chunk, True)
-        factor(nc.vector, 0, 0, (0, 1))
-        permute(plane_perm[Y], plane_raw[Y], 0, 8)
-        factor(nc.vector, 0, 0, (2, 3))
-        permute(w_perm[Y], w_raw[Y], 0, 8)
+        factor(nc.vector, 0, 0, range(4))
+        permute(plane_perm[Y], plane_raw[Y])
         product(0, 0)
-        factor(nc.vector, 0, 1, (0, 1, 2, 3))
+        factor(nc.vector, 0, 1, range(4))
+        permute(w_perm[Y], w_raw[Y])
         quant_in(Y, 0, 2)
         product(0, 1)
-        shared_stage(1, ())
+        wide_stage(1, ())
+
         for u, (side, chunk) in zip((1, 2, 3), ((X, 2), (X, 3), (Y, 2))):
             turn(side, chunk, True)
-            factor(nc.vector, u, 0, (0, 1, 2, 3) if u == 1 else (1, 3))
+            factor(nc.vector, u, 0, range(4) if u == 1 else VECTOR_SLOTS)
             quant_d(u - 1)
             if u > 1:
                 quant_in(side, 2, 2 if side == X else 1)
-            shared_stage(u + 1, (0, 2))
+            wide_stage(u + 1, SCALAR_SLOTS)
             if u == 3:
-                base_mm(0, (0, 1, 2))
-                base_mm(0, (3,))
+                base_mm(0, BANKS)
                 gram_mm(0, BANKS, (0,))
             product(u)
 
-        base_out(0, BANKS)
-        factor(nc.vector, 4, 0, (1, 3))
+        base_out(0, (0, 1))
+        factor(nc.vector, 4, 0, VECTOR_SLOTS)
         quant_d(3)
         z_mm(5, (0, 1))
         gram_mm(0, BANKS, (1,))
+        for k in (0, 1):
+            sigmoid(5, (k,))
+            base_out(0, (k + 2,))
         z_mm(5, (2, 3))
+        sigmoid(5, (2, 3))
         product(4)
-        sigmoid(5, BANKS)
-        factor(nc.gpsimd, 5, 0, (0, 1, 2))
+        factor(nc.vector, 5, 0, (0,))
+        factor(nc.gpsimd, 5, 0, POOL_SLOTS)
         z_mm(6, (0, 1))
         hadamard(0, BANKS)
         turn(Y, 3, False)
-        factor(nc.vector, 5, 0, (3,))
         quant_d(4)
+
         narrow_stage(6, 0)
         z_mm(6, (2, 3))
         base_mm(1, (0, 1))
@@ -520,49 +519,57 @@ def tile_twotimehiddentangentkernel_x2_kernel(
         z_mm(7, (1,))
         gram_mm(1, (2, 3), (1,))
         z_mm(7, (2, 3))
-        whole_product(6)
-        pair_tile(0, 0, "fac6")
+        for part in (0, 1):
+            product(6, part)
+        quant_d(6, (0,))
+        relay_tile(0, "run1")
         pool_cast(0, 0)
         narrow_stage(7, 0)
         base_mm(2, (0, 1))
         hadamard(1, BANKS)
-        quant_d(6)
-        quant_o(0, 0)
-        store_words(0, 0, 1)
+
+        quant_d(6, (1,))
+        base_out(2, (0, 1))
         for k in (0, 1):
-            base_out(2, (k,))
+            gram_mm(2, (k,), (0,))
             base_mm(2, (k + 2,))
-        gram_mm(2, BANKS, (0, 1))
+        gram_mm(2, (2, 3), (0,))
+        gram_mm(2, BANKS, (1,))
+        sigmoid(7, (2, 3))
         base_out(2, (2, 3))
-        narrow_stage(7, 1)
+        for t in range(4):
+            scalar_factor(7, t, 1)
         base_mm(3, BANKS)
         product(7, 0)
-        pair_tile(1, 0, "fac7")
+        quant_o(0, 0)
+        store_words(0, 0, 1)
+        relay_tile(1, "run2")
         pool_cast(1, 0)
         hadamard(2, BANKS)
-        for h in (0, 1):
+
+        for h in (1, 0):
             scalar_cast(h, 1)
         base_out(3, BANKS)
         scalar_cast(0, 2)
         quant_d(7, (0,))
         gram_mm(3, BANKS, (0,))
         product(7, 1)
-        quant_o(1, 0)
-        store_words(1, 0, 1)
+        quant_o(1, 1)
         quant_d(7, (1,))
         gram_mm(3, BANKS, (1,))
-        for h in (0, 1):
-            quant_o(h, 1)
-            store_words(h, 1, 2)
-        pool_cast(1, 2, "fac7", 1)
+        quant_o(1, 0)
+        store_words(1, 0, 2)
+        quant_o(0, 1)
+        store_words(0, 1, 2)
+        pool_cast(1, 2, "run2", 1)
         hadamard(3, (0, 1))
         scalar_cast(0, 3)
         hadamard(3, (2, 3))
         quant_o(1, 2)
         vector_cast(1, 3)
+        quant_o(0, 3)
         quant_o(0, 2)
+        store_words(0, 2, 4)
         quant_o(1, 3)
         store_words(1, 2, 4)
-        quant_o(0, 3)
-        store_words(0, 2, 4)
         store_scales()

@@ -28,12 +28,13 @@ UNITS = (
     + [[(side, g, token, BANK)] for side, token in ((Y, 0), (X, BANK)) for g in (0, 1)]
     + [[(Y, g, CHUNK * chunk, CHUNK) for g in (0, 1)] for chunk in (2, 3)]
 )
-FIRST_UNIT_BANKS = [
-    [(0, t, P * j, P) for t in slots] for j, slots in ((0, (0,)), (0, (1, 2, 3)), (1, (0, 1)), (1, (2, 3)))
-] + [[(1, t, 0, CHUNK) for t in slots] for slots in ((0,), (1, 2), (3,))]
+FIRST_UNIT_BANKS = [[(0, t, P * j, P) for t in slots] for j in (0, 1) for slots in ((0, 1), (2, 3))] + [
+    [(1, t, 0, CHUNK)] for t in range(4)
+]
 BLOCKS = [[(0, 0), (0, 1)], [(1, 0), (1, 1)], [(0, 2), (1, 2)], [(0, 3), (1, 3)]]
 SCALAR_SLOTS, VECTOR_SLOTS = (0, 2), (1, 3)
-POOL_SLOTS = (1, 2, 3)
+POOL_SLOTS = (0, 1, 2)
+POOL_COLS = 272
 SIG_BUFS = 4
 O16_BUFS = 4
 
@@ -247,18 +248,14 @@ def tile_twotimehiddentangentkernel_x2_kernel(
                         bias=bias2[:, r : r + 1], scale=2.0,
                     )
 
-        run0 = keep.tile([P, 5 * BANK], F32, name="run0", align_bytes=64)
-
         def factor_part(u, part):
             if u == 7:
                 if (u, part) not in fac:
                     tag = ("run2", "fac_last")[part]
                     fac[u, part] = work.tile([P, 4, CHUNK], F32, name="fac", tag=tag, bufs=1, align_bytes=64)
                 return fac[u, part][:]
-            if u in (4, 5):
-                fac[u] = run0[:, BANK * (5 - u) : BANK * (9 - u)]
             if u not in fac:
-                tag, bufs = ("fac", 2) if u < 4 else ("run1", 1)
+                tag, bufs = ("fac", 2) if u < 4 else ("run0", 1) if u < 6 else ("run1", 1)
                 fac[u] = work.tile([P, 4 * BANK], F32, name="fac", tag=tag, bufs=bufs, align_bytes=64)
             return part_of(fac[u], u, part)
 
@@ -404,6 +401,8 @@ def tile_twotimehiddentangentkernel_x2_kernel(
             pair = work.tile([P, 2 * CHUNK, 4], BF16, name="o16pair", tag=tag, bufs=1, align_bytes=64)
             for i, piece in enumerate(BLOCKS[n]):
                 o16[piece] = pair[:, chunk_cols(i), :]
+            o16[n, "pool"], o16[n, "rest"] = pair[:, :POOL_COLS, :], pair[:, POOL_COLS:, :]
+            o32[n, "pool"], o32[n, "rest"] = o32[n, 0, BANK][:, :, :POOL_COLS], o32[n, 0, BANK][:, :, POOL_COLS:]
 
         def scalar_cast(h, j):
             nc.scalar.copy(out=into_words(o16_tile(h, j)), in_=by_runs(o32[h, j][:]))
@@ -458,10 +457,10 @@ def tile_twotimehiddentangentkernel_x2_kernel(
         quant_in(X, 1)
         vector_out(v_bank, minus4v, -4.0)
         vector_out(v_bank, plus4v, 4.0)
-        for k in (0, 1, 2):
+        for k in BANKS:
             sigmoid(0, (k,))
             z_mm(0, (4 + k,))
-        sigmoid(0, (3, 4, 5, 6))
+        sigmoid(0, (4, 5, 6, 7))
         for chunk in (0, 1):
             transposes(Y, chunk, vector_bank("turn"))
             turn_out(Y, chunk, True)
@@ -486,22 +485,19 @@ def tile_twotimehiddentangentkernel_x2_kernel(
                 gram_mm(0, BANKS, (0,))
             product(u)
 
-        base_out(0, (0, 1))
+        base_out(0, BANKS)
         factor(nc.vector, 4, 0, VECTOR_SLOTS)
         quant_d(3)
         z_mm(5, (0, 1))
         gram_mm(0, BANKS, (1,))
-        for k in (0, 1):
-            sigmoid(5, (k,))
-            base_out(0, (k + 2,))
         z_mm(5, (2, 3))
-        sigmoid(5, (2, 3))
         product(4)
-        factor(nc.vector, 5, 0, (0,))
+        sigmoid(5, BANKS)
         factor(nc.gpsimd, 5, 0, POOL_SLOTS)
         z_mm(6, (0, 1))
         hadamard(0, BANKS)
         turn(Y, 3, False)
+        factor(nc.vector, 5, 0, [t for t in range(4) if t not in POOL_SLOTS])
         quant_d(4)
 
         narrow_stage(6, 0)
@@ -523,17 +519,15 @@ def tile_twotimehiddentangentkernel_x2_kernel(
             product(6, part)
         quant_d(6, (0,))
         relay_tile(0, "run1")
-        pool_cast(0, 0)
+        pool_cast(0, "pool")
         narrow_stage(7, 0)
         base_mm(2, (0, 1))
         hadamard(1, BANKS)
 
         quant_d(6, (1,))
         base_out(2, (0, 1))
-        for k in (0, 1):
-            gram_mm(2, (k,), (0,))
-            base_mm(2, (k + 2,))
-        gram_mm(2, (2, 3), (0,))
+        gram_mm(2, BANKS, (0,))
+        base_mm(2, (2, 3))
         gram_mm(2, BANKS, (1,))
         sigmoid(7, (2, 3))
         base_out(2, (2, 3))
@@ -544,32 +538,32 @@ def tile_twotimehiddentangentkernel_x2_kernel(
         quant_o(0, 0)
         store_words(0, 0, 1)
         relay_tile(1, "run2")
-        pool_cast(1, 0)
+        pool_cast(1, "pool")
         hadamard(2, BANKS)
 
-        for h in (1, 0):
-            scalar_cast(h, 1)
+        for h in (0, 1):
+            scalar_cast(h, "rest")
         base_out(3, BANKS)
         scalar_cast(0, 2)
         quant_d(7, (0,))
         gram_mm(3, BANKS, (0,))
         product(7, 1)
-        quant_o(1, 1)
-        quant_d(7, (1,))
-        gram_mm(3, BANKS, (1,))
-        quant_o(1, 0)
-        store_words(1, 0, 2)
         quant_o(0, 1)
         store_words(0, 1, 2)
+        quant_d(7, (1,))
+        gram_mm(3, BANKS, (1,))
+        for j in (0, 1):
+            quant_o(1, j)
+            store_words(1, j, j + 1)
         pool_cast(1, 2, "run2", 1)
         hadamard(3, (0, 1))
         scalar_cast(0, 3)
         hadamard(3, (2, 3))
-        quant_o(1, 2)
         vector_cast(1, 3)
-        quant_o(0, 3)
-        quant_o(0, 2)
-        store_words(0, 2, 4)
-        quant_o(1, 3)
+        for j in (2, 3):
+            quant_o(1, j)
         store_words(1, 2, 4)
+        for j in (2, 3):
+            quant_o(0, j)
+            store_words(0, j, j + 1)
         store_scales()

@@ -111,9 +111,9 @@ def tile_twotimehiddentangentkernel_x2_kernel(
         load_words(X)
         load_scales(X)
         load_vector(b_rows, 0, b)
-        load_vector(v_rows, 8 * X, va)
-        load_vector(v_rows, 8 * Y, vb)
+        load_vector(b_rows, 8, va)
         load_rows(Y, 0, 2)
+        load_vector(v_rows, 0, vb)
         load_scales(Y)
         load_words(Y)
         for side in (X, Y):
@@ -197,9 +197,9 @@ def tile_twotimehiddentangentkernel_x2_kernel(
             nc.tensor.transpose(bank[:, 0:P], rows[:], ident16[:])
             return bank
 
-        def vector_out(bank, dst, times):
+        def vector_out(bank, first, dst, times):
             nc.vector.tensor_scalar(
-                out=dst[:], in0=bank[:, 0 : dst.shape[1]], scalar1=times, scalar2=None, op0=ALU.mult
+                out=dst, in0=bank[:, first : first + 8], scalar1=times, scalar2=None, op0=ALU.mult
             )
 
         z_banks, sig, fac, d16, d_codes, d_planes, d_at = {}, {}, {}, {}, {}, {}, {}
@@ -219,9 +219,9 @@ def tile_twotimehiddentangentkernel_x2_kernel(
             width = UNITS[u][part][3]
             return four_slots(tile)[:, :, width * part : width * (part + 1)]
 
-        def z_mm(u, banks):
+        def z_mm(u, banks, new_bank=scalar_bank):
             for k in banks:
-                z = scalar_bank("z")
+                z = new_bank("z")
                 z_banks[u, k] = z
                 for part, t, cols, at in slots_in_bank(u, k):
                     side, g, token, width = UNITS[u][part]
@@ -450,28 +450,36 @@ def tile_twotimehiddentangentkernel_x2_kernel(
         first_tile_quant(0)
         permute(plane_perm[X], plane_raw[X])
         first_tile_quant(1)
-        vector_out(b_bank, bias2, 2.0)
+        vector_out(b_bank, 0, bias2[:], 2.0)
+        vector_out(b_bank, 8, minus4v[:, 0:8], -4.0)
+        vector_out(b_bank, 8, plus4v[:, 0:8], 4.0)
         turn_out(X, 1, True)
         z_mm(0, BANKS)
-        v_bank = turn_vector(v_rows)
         quant_in(X, 1)
-        vector_out(v_bank, minus4v, -4.0)
-        vector_out(v_bank, plus4v, 4.0)
         for k in BANKS:
             sigmoid(0, (k,))
             z_mm(0, (4 + k,))
+        z_mm(1, (0,), vector_bank)
         sigmoid(0, (4, 5, 6, 7))
         for chunk in (0, 1):
             transposes(Y, chunk, vector_bank("turn"))
-            turn_out(Y, chunk, True)
+        v_bank = turn_vector(v_rows)
+        z_mm(1, (1, 2, 3))
+        sigmoid(1, (0,))
+
+        turn_out(Y, 1, True)
+        sigmoid(1, (1, 2, 3))
         factor(nc.vector, 0, 0, range(4))
         permute(plane_perm[Y], plane_raw[Y])
         product(0, 0)
+        turn_out(Y, 0, False)
         factor(nc.vector, 0, 1, range(4))
         permute(w_perm[Y], w_raw[Y])
+
+        vector_out(v_bank, 0, minus4v[:, 8:16], -4.0)
+        vector_out(v_bank, 0, plus4v[:, 8:16], 4.0)
         quant_in(Y, 0, 2)
         product(0, 1)
-        wide_stage(1, ())
 
         for u, (side, chunk) in zip((1, 2, 3), ((X, 2), (X, 3), (Y, 2))):
             turn(side, chunk, True)

@@ -32,7 +32,7 @@ FIRST_UNIT_BANKS = [[(0, t, P * j, P) for t in slots] for j in (0, 1) for slots 
     [(1, t, 0, CHUNK)] for t in range(4)
 ]
 BLOCKS = [[(0, 0), (0, 1)], [(1, 0), (1, 1)], [(0, 2), (1, 2)], [(0, 3), (1, 3)]]
-SCALAR_SLOTS, VECTOR_SLOTS = (0, 2), (1, 3)
+ON_SCALAR = {1: (), 2: (0,), 3: (0, 2), 4: (0, 2)}
 POOL_SLOTS = (0, 1, 2)
 POOL_COLS = 272
 SIG_BUFS = 4
@@ -112,10 +112,10 @@ def tile_twotimehiddentangentkernel_x2_kernel(
         load_scales(X)
         load_vector(b_rows, 0, b)
         load_vector(b_rows, 8, va)
-        load_rows(Y, 0, 2)
-        load_vector(v_rows, 0, vb)
-        load_scales(Y)
         load_words(Y)
+        load_rows(Y, 0, 2)
+        load_scales(Y)
+        load_vector(v_rows, 0, vb)
         for side in (X, Y):
             load_rows(side, 2, 2)
 
@@ -435,7 +435,7 @@ def tile_twotimehiddentangentkernel_x2_kernel(
 
         def store_scales():
             for quad in range(4):
-                nc.scalar.dma_start(
+                (nc.scalar, nc.sync)[quad % 2].dma_start(
                     out=out_2[:, 4 * quad : 4 * quad + 4, :].bitcast(I32),
                     in_=o_planes[32 * quad : 32 * quad + 8, :].bitcast(I32),
                 )
@@ -456,6 +456,7 @@ def tile_twotimehiddentangentkernel_x2_kernel(
         turn_out(X, 1, True)
         z_mm(0, BANKS)
         quant_in(X, 1)
+        permute(w_perm[Y], w_raw[Y])
         for k in BANKS:
             sigmoid(0, (k,))
             z_mm(0, (4 + k,))
@@ -474,7 +475,6 @@ def tile_twotimehiddentangentkernel_x2_kernel(
         product(0, 0)
         turn_out(Y, 0, False)
         factor(nc.vector, 0, 1, range(4))
-        permute(w_perm[Y], w_raw[Y])
 
         vector_out(v_bank, 0, minus4v[:, 8:16], -4.0)
         vector_out(v_bank, 0, plus4v[:, 8:16], 4.0)
@@ -483,23 +483,24 @@ def tile_twotimehiddentangentkernel_x2_kernel(
 
         for u, (side, chunk) in zip((1, 2, 3), ((X, 2), (X, 3), (Y, 2))):
             turn(side, chunk, True)
-            factor(nc.vector, u, 0, range(4) if u == 1 else VECTOR_SLOTS)
+            factor(nc.vector, u, 0, [t for t in range(4) if t not in ON_SCALAR[u]])
             quant_d(u - 1)
-            if u > 1:
-                quant_in(side, 2, 2 if side == X else 1)
-            wide_stage(u + 1, SCALAR_SLOTS)
+            if u == 2:
+                quant_in(X, 2, 2)
+            wide_stage(u + 1, ON_SCALAR[u + 1])
             if u == 3:
                 base_mm(0, BANKS)
                 gram_mm(0, BANKS, (0,))
             product(u)
 
         base_out(0, BANKS)
-        factor(nc.vector, 4, 0, VECTOR_SLOTS)
+        factor(nc.vector, 4, 0, [t for t in range(4) if t not in ON_SCALAR[4]])
         quant_d(3)
         z_mm(5, (0, 1))
         gram_mm(0, BANKS, (1,))
         z_mm(5, (2, 3))
         product(4)
+        quant_in(Y, 2)
         sigmoid(5, BANKS)
         factor(nc.gpsimd, 5, 0, POOL_SLOTS)
         z_mm(6, (0, 1))
@@ -552,7 +553,6 @@ def tile_twotimehiddentangentkernel_x2_kernel(
         for h in (0, 1):
             scalar_cast(h, "rest")
         base_out(3, BANKS)
-        scalar_cast(0, 2)
         quant_d(7, (0,))
         gram_mm(3, BANKS, (0,))
         product(7, 1)
@@ -563,15 +563,22 @@ def tile_twotimehiddentangentkernel_x2_kernel(
         for j in (0, 1):
             quant_o(1, j)
             store_words(1, j, j + 1)
+        shared = o16_tile(0, 2)
+        for half, share in enumerate(("low", "high")):
+            cols = slice(P * half, P * (half + 1))
+            o16[0, share], o32[0, share] = shared[:, cols, :], o32[0, 2][:, :, cols]
+        vector_cast(0, "low")
         pool_cast(1, 2, "run2", 1)
         hadamard(3, (0, 1))
         scalar_cast(0, 3)
+        scalar_cast(0, "high")
         hadamard(3, (2, 3))
+        quant_o(1, 2)
+        store_words(1, 2, 3)
         vector_cast(1, 3)
-        for j in (2, 3):
-            quant_o(1, j)
-        store_words(1, 2, 4)
-        for j in (2, 3):
+        for j in (3, 2):
             quant_o(0, j)
-            store_words(0, j, j + 1)
+        store_words(0, 2, 4)
+        quant_o(1, 3)
+        store_words(1, 3, 4)
         store_scales()

@@ -32,7 +32,7 @@ FIRST_UNIT_BANKS = [[(0, t, P * j, P) for t in slots] for j in (0, 1) for slots 
     [(1, t, 0, CHUNK)] for t in range(4)
 ]
 BLOCKS = [[(0, 0), (0, 1)], [(1, 0), (1, 1)], [(0, 2), (1, 2)], [(0, 3), (1, 3)]]
-ON_SCALAR = {1: (), 2: (0,), 3: (0, 2), 4: (0, 2)}
+ON_SCALAR = {1: (), 2: (0, 2), 3: (0, 2), 4: (0, 2)}
 POOL_SLOTS = (0, 1, 2)
 POOL_COLS = 272
 SIG_BUFS = 4
@@ -284,10 +284,16 @@ def tile_twotimehiddentangentkernel_x2_kernel(
             side, g, token, width = UNITS[u][part]
             for t in slots:
                 c = 8 * side + 4 * g + t
-                engine.tensor_scalar(
-                    out=factor_part(u, part)[:, t, :], in0=part_of(sig[u], u, part)[:, t, :],
-                    scalar1=minus4v[:, c : c + 1], scalar2=plus4v[:, c : c + 1], op0=ALU.mult, op1=ALU.add,
-                )
+                if engine is nc.vector:
+                    engine.tensor_scalar(
+                        out=factor_part(u, part)[:, t, :], in0=part_of(sig[u], u, part)[:, t, :],
+                        scalar1=1.0, scalar2=minus4v[:, c : c + 1], op0=ALU.subtract, op1=ALU.mult,
+                    )
+                else:
+                    engine.tensor_scalar(
+                        out=factor_part(u, part)[:, t, :], in0=part_of(sig[u], u, part)[:, t, :],
+                        scalar1=minus4v[:, c : c + 1], scalar2=plus4v[:, c : c + 1], op0=ALU.mult, op1=ALU.add,
+                    )
 
         def by_runs(slots4):
             return slots4.rearrange("p t (c i) -> p c t i", i=RUN)
@@ -468,18 +474,20 @@ def tile_twotimehiddentangentkernel_x2_kernel(
         z_mm(1, (1, 2, 3))
         sigmoid(1, (0,))
 
+        turn_out(Y, 0, True)
         turn_out(Y, 1, True)
         sigmoid(1, (1, 2, 3))
+        for t in ON_SCALAR[1]:
+            scalar_factor(1, t)
         factor(nc.vector, 0, 0, range(4))
         permute(plane_perm[Y], plane_raw[Y])
         product(0, 0)
-        turn_out(Y, 0, False)
         factor(nc.vector, 0, 1, range(4))
 
         vector_out(v_bank, 0, minus4v[:, 8:16], -4.0)
         vector_out(v_bank, 0, plus4v[:, 8:16], 4.0)
-        quant_in(Y, 0, 2)
         product(0, 1)
+        quant_in(Y, 0, 2)
 
         for u, (side, chunk) in zip((1, 2, 3), ((X, 2), (X, 3), (Y, 2))):
             turn(side, chunk, True)

@@ -32,7 +32,7 @@ FIRST_UNIT_BANKS = [[(0, t, P * j, P) for t in slots] for j in (0, 1) for slots 
     [(1, t, 0, CHUNK)] for t in range(4)
 ]
 BLOCKS = [[(0, 0), (0, 1)], [(1, 0), (1, 1)], [(0, 2), (1, 2)], [(0, 3), (1, 3)]]
-ON_SCALAR = {1: (), 2: (0, 2), 3: (0, 2), 4: (0, 2)}
+ON_SCALAR = {1: (0,), 2: (0,), 3: (0, 2), 4: (0, 2)}
 POOL_SLOTS = (0, 1, 2)
 POOL_COLS = 272
 SIG_BUFS = 4
@@ -480,9 +480,10 @@ def tile_twotimehiddentangentkernel_x2_kernel(
         for t in ON_SCALAR[1]:
             scalar_factor(1, t)
         factor(nc.vector, 0, 0, range(4))
-        permute(plane_perm[Y], plane_raw[Y])
+        factor(nc.vector, 0, 1, (0,))
         product(0, 0)
-        factor(nc.vector, 0, 1, range(4))
+        factor(nc.vector, 0, 1, (1, 2, 3))
+        permute(plane_perm[Y], plane_raw[Y])
 
         vector_out(v_bank, 0, minus4v[:, 8:16], -4.0)
         vector_out(v_bank, 0, plus4v[:, 8:16], 4.0)

@@ -32,9 +32,9 @@ FIRST_UNIT_BANKS = [[(0, t, P * j, P) for t in slots] for j in (0, 1) for slots 
     [(1, t, 0, CHUNK)] for t in range(4)
 ]
 BLOCKS = [[(0, 0), (0, 1)], [(1, 0), (1, 1)], [(0, 2), (1, 2)], [(0, 3), (1, 3)]]
-ON_SCALAR = {1: (0,), 2: (0,), 3: (0, 2), 4: (0, 2)}
+ON_SCALAR = {1: (1,), 2: (0,), 3: (0, 2), 4: (0, 2)}
 POOL_SLOTS = (0, 1, 2)
-POOL_COLS = 272
+POOL_COLS = 296
 SIG_BUFS = 4
 O16_BUFS = 4
 
@@ -113,8 +113,8 @@ def tile_twotimehiddentangentkernel_x2_kernel(
         load_vector(b_rows, 0, b)
         load_vector(b_rows, 8, va)
         load_words(Y)
-        load_rows(Y, 0, 2)
         load_scales(Y)
+        load_rows(Y, 0, 2)
         load_vector(v_rows, 0, vb)
         for side in (X, Y):
             load_rows(side, 2, 2)
@@ -170,11 +170,12 @@ def tile_twotimehiddentangentkernel_x2_kernel(
         def dealt_transposes(side, chunk):
             dealt = keep.tile([P, 2, 2, P], I32, name="dealt", align_bytes=64)
             nc.vector.tensor_copy(out=dealt[:], in_=raw[side, chunk].bitcast(I32).rearrange("p j (r u) -> p j u r", u=2))
-            turned[side, chunk] = vector_bank("turn")
+            banks = []
             for j in (0, 1):
+                banks.append(scalar_bank("turn"))
                 for u in (0, 1):
-                    col = P * (2 * j + u)
-                    nc.tensor.transpose(turned[side, chunk][:, col : col + P], dealt[:, j, u, :].bitcast(F32), ident[:])
+                    nc.tensor.transpose(banks[j][:, P * u : P * (u + 1)], dealt[:, j, u, :].bitcast(F32), ident[:])
+            return banks
 
         def turn(side, chunk, on_scalar):
             transposes(side, chunk, (scalar_bank if on_scalar else vector_bank)("turn"))
@@ -448,9 +449,9 @@ def tile_twotimehiddentangentkernel_x2_kernel(
 
 
         tile_banks = [first_tile(j) for j in (0, 1)]
-        dealt_transposes(X, 1)
+        tile_banks = tile_banks + dealt_transposes(X, 1)
         b_bank = turn_vector(b_rows)
-        for j in (0, 1):
+        for j in range(4):
             first_tile_out(j, tile_banks[j])
         permute(w_perm[X], w_raw[X])
         first_tile_quant(0)
@@ -459,13 +460,14 @@ def tile_twotimehiddentangentkernel_x2_kernel(
         vector_out(b_bank, 0, bias2[:], 2.0)
         vector_out(b_bank, 8, minus4v[:, 0:8], -4.0)
         vector_out(b_bank, 8, plus4v[:, 0:8], 4.0)
-        turn_out(X, 1, True)
         z_mm(0, BANKS)
         quant_in(X, 1)
         permute(w_perm[Y], w_raw[Y])
-        for k in BANKS:
-            sigmoid(0, (k,))
-            z_mm(0, (4 + k,))
+        permute(plane_perm[Y], plane_raw[Y])
+        z_mm(0, (4, 5), vector_bank)
+        sigmoid(0, (0, 1))
+        z_mm(0, (6, 7))
+        sigmoid(0, (2, 3))
         z_mm(1, (0,), vector_bank)
         sigmoid(0, (4, 5, 6, 7))
         for chunk in (0, 1):
@@ -483,19 +485,24 @@ def tile_twotimehiddentangentkernel_x2_kernel(
         factor(nc.vector, 0, 1, (0,))
         product(0, 0)
         factor(nc.vector, 0, 1, (1, 2, 3))
-        permute(plane_perm[Y], plane_raw[Y])
 
         vector_out(v_bank, 0, minus4v[:, 8:16], -4.0)
         vector_out(v_bank, 0, plus4v[:, 8:16], 4.0)
+        factor(nc.vector, 1, 0, (0,))
         product(0, 1)
         quant_in(Y, 0, 2)
 
         for u, (side, chunk) in zip((1, 2, 3), ((X, 2), (X, 3), (Y, 2))):
             turn(side, chunk, True)
-            factor(nc.vector, u, 0, [t for t in range(4) if t not in ON_SCALAR[u]])
-            quant_d(u - 1)
+            slots = [t for t in range(u == 1, 4) if t not in ON_SCALAR[u]]
             if u == 2:
+                factor(nc.vector, u, 0, slots[:-1])
+                quant_d(u - 1)
+                factor(nc.vector, u, 0, slots[-1:])
                 quant_in(X, 2, 2)
+            else:
+                factor(nc.vector, u, 0, slots)
+                quant_d(u - 1)
             wide_stage(u + 1, ON_SCALAR[u + 1])
             if u == 3:
                 base_mm(0, BANKS)
@@ -574,7 +581,7 @@ def tile_twotimehiddentangentkernel_x2_kernel(
             store_words(1, j, j + 1)
         shared = o16_tile(0, 2)
         for half, share in enumerate(("low", "high")):
-            cols = slice(P * half, P * (half + 1))
+            cols = (slice(0, 160), slice(160, CHUNK))[half]
             o16[0, share], o32[0, share] = shared[:, cols, :], o32[0, 2][:, :, cols]
         vector_cast(0, "low")
         pool_cast(1, 2, "run2", 1)

@@ -442,7 +442,7 @@ def tile_twotimehiddentangentkernel_x2_kernel(
 
         def store_scales():
             for quad in range(4):
-                (nc.scalar, nc.sync)[quad % 2].dma_start(
+                nc.scalar.dma_start(
                     out=out_2[:, 4 * quad : 4 * quad + 4, :].bitcast(I32),
                     in_=o_planes[32 * quad : 32 * quad + 8, :].bitcast(I32),
                 )

@@ -32,9 +32,9 @@ FIRST_UNIT_BANKS = [[(0, t, P * j, P) for t in slots] for j in (0, 1) for slots 
     [(1, t, 0, CHUNK)] for t in range(4)
 ]
 BLOCKS = [[(0, 0), (0, 1)], [(1, 0), (1, 1)], [(0, 2), (1, 2)], [(0, 3), (1, 3)]]
-ON_SCALAR = {1: (1,), 2: (0,), 3: (0, 2), 4: (0, 2)}
+ON_SCALAR = {1: (1,), 2: (0,), 3: (0,), 4: (0, 2)}
 POOL_SLOTS = (0, 1, 2)
-POOL_COLS = 296
+POOL_COLS = 272
 SIG_BUFS = 4
 O16_BUFS = 4
 
@@ -586,12 +586,17 @@ def tile_twotimehiddentangentkernel_x2_kernel(
         vector_cast(0, "low")
         pool_cast(1, 2, "run2", 1)
         hadamard(3, (0, 1))
-        scalar_cast(0, 3)
         scalar_cast(0, "high")
+        scalar_cast(0, 3)
         hadamard(3, (2, 3))
         quant_o(1, 2)
         store_words(1, 2, 3)
-        vector_cast(1, 3)
+        last = o16_tile(1, 3)
+        for half, share in enumerate(("low", "high")):
+            cols = (slice(0, 176), slice(176, CHUNK))[half]
+            o16[1, share], o32[1, share] = last[:, cols, :], o32[1, 3][:, :, cols]
+        vector_cast(1, "low")
+        scalar_cast(1, "high")
         for j in (3, 2):
             quant_o(0, j)
         store_words(0, 2, 4)

from contextlib import ExitStack

import concourse.mybir as mybir
from concourse.masks import make_identity

F32 = mybir.dt.float32
BF16 = mybir.dt.bfloat16
I32 = mybir.dt.int32
U32 = mybir.dt.uint32
U8 = mybir.dt.uint8
FP8X4 = mybir.dt.float8_e4m3fn_x4
FP4X4 = mybir.dt.float4_e2m1fn_x4
ACT = mybir.ActivationFunctionType
ALU = mybir.AluOpType

N, M, D, F = 1024, 1024, 512, 1024
P = 128
BANK = 512
CHUNK = 256
RUN = 4
FLOPS = 2 * (N * D * F + M * D * F + N * D * M + N * F * M)
SCALE = 1.0 / (F ** 0.5 * D ** 0.5)
X, Y = 0, 1
BANKS = range(4)

UNITS = (
    [[(X, 0, 0, CHUNK), (X, 0, CHUNK, CHUNK)], [(X, 1, 0, BANK)]]
    + [[(side, g, token, BANK)] for side, token in ((Y, 0), (X, BANK)) for g in (0, 1)]
    + [[(Y, g, CHUNK * chunk, CHUNK) for g in (0, 1)] for chunk in (2, 3)]
)
FIRST_UNIT_BANKS = [[(0, t, P * j, P) for t in slots] for j in (0, 1) for slots in ((0, 1), (2, 3))] + [
    [(1, t, 0, CHUNK)] for t in range(4)
]
BLOCKS = [[(0, 0), (0, 1)], [(1, 0), (1, 1)], [(0, 2), (1, 2)], [(0, 3), (1, 3)]]
ON_SCALAR = {1: (1,), 2: (0,), 3: (0,), 4: (0, 2)}
POOL_SLOTS = (0, 1, 2)
POOL_COLS = 272
SIG_BUFS = 4
O16_BUFS = 4


def tile_twotimehiddentangentkernel_x2_kernel(
    tc, x, y, wa_words, wa_scales, wb_words, wb_scales, b, va, vb, out_0, out_1, out_2
):
    nc = tc.nc
    with ExitStack() as ctx:
        keep = ctx.enter_context(tc.tile_pool(name="keep", bufs=1))
        work = ctx.enter_context(tc.tile_pool(name="work", bufs=3))
        psum = ctx.enter_context(tc.psum_pool(name="psum", bufs=1))
        ctx.enter_context(tc.manual_schedule())

        def scalar_bank(name):
            return psum.tile([P, BANK], F32, name=name, tag="act", bufs=4)

        def vector_bank(name):
            return psum.tile([P, BANK], F32, name=name, tag="dve", bufs=4)

        warm = keep.tile([P, 8], F32, name="warm")
        nc.vector.memset(warm[:, 0:1], 0.0)
        nc.scalar.activation(out=warm[:, 1:2], in_=warm[:, 0:1], func=ACT.Sigmoid)

        plane_raw = [keep.tile([P, F], U8, name="plane_raw%d" % side, align_bytes=64) for side in (X, Y)]
        nc.vector.memset(plane_raw[X][:].bitcast(I32), 0)
        b_rows = keep.tile([P, P], BF16, name="b_rows", align_bytes=64)
        v_rows = keep.tile([P, P], BF16, name="v_rows", align_bytes=64)
        nc.vector.memset(b_rows[:], 0.0)
        nc.vector.memset(v_rows[:], 0.0)

        ident = keep.tile([P, P], F32, name="ident", align_bytes=64)
        nc.vector.memset(ident[:], 0.0)
        make_identity(nc, ident[:], nomemset=True)
        ident16 = keep.tile([P, P], BF16, name="ident16", align_bytes=64)
        nc.vector.tensor_copy(out=ident16[:], in_=ident[:])
        nc.vector.memset(plane_raw[Y][:].bitcast(I32), 0)

        raw = {}

        def load_rows(side, chunk, chunks):
            tiles = keep.tile([P, 2 * chunks, D], BF16, name="raw_%d%d" % (side, chunk), align_bytes=64)
            if side == X:
                group = x[BANK * (chunk // 2) : BANK * (chunk // 2 + 1), :].rearrange("(p t) k -> p t k", t=4)
                view = group[:, 2 * (chunk % 2) : 2 * (chunk % 2 + chunks), :]
            else:
                view = y[CHUNK * chunk : CHUNK * (chunk + chunks), :].rearrange("(j p) k -> p j k", p=P)
            nc.sync.dma_start(out=tiles[:], in_=view)
            for i in range(chunks):
                raw[side, chunk + i] = tiles[:, 2 * i : 2 * i + 2, :]

        w_raw = [keep.tile([P, 2 * F], U8, name="w_raw%d" % side, align_bytes=64) for side in (X, Y)]
        w_perm = [keep.tile([P, 2 * F], U8, name="w_perm%d" % side, align_bytes=64) for side in (X, Y)]
        plane_perm = [keep.tile([P, F], U8, name="plane_perm%d" % side, align_bytes=64) for side in (X, Y)]

        def load_scales(side):
            for quad in range(4):
                nc.sync.dma_start(
                    out=plane_raw[side][32 * quad : 32 * quad + 4, :].bitcast(I32),
                    in_=(wa_scales, wb_scales)[side][0][4 * quad : 4 * quad + 4, :].bitcast(I32),
                )

        def load_words(side):
            nc.sync.dma_start(out=w_raw[side][:].bitcast(I32), in_=(wa_words, wb_words)[side][0].bitcast(I32))

        def load_vector(rows, first, vec):
            nc.sync.dma_start(
                out=rows[first : first + 8, :].rearrange("r (q i) -> r q i", i=8),
                in_=vec.rearrange("(q r i) -> r q i", r=8, i=8),
            )

        load_rows(X, 0, 1)
        load_rows(X, 1, 1)
        load_words(X)
        load_scales(X)
        load_vector(b_rows, 0, b)
        load_vector(b_rows, 8, va)
        load_words(Y)
        load_scales(Y)
        load_rows(Y, 0, 2)
        load_vector(v_rows, 0, vb)
        for side in (X, Y):
            load_rows(side, 2, 2)

        def permute(dst, src):
            nc.vector.tensor_copy(
                out=dst[:].bitcast(I32).rearrange("p (r q i) -> p r q i", r=8, q=16),
                in_=src[:].bitcast(I32).rearrange("p (q r i) -> p r q i", r=8, q=16),
            )

        turned = {}
        grouped = [keep.tile([P, 4 * N], BF16, name="grouped%d" % side, align_bytes=64) for side in (X, Y)]
        codes = [keep.tile([P, N], U32, name="codes%d" % side, align_bytes=64) for side in (X, Y)]
        planes = [keep.tile([P, N], U8, name="planes%d" % side, align_bytes=64) for side in (X, Y)]

        def transposes(side, chunk, bank):
            turned[side, chunk] = bank
            for j in (0, 1):
                pairs = raw[side, chunk][:, j, :].bitcast(F32)
                for u in (0, 1):
                    col = P * (2 * j + u)
                    nc.tensor.transpose(bank[:, col : col + P], pairs[:, u : D // 2 : 2], ident[:])

        def turn_out(side, chunk, on_scalar):
            pairs = grouped[side][:, 4 * CHUNK * chunk : 4 * CHUNK * (chunk + 1)].bitcast(F32)
            dst = pairs.rearrange("p (j r u) -> p j r u", j=2, u=2)
            src = turned[side, chunk][:].rearrange("p (j u r) -> p j r u", j=2, u=2)
            if on_scalar:
                nc.scalar.copy(out=dst, in_=src)
            else:
                nc.vector.tensor_copy(out=dst, in_=src)

        def first_tile(j):
            bank = vector_bank("turn")
            pairs = raw[X, 0][:, j, :].bitcast(F32)
            for u in (0, 1):
                nc.tensor.transpose(bank[:, P * u : P * (u + 1)], pairs[:, u : D // 2 : 2], ident[:])
            return bank

        def first_tile_out(j, bank):
            pairs = grouped[X][:, 4 * P * j : 4 * P * (j + 1)].bitcast(F32)
            nc.scalar.copy(
                out=pairs.rearrange("p (r u) -> p r u", u=2), in_=bank[:, 0 : 2 * P].rearrange("p (u r) -> p r u", u=2)
            )

        def first_tile_quant(j):
            nc.vector.quantize_mx(
                out=codes[X][:, P * j : P * (j + 1)].bitcast(FP8X4),
                scales=planes[X][:, P * j : P * (j + 1)],
                in_=grouped[X][:, 4 * P * j : 4 * P * (j + 1)],
            )

        def dealt_transposes(side, chunk):
            dealt = keep.tile([P, 2, 2, P], I32, name="dealt", align_bytes=64)
            nc.vector.tensor_copy(out=dealt[:], in_=raw[side, chunk].bitcast(I32).rearrange("p j (r u) -> p j u r", u=2))
            banks = []
            for j in (0, 1):
                banks.append(scalar_bank("turn"))
                for u in (0, 1):
                    nc.tensor.transpose(banks[j][:, P * u : P * (u + 1)], dealt[:, j, u, :].bitcast(F32), ident[:])
            return banks

        def turn(side, chunk, on_scalar):
            transposes(side, chunk, (scalar_bank if on_scalar else vector_bank)("turn"))
            turn_out(side, chunk, on_scalar)

        def quant_in(side, chunk, chunks=1):
            c0, c1 = CHUNK * chunk, CHUNK * (chunk + chunks)
            nc.vector.quantize_mx(
                out=codes[side][:, c0:c1].bitcast(FP8X4),
                scales=planes[side][:, c0:c1],
                in_=grouped[side][:, 4 * c0 : 4 * c1],
            )

        bias2 = keep.tile([P, 8], F32, name="bias2")
        minus4v = keep.tile([P, 16], F32, name="minus4v")
        plus4v = keep.tile([P, 16], F32, name="plus4v")

        def turn_vector(rows):
            bank = psum.tile([P, 2 * BANK], BF16, name="vbank", tag="dve", bufs=4)
            nc.tensor.transpose(bank[:, 0:P], rows[:], ident16[:])
            return bank

        def vector_out(bank, first, dst, times):
            nc.vector.tensor_scalar(
                out=dst, in0=bank[:, first : first + 8], scalar1=times, scalar2=None, op0=ALU.mult
            )

        z_banks, sig, fac, d16, d_codes, d_planes, d_at = {}, {}, {}, {}, {}, {}, {}

        def slots_in_bank(u, k):
            if u == 0:
                chosen = FIRST_UNIT_BANKS[k]
            else:
                each = len(UNITS[u])
                chosen = [divmod(s, 4) + (0, BANK // each) for s in range(each * k, each * (k + 1))]
            return [(part, t, slice(c, c + w), slice(w * i, w * (i + 1))) for i, (part, t, c, w) in enumerate(chosen)]

        def four_slots(tile):
            return tile[:].rearrange("p (t n) -> p t n", t=4)

        def part_of(tile, u, part):
            width = UNITS[u][part][3]
            return four_slots(tile)[:, :, width * part : width * (part + 1)]

        def z_mm(u, banks, new_bank=scalar_bank):
            for k in banks:
                z = new_bank("z")
                z_banks[u, k] = z
                for part, t, cols, at in slots_in_bank(u, k):
                    side, g, token, width = UNITS[u][part]
                    tokens = slice(token + cols.start, token + cols.stop)
                    r = 4 * g + t
                    nc.tensor.matmul_mx(
                        out=z[:, at],
                        lhsT=w_perm[side][:, 2 * P * r : 2 * P * (r + 1)].bitcast(FP4X4),
                        lhsT_scale=plane_perm[side][:, P * r : P * (r + 1)],
                        rhs=codes[side][:, tokens].bitcast(FP8X4),
                        rhs_scale=planes[side][:, tokens],
                        start=True,
                        stop=True,
                    )

        def sigmoid(u, banks):
            for k in banks:
                if k == 0:
                    sig[u] = work.tile([P, 4 * BANK], F32, name="sig", tag="sig", bufs=SIG_BUFS, align_bytes=64)
                for part, t, cols, at in slots_in_bank(u, k):
                    r = 4 * UNITS[u][part][1] + t
                    nc.scalar.activation(
                        out=part_of(sig[u], u, part)[:, t, cols], in_=z_banks[u, k][:, at], func=ACT.Sigmoid,
                        bias=bias2[:, r : r + 1], scale=2.0,
                    )

        def factor_part(u, part):
            if u == 7:
                if (u, part) not in fac:
                    tag = ("run2", "fac_last")[part]
                    fac[u, part] = work.tile([P, 4, CHUNK], F32, name="fac", tag=tag, bufs=1, align_bytes=64)
                return fac[u, part][:]
            if u not in fac:
                tag, bufs = ("fac", 2) if u < 4 else ("run0", 1) if u < 6 else ("run1", 1)
                fac[u] = work.tile([P, 4 * BANK], F32, name="fac", tag=tag, bufs=bufs, align_bytes=64)
            return part_of(fac[u], u, part)

        def scalar_factor(u, t, part=0):
            side, g, token, width = UNITS[u][part]
            c = 8 * side + 4 * g + t
            nc.scalar.activation(
                out=factor_part(u, part)[:, t, :], in_=part_of(sig[u], u, part)[:, t, :], func=ACT.Identity,
                bias=plus4v[:, c : c + 1], scale=minus4v[:, c : c + 1],
            )

        def wide_stage(u, scalar_slots):
            for pair in ((0, 1), (2, 3)):
                z_mm(u, pair)
                sigmoid(u, pair)
                for t in pair:
                    if t in scalar_slots:
                        scalar_factor(u, t)

        def narrow_stage(u, part):
            sigmoid(u, (2 * part, 2 * part + 1))
            for t in range(4):
                scalar_factor(u, t, part)

        def factor(engine, u, part, slots):
            side, g, token, width = UNITS[u][part]
            for t in slots:
                c = 8 * side + 4 * g + t
                if engine is nc.vector:
                    engine.tensor_scalar(
                        out=factor_part(u, part)[:, t, :], in0=part_of(sig[u], u, part)[:, t, :],
                        scalar1=1.0, scalar2=minus4v[:, c : c + 1], op0=ALU.subtract, op1=ALU.mult,
                    )
                else:
                    engine.tensor_scalar(
                        out=factor_part(u, part)[:, t, :], in0=part_of(sig[u], u, part)[:, t, :],
                        scalar1=minus4v[:, c : c + 1], scalar2=plus4v[:, c : c + 1], op0=ALU.mult, op1=ALU.add,
                    )

        def by_runs(slots4):
            return slots4.rearrange("p t (c i) -> p c t i", i=RUN)

        def into_words(tile16):
            return tile16.rearrange("p (c i) t -> p c t i", i=RUN)

        def new_d16(u):
            tag, bufs = ("d16_extra", 1) if u == 5 else ("d16", 2)
            d16[u] = work.tile([P, BANK, 4], BF16, name="d16", tag=tag, bufs=bufs, align_bytes=64)

        def product(u, part=0):
            width = UNITS[u][part][3]
            if part == 0:
                new_d16(u)
            nc.vector.tensor_tensor(
                out=into_words(d16[u][:, width * part : width * (part + 1), :]),
                in0=by_runs(part_of(sig[u], u, part)),
                in1=by_runs(factor_part(u, part)),
                op=ALU.mult,
            )

        def quant_d(u, halves=(0, 1)):
            if u not in d_codes:
                d_codes[u] = keep.tile([P, BANK], U32, name="d_codes%d" % u, align_bytes=64)
                d_planes[u] = keep.tile([P, BANK], U8, name="d_planes%d" % u, align_bytes=64)
            cols = slice(CHUNK * halves[0], CHUNK * (halves[-1] + 1))
            for part, (side, g, token, width) in enumerate(UNITS[u]):
                for step in range(0, width, P):
                    d_at[side, g, token + step] = (u, width * part + step)
            nc.vector.quantize_mx(
                out=d_codes[u][:, cols].bitcast(FP8X4),
                scales=d_planes[u][:, cols],
                in_=d16[u][:, cols, :].rearrange("p n t -> p (n t)"),
            )

        base_banks, gram_banks, base_sb, o32, o16 = {}, {}, {}, {}, {}

        def chunk_cols(j):
            return slice(CHUNK * j, CHUNK * (j + 1))

        def tiles_in_bank(n, k):
            if n < 2:
                return [(n, k, 0, BANK)]
            h, j = BLOCKS[n][k // 2]
            return [(h, 2 * (k % 2) + i, CHUNK * j, CHUNK) for i in (0, 1)]

        def base_mm(n, banks):
            for k in banks:
                base_banks[n, k] = scalar_bank("base")
                for i, (h, t, col, width) in enumerate(tiles_in_bank(n, k)):
                    rows = slice(BANK * h + P * t, BANK * h + P * (t + 1))
                    nc.tensor.matmul_mx(
                        out=base_banks[n, k][:, width * i : width * (i + 1)],
                        lhsT=codes[X][:, rows].bitcast(FP8X4),
                        lhsT_scale=planes[X][:, rows],
                        rhs=codes[Y][:, col : col + width].bitcast(FP8X4),
                        rhs_scale=planes[Y][:, col : col + width],
                        start=True,
                        stop=True,
                    )

        def base_out(n, banks):
            for k in banks:
                base_sb[n, k] = work.tile([P, BANK], F32, name="base_sb", tag="base_sb", bufs=8, align_bytes=64)
                nc.scalar.activation(out=base_sb[n, k][:], in_=base_banks[n, k][:], func=ACT.Copy, scale=SCALE)

        def gram_mm(n, banks, passes):
            for k in banks:
                tiles = tiles_in_bank(n, k)
                for g in passes:
                    if g == 0:
                        gram_banks[n, k] = vector_bank("gram")
                    for i, (h, t, col, width) in enumerate(tiles):
                        ux, cx = d_at[X, g, BANK * h + P * t]
                        uy, cy = d_at[Y, g, col]
                        nc.tensor.matmul_mx(
                            out=gram_banks[n, k][:, width * i : width * (i + 1)],
                            lhsT=d_codes[ux][:, cx : cx + P].bitcast(FP8X4),
                            lhsT_scale=d_planes[ux][:, cx : cx + P],
                            rhs=d_codes[uy][:, cy : cy + width].bitcast(FP8X4),
                            rhs_scale=d_planes[uy][:, cy : cy + width],
                            start=(g == 0 and i == 0),
                            stop=(g == 1 and i == len(tiles) - 1),
                        )

        def hadamard(n, banks):
            for k in banks:
                tiles = tiles_in_bank(n, k)
                h, t0, col, width = tiles[0]
                if t0 == 0:
                    whole = work.tile(
                        [P, 4, width], F32, name="o32", tag="o32_%d" % width, bufs=2 if n < 2 else 4, align_bytes=64
                    )
                    o32[h, col, width] = whole
                    for i in range(width // CHUNK):
                        o32[h, col // CHUNK + i] = whole[:, :, chunk_cols(i)]
                slots = o32[h, col, width][:, t0 : t0 + len(tiles), :]
                nc.vector.tensor_tensor(
                    out=slots.rearrange("p t c -> p (t c)"), in0=gram_banks[n, k][:], in1=base_sb[n, k][:], op=ALU.mult
                )
                rows = out_0[BANK * h : BANK * (h + 1), col : col + width].rearrange("(p t) m -> p t m", t=4)
                nc.sync.dma_start(out=rows[:, t0 : t0 + len(tiles), :], in_=slots)

        def o16_tile(h, j, tag="o16", bufs=O16_BUFS):
            if (h, j) not in o16:
                o16[h, j] = work.tile([P, CHUNK, 4], BF16, name="o16", tag=tag, bufs=bufs, align_bytes=64)
            return o16[h, j][:]

        def relay_tile(n, tag):
            pair = work.tile([P, 2 * CHUNK, 4], BF16, name="o16pair", tag=tag, bufs=1, align_bytes=64)
            for i, piece in enumerate(BLOCKS[n]):
                o16[piece] = pair[:, chunk_cols(i), :]
            o16[n, "pool"], o16[n, "rest"] = pair[:, :POOL_COLS, :], pair[:, POOL_COLS:, :]
            o32[n, "pool"], o32[n, "rest"] = o32[n, 0, BANK][:, :, :POOL_COLS], o32[n, 0, BANK][:, :, POOL_COLS:]

        def scalar_cast(h, j):
            nc.scalar.copy(out=into_words(o16_tile(h, j)), in_=by_runs(o32[h, j][:]))

        def vector_cast(h, j):
            nc.vector.tensor_copy(out=into_words(o16_tile(h, j)), in_=by_runs(o32[h, j][:]))

        def pool_cast(h, j, *buffer):
            nc.gpsimd.tensor_scalar(
                out=o16_tile(h, j, *buffer), in0=o32[h, j][:].rearrange("p t c -> p c t"),
                scalar1=1.0, scalar2=0.0, op0=ALU.mult, op1=ALU.add,
            )

        o_codes = keep.tile([P, 2, M], U32, name="o_codes", align_bytes=64)
        o_planes = keep.tile([P, M], U8, name="o_planes", align_bytes=64)

        def quant_o(h, j):
            nc.vector.quantize_mx(
                out=o_codes[:, h, chunk_cols(j)].bitcast(FP8X4),
                scales=o_planes[4 * h :, chunk_cols(j)],
                in_=o16[h, j][:].rearrange("p n t -> p (n t)"),
            )

        def store_words(h, j0, j1):
            cols = slice(CHUNK * j0, CHUNK * j1)
            nc.sync.dma_start(
                out=out_1[h][:, cols, :].rearrange("p m t -> p (m t)").bitcast(I32),
                in_=o_codes[:, h, cols].bitcast(I32),
            )

        def store_scales():
            for quad in range(4):
                nc.scalar.dma_start(
                    out=out_2[:, 4 * quad : 4 * quad + 4, :].bitcast(I32),
                    in_=o_planes[32 * quad : 32 * quad + 8, :].bitcast(I32),
                )


        tile_banks = [first_tile(j) for j in (0, 1)]
        tile_banks = tile_banks + dealt_transposes(X, 1)
        b_bank = turn_vector(b_rows)
        for j in range(4):
            first_tile_out(j, tile_banks[j])
        permute(w_perm[X], w_raw[X])
        first_tile_quant(0)
        permute(plane_perm[X], plane_raw[X])
        first_tile_quant(1)
        vector_out(b_bank, 0, bias2[:], 2.0)
        vector_out(b_bank, 8, minus4v[:, 0:8], -4.0)
        vector_out(b_bank, 8, plus4v[:, 0:8], 4.0)
        z_mm(0, BANKS)
        quant_in(X, 1)
        permute(w_perm[Y], w_raw[Y])
        permute(plane_perm[Y], plane_raw[Y])
        z_mm(0, (4, 5), vector_bank)
        sigmoid(0, (0, 1))
        z_mm(0, (6, 7))
        sigmoid(0, (2, 3))
        z_mm(1, (0,), vector_bank)
        sigmoid(0, (4, 5, 6, 7))
        for chunk in (0, 1):
            transposes(Y, chunk, vector_bank("turn"))
        v_bank = turn_vector(v_rows)
        z_mm(1, (1, 2, 3))
        sigmoid(1, (0,))

        turn_out(Y, 0, True)
        turn_out(Y, 1, True)
        sigmoid(1, (1, 2, 3))
        for t in ON_SCALAR[1]:
            scalar_factor(1, t)
        factor(nc.vector, 0, 0, range(4))
        factor(nc.vector, 0, 1, (0,))
        product(0, 0)
        factor(nc.vector, 0, 1, (1, 2, 3))

        vector_out(v_bank, 0, minus4v[:, 8:16], -4.0)
        vector_out(v_bank, 0, plus4v[:, 8:16], 4.0)
        factor(nc.vector, 1, 0, (0,))
        product(0, 1)
        quant_in(Y, 0, 2)

        for u, (side, chunk) in zip((1, 2, 3), ((X, 2), (X, 3), (Y, 2))):
            turn(side, chunk, True)
            slots = [t for t in range(u == 1, 4) if t not in ON_SCALAR[u]]
            if u == 2:
                factor(nc.vector, u, 0, slots[:-1])
                quant_d(u - 1)
                factor(nc.vector, u, 0, slots[-1:])
                quant_in(X, 2, 2)
            else:
                factor(nc.vector, u, 0, slots)
                quant_d(u - 1)
            wide_stage(u + 1, ON_SCALAR[u + 1])
            if u == 3:
                base_mm(0, BANKS)
                gram_mm(0, BANKS, (0,))
            product(u)

        base_out(0, BANKS)
        factor(nc.vector, 4, 0, [t for t in range(4) if t not in ON_SCALAR[4]])
        quant_d(3)
        z_mm(5, (0, 1))
        gram_mm(0, BANKS, (1,))
        z_mm(5, (2, 3))
        product(4)
        quant_in(Y, 2)
        sigmoid(5, BANKS)
        factor(nc.gpsimd, 5, 0, POOL_SLOTS)
        z_mm(6, (0, 1))
        hadamard(0, BANKS)
        turn(Y, 3, False)
        factor(nc.vector, 5, 0, [t for t in range(4) if t not in POOL_SLOTS])
        quant_d(4)

        narrow_stage(6, 0)
        z_mm(6, (2, 3))
        base_mm(1, (0, 1))
        gram_mm(1, BANKS, (0,))
        narrow_stage(6, 1)
        product(5)
        quant_in(Y, 3)
        base_mm(1, (2, 3))
        base_out(1, BANKS)
        quant_d(5)
        z_mm(7, (0,))
        gram_mm(1, (0, 1), (1,))
        z_mm(7, (1,))
        gram_mm(1, (2, 3), (1,))
        z_mm(7, (2, 3))
        for part in (0, 1):
            product(6, part)
        quant_d(6, (0,))
        relay_tile(0, "run1")
        pool_cast(0, "pool")
        narrow_stage(7, 0)
        base_mm(2, (0, 1))
        hadamard(1, BANKS)

        quant_d(6, (1,))
        base_out(2, (0, 1))
        gram_mm(2, BANKS, (0,))
        base_mm(2, (2, 3))
        gram_mm(2, BANKS, (1,))
        sigmoid(7, (2, 3))
        base_out(2, (2, 3))
        for t in range(4):
            scalar_factor(7, t, 1)
        base_mm(3, BANKS)
        product(7, 0)
        quant_o(0, 0)
        store_words(0, 0, 1)
        relay_tile(1, "run2")
        pool_cast(1, "pool")
        hadamard(2, BANKS)

        for h in (0, 1):
            scalar_cast(h, "rest")
        base_out(3, BANKS)
        quant_d(7, (0,))
        gram_mm(3, BANKS, (0,))
        product(7, 1)
        quant_o(0, 1)
        store_words(0, 1, 2)
        quant_d(7, (1,))
        gram_mm(3, BANKS, (1,))
        for j in (0, 1):
            quant_o(1, j)
            store_words(1, j, j + 1)
        shared = o16_tile(0, 2)
        for half, share in enumerate(("low", "high")):
            cols = (slice(0, 160), slice(160, CHUNK))[half]
            o16[0, share], o32[0, share] = shared[:, cols, :], o32[0, 2][:, :, cols]
        vector_cast(0, "low")
        pool_cast(1, 2, "run2", 1)
        hadamard(3, (0, 1))
        scalar_cast(0, "high")
        scalar_cast(0, 3)
        hadamard(3, (2, 3))
        quant_o(1, 2)
        store_words(1, 2, 3)
        last = o16_tile(1, 3)
        for half, share in enumerate(("low", "high")):
            cols = (slice(0, 176), slice(176, CHUNK))[half]
            o16[1, share], o32[1, share] = last[:, cols, :], o32[1, 3][:, :, cols]
        vector_cast(1, "low")
        scalar_cast(1, "high")
        for j in (3, 2):
            quant_o(0, j)
        store_words(0, 2, 4)
        quant_o(1, 3)
        store_words(1, 3, 4)
        store_scales()
